import numpy as np
import ml_dtypes


def mxq(x, axis, fmt="e4m3"):
    dtype, down = {"e4m3": (ml_dtypes.float8_e4m3fn, 7), "e5m2": (ml_dtypes.float8_e5m2, 14)}[fmt]
    v = np.moveaxis(np.asarray(x, np.float32).astype(ml_dtypes.bfloat16).astype(np.float64), axis, -1)
    blocks = v.reshape(v.shape[:-1] + (-1, 32))
    amax = np.abs(blocks).max(-1, keepdims=True)
    byte = np.maximum(np.where(amax > 0, np.frexp(amax)[1] - 1 + 127, 0) - down, 1)
    scale = np.exp2(byte - 127.0)
    codes = (blocks / scale).astype(np.float32).astype(dtype).astype(np.float64)
    return np.moveaxis((codes * scale).reshape(v.shape), -1, axis)


WIDE = False


def mx_kscale(k):
    if not WIDE:
        return np.ones(k)
    levels = np.array([10, -10, 5, -5, 0])
    if k % 512:
        return np.exp2(np.random.permutation(np.resize(levels, k // 32))).repeat(32)
    a = np.empty((k // 512, 16))
    for p in range(k // 512):
        a[p, :8] = np.random.permutation(np.resize(levels, 8))
        for g in range(8):
            far = levels[np.abs(levels - a[p, g]) >= 10]
            a[p, g + 8] = far[np.random.randint(len(far))]
    return np.exp2(a.ravel()).repeat(32)


def f64(x):
    return np.asarray(x).astype(np.float64)


def striped(idx):
    return np.tile(idx.reshape(-1, 16).T, (8, 1)).astype(np.uint16)


def unstriped(offs):
    return offs[:16].T.reshape(-1).astype(np.int64)


E2M1 = np.array([0.0, 0.5, 1.0, 1.5, 2.0, 3.0, 4.0, 6.0, -0.0, -0.5, -1.0, -1.5, -2.0, -3.0, -4.0, -6.0])


def pack_weight(w, fmt):
    k, n = w.shape
    w = f64(np.asarray(w, np.float32).astype(ml_dtypes.bfloat16)).reshape(k // 32, 32, n)
    amax = np.abs(w).max(1)
    if fmt == "e4m3":
        byte = np.frexp(amax)[1] - 1 + 127 - 7
    else:
        mant, ex = np.frexp(amax / 6.0)
        byte = np.where(mant > 0.5, ex, ex - 1) + 127
    byte = np.clip(np.where(amax > 0, byte, 1), 1, 254)
    scaled = (w * np.exp2(127.0 - byte)[:, None, :]).reshape(k, n).astype(np.float32)
    by_word = np.ascontiguousarray(scaled.reshape(k // 512, 128, 4, n).transpose(0, 1, 3, 2))
    if fmt == "e4m3":
        words = by_word.astype(ml_dtypes.float8_e4m3fn).view(np.uint8)
    else:
        c = by_word.astype(ml_dtypes.float4_e2m1fn).view(np.uint8) & 0xF
        words = (c[..., 0::2] | (c[..., 1::2] << 4)).reshape(k // 512, 128, 2 * n)
    return np.ascontiguousarray(words), np.ascontiguousarray(byte.astype(np.uint8).reshape(k // 512, 16, n))


def unpack_weight(words, scales, fmt):
    g, _, n = scales.shape
    words = np.ascontiguousarray(words).reshape(g, 128, n, -1)
    if fmt == "e4m3":
        vals = words.view(ml_dtypes.float8_e4m3fn).astype(np.float64)
    else:
        nib = np.empty((g, 128, n, 4), np.uint8)
        nib[..., 0::2] = words & 0xF
        nib[..., 1::2] = words >> 4
        vals = E2M1[nib]
    vals = vals * np.repeat(np.exp2(scales.astype(np.float64) - 127.0), 8, axis=1)[..., None]
    return vals.transpose(0, 1, 3, 2).reshape(g * 512, n)


def gelu(v):
    return 0.5 * v * (1.0 + np.tanh(np.sqrt(2.0 / np.pi) * (v + 0.044715 * v**3)))


def striped8(idx):
    return np.concatenate([v.reshape(-1, 16).T for v in idx]).astype(np.uint16)


def unstriped8(offs):
    return np.stack([offs[16 * g:16 * g + 16].T.reshape(-1) for g in range(8)]).astype(np.int64)


def put_heads(h, wgs, idx8, t2):
    r = np.arange(h.shape[0])
    page = np.zeros((h.shape[0], t2))
    page[r[:, None], idx8[r % 512 // 64]] = wgs[r // 4 % 128] * h
    return page


def bf(x):
    return np.asarray(x, np.float32).astype(ml_dtypes.bfloat16)


def planes(Y):
    n, m = Y.shape
    b = f64(bf(Y)).reshape(n // 32, 32, m)
    amax = np.abs(b).max(1)
    byte = np.clip(np.where(amax > 0, np.frexp(amax)[1] - 1 + 127 - 7, 1), 1, 254)
    codes = (b * np.exp2(127.0 - byte)[:, None, :]).reshape(n, m).astype(np.float32).astype(ml_dtypes.float8_e4m3fn).view(np.uint8)
    words = codes.reshape(n // 512, 128, 4, m).transpose(0, 1, 3, 2)
    return np.ascontiguousarray(words), np.ascontiguousarray(byte.astype(np.uint8).reshape(n // 512, 16, m))


K, H, N, T, S, T2 = 1536, 1024, 1024, 2048, 512, 1024

def setup_inputs():
    n = np.random.standard_normal
    s = mx_kscale(K)[:, None]
    u = mx_kscale(H)[:, None]
    size = np.exp(0.8 * n(N))
    tab_words, tab_scales = pack_weight(n((K, T)) * s, "e4m3")
    w4_words, w4_scales = pack_weight(n((H, N)) * 1.4 / np.sqrt(H) / u, "e2m1")
    return {
        "tab_words": tab_words, "tab_scales": tab_scales,
        "offs": striped(np.random.permutation(T)[:S]),
        "w1": (n((K, H)) * 1.5 / np.sqrt(K) / s).astype(np.float32),
        "wgs": np.repeat(np.random.uniform(0.5, 2.0, (8, S)), 16, axis=0).astype(np.float32),
        "offs2": striped8(np.stack([np.random.permutation(T2)[:S] for _ in range(8)])),
        "aff": (n((H, T2)) * u).astype(np.float32),
        "w4_words": w4_words, "w4_scales": w4_scales,
        "w2": (n((H, N)) * 1.2 / np.sqrt(H) / u * size).astype(np.float32),
        "fall": (n((N, T2)) * size[:, None]).astype(np.float32),
    }

def reference(tab_words, tab_scales, offs, w1, wgs, offs2, aff, w4_words, w4_scales, w2, fall):
    v = unpack_weight(tab_words, tab_scales, "e4m3")[:, unstriped(offs)]
    a = mxq(f64(w1), 0, "e4m3").T @ v
    h = a / (1 + np.exp(-a))
    page = put_heads(h, f64(wgs), unstriped8(offs2), T2)
    z = mxq(page * f64(aff), 0, "e4m3")
    p = unpack_weight(w4_words, w4_scales, "e2m1").T @ z
    gate = 1 / (1 + np.exp(-p))
    q = mxq(f64(w2), 0, "e4m3").T @ z
    f = f64(fall)
    y = f + gate * (q - f)
    words, scales = planes(y)
    return y, words, scales

@@ -1,0 +1,297 @@
+from contextlib import ExitStack
+
+import concourse.mybir as mybir
+
+K, H, N, T, S, T2 = 1536, 1024, 1024, 2048, 512, 1024
+FLOPS = 2 * K * H * S + 2 * 2 * H * N * T2
+
+F32 = mybir.dt.float32
+BF16 = mybir.dt.bfloat16
+I32 = mybir.dt.int32
+U32 = mybir.dt.uint32
+U16 = mybir.dt.uint16
+U8 = mybir.dt.uint8
+FP8X4 = mybir.dt.float8_e4m3fn_x4
+FP4X4 = mybir.dt.float4_e2m1fn_x4
+ALU = mybir.AluOpType
+ACT = mybir.ActivationFunctionType
+
+P = 128
+PACK = 4
+W = 512
+KP = K // W
+HB = H // W
+NG = N // W
+MH = T2 // W
+PAGES = 3
+
+
+def tile_list_replacement_item_scores_kernel(
+    tc, tab_words, tab_scales, offs, w1, wgs, offs2, aff, w4_words, w4_scales, w2, fall, out_0, out_1, out_2
+):
+    nc = tc.nc
+    with ExitStack() as ctx:
+        keep = ctx.enter_context(tc.tile_pool(name="keep", bufs=1))
+        ring = ctx.enter_context(tc.tile_pool(name="ring", bufs=1))
+        psum = ctx.enter_context(tc.psum_pool(name="psum", bufs=8))
+
+        idx = keep.tile([P, S // 16], U16, name="idx")
+        idx2 = keep.tile([P, S // 16], U16, name="idx2")
+        nc.sync.dma_start(idx[:], offs)
+
+        def load_rows(src, k0, c0, pieces=1):
+            raw = ring.tile([P, PACK, W], F32, name="raw", bufs=7, align_bytes=64)
+            rows = src[k0 : k0 + W, c0 : c0 + W].rearrange("(p j) c -> p j c", j=PACK)
+            step = PACK // pieces
+            for j in range(0, PACK, step):
+                nc.sync.dma_start(raw[:, j : j + step, :], rows[:, j : j + step, :])
+            return raw
+
+        def grouped_tile():
+            return ring.tile([P, PACK * W], BF16, name="grouped", bufs=6, align_bytes=64)
+
+        def cast_weight(raw):
+            grouped = grouped_tile()
+            nc.scalar.copy(
+                grouped[:].rearrange("p (t m j) -> p m j t", t=PACK, j=PACK),
+                raw[:].rearrange("p j (m t) -> p m j t", t=PACK),
+            )
+            return grouped
+
+        def interleave(copy, planes):
+            grouped = grouped_tile()
+            copy(
+                grouped[:].rearrange("p (c i t) -> p c t i", i=PACK, t=PACK),
+                planes.rearrange("p t (c i) -> p c t i", i=PACK),
+            )
+            return grouped
+
+        def quantise(grouped, name):
+            codes = keep.tile([P, W], U32, name=name + "_codes", align_bytes=64)
+            scales = keep.tile([P, W], U8, name=name + "_scales", align_bytes=64)
+            nc.vector.quantize_mx(codes[:].bitcast(FP8X4), scales[:], grouped[:])
+            return codes, scales
+
+        warm = keep.tile([P, 1], F32, name="warm")
+        tab_s = keep.tile([P, T], U8, name="tab_s", align_bytes=64)
+        nc.gpsimd.memset(tab_s[:].bitcast(I32), 0)
+        w4s_raw = keep.tile([P, HB, N], U8, name="w4s_raw", align_bytes=64)
+        nc.gpsimd.memset(w4s_raw[:].rearrange("p a n -> p (a n)").bitcast(I32), 0)
+        nc.gpsimd.memset(warm[:], 0.0)
+        for q in range(4):
+            nc.scalar.dma_start(
+                tab_s[32 * q : 32 * q + 4 * KP, :].bitcast(I32), tab_scales[:, 4 * q : 4 * q + 4, :].bitcast(I32)
+            )
+        nc.scalar.activation(warm[:], warm[:], ACT.Silu)
+        pages = [keep.tile([P, T2], F32, name="page%d" % i) for i in range(PAGES)]
+        for page in pages:
+            nc.gpsimd.memset(page[:], 0.0)
+
+        tab_w = [keep.tile([P, T], U32, name="tab_w%d" % a) for a in range(KP)]
+
+        def load_table(a):
+            nc.sync.dma_start(tab_w[a][:].bitcast(I32), tab_words[a].rearrange("p t i -> p (t i)").bitcast(I32))
+
+        raw1 = {}
+        raw1[0, 0] = load_rows(w1, 0, 0, 4)
+        raw1[1, 0] = load_rows(w1, W, 0, 2)
+        load_table(0)
+        raw1[2, 0] = load_rows(w1, 2 * W, 0)
+        load_table(1)
+        load_table(2)
+        nc.sync.dma_start(idx2[:], offs2)
+        wg = keep.tile([P, S], F32, name="wg")
+        nc.sync.dma_start(wg[:], wgs)
+        w4w_raw = keep.tile([P, HB, 2 * N], U8, name="w4w_raw", align_bytes=64)
+        nc.sync.dma_start(w4w_raw[:].bitcast(I32), w4_words.rearrange("a p c -> p a c").bitcast(I32))
+
+        for q in range(4):
+            nc.sync.dma_start(
+                w4s_raw[32 * q : 32 * q + 4, :, :].bitcast(I32),
+                w4_scales[:, 4 * q : 4 * q + 4, :].rearrange("a r n -> r a n").bitcast(I32),
+            )
+        affs = {}
+
+        def load_aff(b, i):
+            t = ring.tile([P, T2], F32, name="aff", bufs=5)
+            nc.sync.dma_start(t[:], aff[b * W : (b + 1) * W, :].rearrange("(p i) m -> p i m", i=PACK)[:, i, :])
+            affs[b, i] = t
+
+        load_aff(0, 0)
+        for a in range(KP):
+            raw1[a, 1] = load_rows(w1, a * W, W)
+        load_aff(0, 1)
+        load_aff(0, 2)
+        raw2 = {}
+        for g in range(NG):
+            for b in range(HB):
+                raw2[b, g] = load_rows(w2, b * W, g * W)
+        load_aff(0, 3)
+        for i in range(PACK):
+            load_aff(1, i)
+        falls = {}
+        for mh in range(MH):
+            for g in range(NG):
+                falls[g, mh] = load_rows(fall, g * W, mh * W)
+
+        v_s = keep.tile([P, S], U8, name="v_s", align_bytes=64)
+        v_w = [keep.tile([P, S], U32, name="v_w%d" % a, align_bytes=64) for a in range(KP)]
+        w1q = {}
+        nc.vector.tensor_copy(v_s[:], tab_s[:].indirect(idx[:]))
+        for a in range(KP):
+            w1q[a, 0] = quantise(cast_weight(raw1[a, 0]), "w1q%d0" % a)
+        for a in range(KP):
+            nc.vector.tensor_copy(v_w[a][:], tab_w[a][:].indirect(idx[:]))
+
+        w4s = keep.tile([P, HB * NG, PACK, P], U8, name="w4s", align_bytes=64)
+        nc.vector.tensor_copy(w4s[:], w4s_raw[:].rearrange("p a (g m t) -> p (a g) t m", g=NG, t=PACK))
+        w4w = keep.tile([P, HB * NG, PACK, 2 * P], U8, name="w4w", align_bytes=64)
+        nc.vector.tensor_copy(
+            w4w[:].bitcast(U16), w4w_raw[:].bitcast(U16).rearrange("p a (g m t) -> p (a g) t m", g=NG, t=PACK)
+        )
+
+        hs = {}
+
+        def first_product(b):
+            accs = [psum.tile([P, S], F32, name="acc") for i in range(PACK)]
+            for a in range(KP):
+                codes, scales = w1q[a, b]
+                for i in range(PACK):
+                    cols = slice(i * P, (i + 1) * P)
+                    nc.tensor.matmul_mx(
+                        accs[i][:],
+                        lhsT=codes[:, cols].bitcast(FP8X4),
+                        lhsT_scale=scales[:, cols],
+                        rhs=v_w[a][:].bitcast(FP8X4),
+                        rhs_scale=v_s[4 * a :, :],
+                        start=(a == 0),
+                        stop=(a == KP - 1),
+                    )
+            for i in range(PACK):
+                if i % 2 == 0:
+                    pair = ring.tile([P, 2, W], F32, name="pair", bufs=4)
+                hs[b, i] = pair[:, i % 2, :]
+                nc.scalar.activation(hs[b, i], accs[i][:], ACT.Silu)
+
+        zplanes = [keep.tile([P, PACK, T2], BF16, name="zplanes%d" % b) for b in range(HB)]
+
+        def scatter(n):
+            nc.vector.tensor_tensor(pages[n % PAGES][:].indirect(idx2[:]), hs[n // PACK, n % PACK], wg[:], ALU.mult)
+
+        def weigh(n, cols):
+            b, i = divmod(n, PACK)
+            nc.vector.tensor_tensor(zplanes[b][:, i, cols], pages[n % PAGES][:, cols], affs[b, i][:, cols], ALU.mult)
+
+        whole = slice(0, T2)
+        halves = [slice(mh * W, (mh + 1) * W) for mh in range(MH)]
+        zq = {}
+        w2q = {}
+
+        first_product(0)
+        scatter(0)
+        scatter(1)
+        weigh(0, whole)
+        for a in range(KP):
+            w1q[a, 1] = quantise(cast_weight(raw1[a, 1]), "w1q%d1" % a)
+        first_product(1)
+        scatter(2)
+        weigh(1, whole)
+        scatter(3)
+        weigh(2, whole)
+        scatter(4)
+        for g in range(NG):
+            for b in range(HB):
+                w2q[b, g] = quantise(cast_weight(raw2[b, g]), "w2q%d%d" % (b, g))
+        weigh(3, whole)
+        z0 = [interleave(nc.scalar.copy, zplanes[0][:, :, halves[mh]]) for mh in range(MH)]
+        scatter(5)
+        weigh(4, whole)
+        scatter(6)
+        for mh in range(MH):
+            zq[0, mh] = quantise(z0[mh], "zq0%d" % mh)
+        weigh(5, whole)
+        scatter(7)
+        weigh(6, whole)
+        weigh(7, halves[0])
+        weigh(7, halves[1])
+        zq[1, 0] = quantise(interleave(nc.vector.tensor_copy, zplanes[1][:, :, halves[0]]), "zq10")
+        zq[1, 1] = quantise(interleave(nc.scalar.copy, zplanes[1][:, :, halves[1]]), "zq11")
+
+        y_s = keep.tile([P, NG, T2], U8, name="y_s", align_bytes=64)
+        steps = [(mh, g, u) for mh in range(MH) for g in range(NG) for u in range(2)]
+        th = {}
+        dif = {}
+        ygrouped = {}
+
+        def products(s):
+            mh, g, u = steps[s]
+            th[s] = ring.tile([P, 2, W], F32, name="pair", bufs=4)
+            dif[s] = ring.tile([P, 2, W], F32, name="pair", bufs=4)
+            for k in range(2):
+                t = 2 * u + k
+                gate_acc = psum.tile([P, W], F32, name="acc")
+                q_acc = psum.tile([P, W], F32, name="acc")
+                for b in range(HB):
+                    nc.tensor.matmul_mx(
+                        gate_acc[:],
+                        lhsT=w4w[:, b * NG + g, t, :].bitcast(FP4X4),
+                        lhsT_scale=w4s[:, b * NG + g, t, :],
+                        rhs=zq[b, mh][0][:].bitcast(FP8X4),
+                        rhs_scale=zq[b, mh][1][:],
+                        start=(b == 0),
+                        stop=(b == HB - 1),
+                    )
+                cols = slice(t * P, (t + 1) * P)
+                for b in range(HB):
+                    nc.tensor.matmul_mx(
+                        q_acc[:],
+                        lhsT=w2q[b, g][0][:, cols].bitcast(FP8X4),
+                        lhsT_scale=w2q[b, g][1][:, cols],
+                        rhs=zq[b, mh][0][:].bitcast(FP8X4),
+                        rhs_scale=zq[b, mh][1][:],
+                        start=(b == 0),
+                        stop=(b == HB - 1),
+                    )
+                nc.scalar.activation(th[s][:, k, :], gate_acc[:], ACT.Tanh, scale=0.5)
+                nc.vector.tensor_tensor(dif[s][:, k, :], q_acc[:], falls[g, mh][:, t, :], ALU.subtract)
+
+        def flat(ap):
+            return ap.rearrange("p k c -> p (k c)")
+
+        def gate(s):
+            nc.vector.scalar_tensor_tensor(flat(dif[s][:]), flat(th[s][:]), 1.0, flat(dif[s][:]), ALU.add, ALU.mult)
+
+        def blend(s):
+            mh, g, u = steps[s]
+            y = falls[g, mh][:, 2 * u : 2 * u + 2, :]
+            nc.vector.scalar_tensor_tensor(flat(y), flat(dif[s][:]), 0.5, flat(y), ALU.mult, ALU.add)
+            rows = out_0[g * W : (g + 1) * W, halves[mh]].rearrange("(p t) m -> p t m", t=PACK)
+            nc.sync.dma_start(rows[:, 2 * u : 2 * u + 2, :], y)
+            if u == 1:
+                last = s == len(steps) - 1
+                ygrouped[s] = interleave(nc.vector.tensor_copy if last else nc.scalar.copy, falls[g, mh][:])
+
+        def planes_out(s):
+            mh, g, u = steps[s]
+            codes = ring.tile([P, W], U32, name="y_codes", bufs=2, align_bytes=64)
+            nc.vector.quantize_mx(codes[:].bitcast(FP8X4), y_s[:, g, halves[mh]], ygrouped[s][:])
+            nc.sync.dma_start(
+                out_1[g, :, halves[mh], :].rearrange("p m t -> p (m t)").bitcast(I32), codes[:].bitcast(I32)
+            )
+            if g == NG - 1:
+                for q in range(4):
+                    eng = nc.sync if q % 2 == 0 else nc.scalar
+                    eng.dma_start(
+                        out_2[:, 4 * q : 4 * q + 4, halves[mh]].rearrange("g r m -> r g m").bitcast(I32),
+                        y_s[32 * q : 32 * q + 4, :, halves[mh]].bitcast(I32),
+                    )
+
+        for s in range(len(steps) + 2):
+            if s < len(steps):
+                products(s)
+            if 1 <= s <= len(steps):
+                blend(s - 1)
+            if s < len(steps):
+                gate(s)
+            if s >= 2 and steps[s - 2][2] == 1:
+                planes_out(s - 2)

@@ -23,7 +23,8 @@ KP = K // W
 HB = H // W
 NG = N // W
 MH = T2 // W
-PAGES = 3
+PAGES = 4
+LAST_SCALAR_COLS = 80
 
 
 def tile_list_replacement_item_scores_kernel(
@@ -39,8 +40,8 @@ def tile_list_replacement_item_scores_kernel(
         idx2 = keep.tile([P, S // 16], U16, name="idx2")
         nc.sync.dma_start(idx[:], offs)
 
-        def load_rows(src, k0, c0, pieces=1):
-            raw = ring.tile([P, PACK, W], F32, name="raw", bufs=7, align_bytes=64)
+        def load_rows(src, k0, c0, slot, pieces=1):
+            raw = keep.tile([P, PACK, W], F32, name=slot, align_bytes=64)
             rows = src[k0 : k0 + W, c0 : c0 + W].rearrange("(p j) c -> p j c", j=PACK)
             step = PACK // pieces
             for j in range(0, PACK, step):
@@ -50,102 +51,101 @@ def tile_list_replacement_item_scores_kernel(
         def grouped_tile():
             return ring.tile([P, PACK * W], BF16, name="grouped", bufs=6, align_bytes=64)
 
-        def cast_weight(raw):
-            grouped = grouped_tile()
+        def cast_weight(raw, slot=None):
+            grouped = grouped_tile() if slot is None else keep.tile([P, PACK * W], BF16, name=slot, align_bytes=64)
             nc.scalar.copy(
                 grouped[:].rearrange("p (t m j) -> p m j t", t=PACK, j=PACK),
                 raw[:].rearrange("p j (m t) -> p m j t", t=PACK),
             )
             return grouped
 
+        def interleave_into(copy, grouped, planes, c0, c1):
+            copy(
+                grouped[:, PACK * c0 : PACK * c1].rearrange("p (c i t) -> p c t i", i=PACK, t=PACK),
+                planes[:, :, c0:c1].rearrange("p t (c i) -> p c t i", i=PACK),
+            )
+
         def interleave(copy, planes):
             grouped = grouped_tile()
-            copy(
-                grouped[:].rearrange("p (c i t) -> p c t i", i=PACK, t=PACK),
-                planes.rearrange("p t (c i) -> p c t i", i=PACK),
-            )
+            interleave_into(copy, grouped, planes, 0, W)
             return grouped
 
-        def quantise(grouped, name):
-            codes = keep.tile([P, W], U32, name=name + "_codes", align_bytes=64)
+        def quantise(grouped, name, codes=None):
+            if codes is None:
+                codes = keep.tile([P, W], U32, name=name + "_codes", align_bytes=64)[:]
             scales = keep.tile([P, W], U8, name=name + "_scales", align_bytes=64)
-            nc.vector.quantize_mx(codes[:].bitcast(FP8X4), scales[:], grouped[:])
+            nc.vector.quantize_mx(codes.bitcast(FP8X4), scales[:], grouped[:])
             return codes, scales
 
-        warm = keep.tile([P, 1], F32, name="warm")
         tab_s = keep.tile([P, T], U8, name="tab_s", align_bytes=64)
         nc.gpsimd.memset(tab_s[:].bitcast(I32), 0)
         w4s_raw = keep.tile([P, HB, N], U8, name="w4s_raw", align_bytes=64)
         nc.gpsimd.memset(w4s_raw[:].rearrange("p a n -> p (a n)").bitcast(I32), 0)
-        nc.gpsimd.memset(warm[:], 0.0)
         for q in range(4):
             nc.scalar.dma_start(
                 tab_s[32 * q : 32 * q + 4 * KP, :].bitcast(I32), tab_scales[:, 4 * q : 4 * q + 4, :].bitcast(I32)
             )
-        nc.scalar.activation(warm[:], warm[:], ACT.Silu)
         pages = [keep.tile([P, T2], F32, name="page%d" % i) for i in range(PAGES)]
         for page in pages:
             nc.gpsimd.memset(page[:], 0.0)
 
-        tab_w = [keep.tile([P, T], U32, name="tab_w%d" % a) for a in range(KP)]
+        tab_w = [keep.tile([P, T], U32, name="tab_w%d" % a, align_bytes=64) for a in range(KP)]
 
         def load_table(a):
             nc.sync.dma_start(tab_w[a][:].bitcast(I32), tab_words[a].rearrange("p t i -> p (t i)").bitcast(I32))
 
         raw1 = {}
-        raw1[0, 0] = load_rows(w1, 0, 0, 4)
-        raw1[1, 0] = load_rows(w1, W, 0, 2)
+        raw1[0, 0] = load_rows(w1, 0, 0, "raw0", 4)
+        raw1[1, 0] = load_rows(w1, W, 0, "raw1", 2)
         load_table(0)
-        raw1[2, 0] = load_rows(w1, 2 * W, 0)
-        load_table(1)
-        load_table(2)
-        nc.sync.dma_start(idx2[:], offs2)
-        wg = keep.tile([P, S], F32, name="wg")
-        nc.sync.dma_start(wg[:], wgs)
-        w4w_raw = keep.tile([P, HB, 2 * N], U8, name="w4w_raw", align_bytes=64)
-        nc.sync.dma_start(w4w_raw[:].bitcast(I32), w4_words.rearrange("a p c -> p a c").bitcast(I32))
-
+        raw1[2, 0] = load_rows(w1, 2 * W, 0, "raw2")
         for q in range(4):
             nc.sync.dma_start(
                 w4s_raw[32 * q : 32 * q + 4, :, :].bitcast(I32),
                 w4_scales[:, 4 * q : 4 * q + 4, :].rearrange("a r n -> r a n").bitcast(I32),
             )
+        load_table(1)
+        load_table(2)
+        w4w_raw = keep.tile([P, HB, 2 * N], U8, name="w4w_raw", align_bytes=64)
+        nc.sync.dma_start(w4w_raw[:].bitcast(I32), w4_words.rearrange("a p c -> p a c").bitcast(I32))
+        nc.sync.dma_start(idx2[:], offs2)
+        wg = keep.tile([P, S], F32, name="wg")
+        nc.sync.dma_start(wg[:], wgs)
+
         affs = {}
 
-        def load_aff(b, i):
-            t = ring.tile([P, T2], F32, name="aff", bufs=5)
-            nc.sync.dma_start(t[:], aff[b * W : (b + 1) * W, :].rearrange("(p i) m -> p i m", i=PACK)[:, i, :])
-            affs[b, i] = t
+        def aff_rows(b):
+            return aff[b * W : (b + 1) * W, :].rearrange("(p i) m -> p i m", i=PACK)
 
-        load_aff(0, 0)
+        def load_aff(n0, n1, slot):
+            t = keep.tile([P, (n1 - n0) * T2], F32, name=slot, align_bytes=64)
+            for n in range(n0, n1):
+                b, i = divmod(n, PACK)
+                affs[b, i] = t[:, (n - n0) * T2 : (n - n0 + 1) * T2]
+                nc.sync.dma_start(affs[b, i], aff_rows(b)[:, i, :])
+
         for a in range(KP):
-            raw1[a, 1] = load_rows(w1, a * W, W)
-        load_aff(0, 1)
-        load_aff(0, 2)
-        raw2 = {}
-        for g in range(NG):
-            for b in range(HB):
-                raw2[b, g] = load_rows(w2, b * W, g * W)
-        load_aff(0, 3)
-        for i in range(PACK):
-            load_aff(1, i)
-        falls = {}
-        for mh in range(MH):
-            for g in range(NG):
-                falls[g, mh] = load_rows(fall, g * W, mh * W)
+            raw1[a, 1] = load_rows(w1, a * W, W, "raw%d" % a)
+        load_aff(0, 2, "aff_low")
+        load_aff(2, 4, "aff_high")
 
         v_s = keep.tile([P, S], U8, name="v_s", align_bytes=64)
         v_w = [keep.tile([P, S], U32, name="v_w%d" % a, align_bytes=64) for a in range(KP)]
         w1q = {}
-        nc.vector.tensor_copy(v_s[:], tab_s[:].indirect(idx[:]))
-        for a in range(KP):
-            w1q[a, 0] = quantise(cast_weight(raw1[a, 0]), "w1q%d0" % a)
-        for a in range(KP):
+
+        def gather_words(a):
             nc.vector.tensor_copy(v_w[a][:], tab_w[a][:].indirect(idx[:]))
 
+        nc.vector.tensor_copy(v_s[:], tab_s[:].indirect(idx[:]))
+        w1q[0, 0] = quantise(cast_weight(raw1[0, 0]), "w1q00")
+        w1q[1, 0] = quantise(cast_weight(raw1[1, 0]), "w1q10")
+        gather_words(0)
         w4s = keep.tile([P, HB * NG, PACK, P], U8, name="w4s", align_bytes=64)
         nc.vector.tensor_copy(w4s[:], w4s_raw[:].rearrange("p a (g m t) -> p (a g) t m", g=NG, t=PACK))
-        w4w = keep.tile([P, HB * NG, PACK, 2 * P], U8, name="w4w", align_bytes=64)
+        w1q[2, 0] = quantise(cast_weight(raw1[2, 0]), "w1q20")
+        gather_words(1)
+        gather_words(2)
+        w4w = keep.tile([P, HB * NG, PACK, 2 * P], U8, name="tab_w2", align_bytes=64)
         nc.vector.tensor_copy(
             w4w[:].bitcast(U16), w4w_raw[:].bitcast(U16).rearrange("p a (g m t) -> p (a g) t m", g=NG, t=PACK)
         )
@@ -154,26 +154,27 @@ def tile_list_replacement_item_scores_kernel(
 
         def first_product(b):
             accs = [psum.tile([P, S], F32, name="acc") for i in range(PACK)]
-            for a in range(KP):
+            if b == 0:
+                passes = [(a, i) for a in range(KP) for i in range(PACK)]
+            else:
+                passes = [(a, i) for i in range(PACK) for a in reversed(range(KP))]
+            for a, i in passes:
                 codes, scales = w1q[a, b]
-                for i in range(PACK):
-                    cols = slice(i * P, (i + 1) * P)
-                    nc.tensor.matmul_mx(
-                        accs[i][:],
-                        lhsT=codes[:, cols].bitcast(FP8X4),
-                        lhsT_scale=scales[:, cols],
-                        rhs=v_w[a][:].bitcast(FP8X4),
-                        rhs_scale=v_s[4 * a :, :],
-                        start=(a == 0),
-                        stop=(a == KP - 1),
-                    )
+                cols = slice(i * P, (i + 1) * P)
+                nc.tensor.matmul_mx(
+                    accs[i][:],
+                    lhsT=codes[:, cols].bitcast(FP8X4),
+                    lhsT_scale=scales[:, cols],
+                    rhs=v_w[a][:].bitcast(FP8X4),
+                    rhs_scale=v_s[4 * a :, :],
+                    start=(a == passes[0][0]),
+                    stop=(a == passes[-1][0]),
+                )
             for i in range(PACK):
-                if i % 2 == 0:
-                    pair = ring.tile([P, 2, W], F32, name="pair", bufs=4)
-                hs[b, i] = pair[:, i % 2, :]
+                hs[b, i] = keep.tile([P, S], F32, name="h%d%d" % (b, i), align_bytes=64)[:]
                 nc.scalar.activation(hs[b, i], accs[i][:], ACT.Silu)
 
-        zplanes = [keep.tile([P, PACK, T2], BF16, name="zplanes%d" % b) for b in range(HB)]
+        zplanes = {}
 
         def scatter(n):
             nc.vector.tensor_tensor(pages[n % PAGES][:].indirect(idx2[:]), hs[n // PACK, n % PACK], wg[:], ALU.mult)
@@ -188,97 +189,129 @@ def tile_list_replacement_item_scores_kernel(
         w2q = {}
 
         first_product(0)
-        scatter(0)
-        scatter(1)
-        weigh(0, whole)
+        for n in range(PACK):
+            scatter(n)
         for a in range(KP):
-            w1q[a, 1] = quantise(cast_weight(raw1[a, 1]), "w1q%d1" % a)
+            w1q[a, 1] = quantise(cast_weight(raw1[a, 1], "h0%d" % a), "w1q%d1" % a)
+        raw2 = {}
+        for b in range(HB):
+            raw2[b, 0] = load_rows(w2, b * W, 0, "raw%d" % b)
+        w2g = [cast_weight(raw2[b, 0]) for b in range(HB)]
         first_product(1)
-        scatter(2)
-        weigh(1, whole)
-        scatter(3)
-        weigh(2, whole)
+        zplanes[0] = keep.tile([P, PACK, T2], BF16, name="h02", align_bytes=64)
+        zplanes[1] = keep.tile([P, PACK, T2], BF16, name="tab_w1", align_bytes=64)
+        for n in range(PACK):
+            weigh(n, whole)
+        for b in range(HB):
+            w2q[b, 0] = quantise(w2g[b], "w2q%d0" % b)
+        load_aff(4, 6, "aff_low")
+        load_aff(6, 8, "aff_high")
+        raw2[0, 1] = load_rows(w2, 0, W, "raw2")
+        raw2[1, 1] = load_rows(w2, W, W, "raw0")
         scatter(4)
-        for g in range(NG):
-            for b in range(HB):
-                w2q[b, g] = quantise(cast_weight(raw2[b, g]), "w2q%d%d" % (b, g))
-        weigh(3, whole)
-        z0 = [interleave(nc.scalar.copy, zplanes[0][:, :, halves[mh]]) for mh in range(MH)]
         scatter(5)
+        z0 = []
+        for mh in range(MH):
+            z0.append(keep.tile([P, PACK * W], BF16, name="h1%d" % mh, align_bytes=64))
+            interleave_into(nc.scalar.copy, z0[mh], zplanes[0][:, :, halves[mh]], 0, W)
+        w2g = [cast_weight(raw2[b, 1]) for b in range(HB)]
+        falls = {}
+        falls[0, 0] = load_rows(fall, 0, 0, "raw2")
+        falls[1, 0] = load_rows(fall, W, 0, "raw0")
         weigh(4, whole)
         scatter(6)
-        for mh in range(MH):
-            zq[0, mh] = quantise(z0[mh], "zq0%d" % mh)
         weigh(5, whole)
         scatter(7)
+        falls[0, 1] = load_rows(fall, 0, W, "aff_low")
+        falls[1, 1] = load_rows(fall, W, W, "h13")
         weigh(6, whole)
         weigh(7, halves[0])
         weigh(7, halves[1])
-        zq[1, 0] = quantise(interleave(nc.vector.tensor_copy, zplanes[1][:, :, halves[0]]), "zq10")
-        zq[1, 1] = quantise(interleave(nc.scalar.copy, zplanes[1][:, :, halves[1]]), "zq11")
+        zq[0, 0] = quantise(z0[0], "zq00")
+        zq[0, 1] = quantise(z0[1], "zq01")
+        for b in range(HB):
+            w2q[b, 1] = quantise(w2g[b], "w2q%d1" % b)
+        zq[1, 0] = quantise(interleave(nc.scalar.copy, zplanes[1][:, :, halves[0]]), "zq10")
 
         y_s = keep.tile([P, NG, T2], U8, name="y_s", align_bytes=64)
-        steps = [(mh, g, u) for mh in range(MH) for g in range(NG) for u in range(2)]
+        groups = [(mh, g) for mh in range(MH) for g in range(NG)]
+        steps = [(mh, g, u, 0, W) for mh, g in groups[:-1] for u in range(2)]
+        steps = steps + [groups[-1] + (u, c0, c0 + W // 2) for c0 in (0, W // 2) for u in range(2)]
         th = {}
         dif = {}
+        q_accs = {}
         ygrouped = {}
 
-        def products(s):
-            mh, g, u = steps[s]
-            th[s] = ring.tile([P, 2, W], F32, name="pair", bufs=4)
-            dif[s] = ring.tile([P, 2, W], F32, name="pair", bufs=4)
+        def products(mh, g, u):
+            if (mh, g, u) == (0, 0, 0):
+                th[mh, g, u] = keep.tile([P, 2, W], F32, name="gate_first", align_bytes=64)
+            else:
+                th[mh, g, u] = ring.tile([P, 2, W], F32, name="pair", bufs=5)
+            dif[mh, g, u] = ring.tile([P, 2, W], F32, name="pair", bufs=5)
             for k in range(2):
                 t = 2 * u + k
                 gate_acc = psum.tile([P, W], F32, name="acc")
                 q_acc = psum.tile([P, W], F32, name="acc")
-                for b in range(HB):
-                    nc.tensor.matmul_mx(
-                        gate_acc[:],
-                        lhsT=w4w[:, b * NG + g, t, :].bitcast(FP4X4),
-                        lhsT_scale=w4s[:, b * NG + g, t, :],
-                        rhs=zq[b, mh][0][:].bitcast(FP8X4),
-                        rhs_scale=zq[b, mh][1][:],
-                        start=(b == 0),
-                        stop=(b == HB - 1),
-                    )
                 cols = slice(t * P, (t + 1) * P)
                 for b in range(HB):
                     nc.tensor.matmul_mx(
                         q_acc[:],
                         lhsT=w2q[b, g][0][:, cols].bitcast(FP8X4),
                         lhsT_scale=w2q[b, g][1][:, cols],
-                        rhs=zq[b, mh][0][:].bitcast(FP8X4),
+                        rhs=zq[b, mh][0].bitcast(FP8X4),
                         rhs_scale=zq[b, mh][1][:],
                         start=(b == 0),
                         stop=(b == HB - 1),
                     )
-                nc.scalar.activation(th[s][:, k, :], gate_acc[:], ACT.Tanh, scale=0.5)
-                nc.vector.tensor_tensor(dif[s][:, k, :], q_acc[:], falls[g, mh][:, t, :], ALU.subtract)
+                for b in range(HB):
+                    nc.tensor.matmul_mx(
+                        gate_acc[:],
+                        lhsT=w4w[:, b * NG + g, t, :].bitcast(FP4X4),
+                        lhsT_scale=w4s[:, b * NG + g, t, :],
+                        rhs=zq[b, mh][0].bitcast(FP8X4),
+                        rhs_scale=zq[b, mh][1][:],
+                        start=(b == 0),
+                        stop=(b == HB - 1),
+                    )
+                nc.scalar.activation(th[mh, g, u][:, k, :], gate_acc[:], ACT.Tanh, scale=0.5)
+                q_accs[mh, g, t] = q_acc
 
-        def flat(ap):
-            return ap.rearrange("p k c -> p (k c)")
+        def difference(s):
+            mh, g, u, c0, c1 = steps[s]
+            if c0 == 0:
+                products(mh, g, u)
+            for k in range(2):
+                t = 2 * u + k
+                nc.vector.tensor_tensor(
+                    dif[mh, g, u][:, k, c0:c1], q_accs[mh, g, t][:, c0:c1], falls[g, mh][:, t, c0:c1], ALU.subtract
+                )
 
         def gate(s):
-            nc.vector.scalar_tensor_tensor(flat(dif[s][:]), flat(th[s][:]), 1.0, flat(dif[s][:]), ALU.add, ALU.mult)
+            mh, g, u, c0, c1 = steps[s]
+            d = dif[mh, g, u][:, :, c0:c1]
+            nc.vector.scalar_tensor_tensor(d, th[mh, g, u][:, :, c0:c1], 1.0, d, ALU.add, ALU.mult)
 
         def blend(s):
-            mh, g, u = steps[s]
-            y = falls[g, mh][:, 2 * u : 2 * u + 2, :]
-            nc.vector.scalar_tensor_tensor(flat(y), flat(dif[s][:]), 0.5, flat(y), ALU.mult, ALU.add)
-            rows = out_0[g * W : (g + 1) * W, halves[mh]].rearrange("(p t) m -> p t m", t=PACK)
+            mh, g, u, c0, c1 = steps[s]
+            y = falls[g, mh][:, 2 * u : 2 * u + 2, c0:c1]
+            nc.vector.scalar_tensor_tensor(y, dif[mh, g, u][:, :, c0:c1], 0.5, y, ALU.mult, ALU.add)
+            rows = out_0[g * W : (g + 1) * W, mh * W + c0 : mh * W + c1].rearrange("(p t) m -> p t m", t=PACK)
             nc.sync.dma_start(rows[:, 2 * u : 2 * u + 2, :], y)
             if u == 1:
-                last = s == len(steps) - 1
-                ygrouped[s] = interleave(nc.vector.tensor_copy if last else nc.scalar.copy, falls[g, mh][:])
+                ygrouped[s] = grouped_tile()
+                planes = falls[g, mh][:, :, c0:c1]
+                cut = c1 - c0 if s < len(steps) - 1 else LAST_SCALAR_COLS
+                interleave_into(nc.scalar.copy, ygrouped[s], planes, 0, cut)
+                if cut < c1 - c0:
+                    interleave_into(nc.vector.tensor_copy, ygrouped[s], planes, cut, c1 - c0)
 
         def planes_out(s):
-            mh, g, u = steps[s]
-            codes = ring.tile([P, W], U32, name="y_codes", bufs=2, align_bytes=64)
-            nc.vector.quantize_mx(codes[:].bitcast(FP8X4), y_s[:, g, halves[mh]], ygrouped[s][:])
-            nc.sync.dma_start(
-                out_1[g, :, halves[mh], :].rearrange("p m t -> p (m t)").bitcast(I32), codes[:].bitcast(I32)
-            )
-            if g == NG - 1:
+            mh, g, u, c0, c1 = steps[s]
+            cols = slice(mh * W + c0, mh * W + c1)
+            codes = ring.tile([P, c1 - c0], U32, name="y_codes", bufs=2, align_bytes=64)
+            nc.vector.quantize_mx(codes[:].bitcast(FP8X4), y_s[:, g, cols], ygrouped[s][:, : PACK * (c1 - c0)])
+            nc.sync.dma_start(out_1[g, :, cols, :].rearrange("p m t -> p (m t)").bitcast(I32), codes[:].bitcast(I32))
+            if g == NG - 1 and c1 == W:
                 for q in range(4):
                     eng = nc.sync if q % 2 == 0 else nc.scalar
                     eng.dma_start(
@@ -286,12 +319,17 @@ def tile_list_replacement_item_scores_kernel(
                         y_s[32 * q : 32 * q + 4, :, halves[mh]].bitcast(I32),
                     )
 
-        for s in range(len(steps) + 2):
+        for s in range(len(steps) + 3):
             if s < len(steps):
-                products(s)
+                difference(s)
             if 1 <= s <= len(steps):
                 blend(s - 1)
             if s < len(steps):
                 gate(s)
-            if s >= 2 and steps[s - 2][2] == 1:
-                planes_out(s - 2)
+            if s == 0:
+                grouped = keep.tile([P, PACK * W], BF16, name="gate_first", align_bytes=64)
+                interleave_into(nc.scalar.copy, grouped, zplanes[1][:, :, halves[1]], 0, W)
+            if s == 1:
+                zq[1, 1] = quantise(grouped, "zq11")
+            if s >= 3 and steps[s - 3][2] == 1:
+                planes_out(s - 3)

@@ -19,11 +19,14 @@ ACT = mybir.ActivationFunctionType
 P = 128
 PACK = 4
 W = 512
+G = PACK * W
 KP = K // W
 HB = H // W
 NG = N // W
 MH = T2 // W
-PAGES = 4
+PLANES = HB * PACK
+GP_COLS = 768
+GP_LAST_WEIGH = 640
 LAST_SCALAR_COLS = 80
 
 
@@ -33,63 +36,55 @@ def tile_list_replacement_item_scores_kernel(
     nc = tc.nc
     with ExitStack() as ctx:
         keep = ctx.enter_context(tc.tile_pool(name="keep", bufs=1))
-        ring = ctx.enter_context(tc.tile_pool(name="ring", bufs=1))
-        psum = ctx.enter_context(tc.psum_pool(name="psum", bufs=8))
+        psum = ctx.enter_context(tc.psum_pool(name="psum", bufs=4))
+
+        def sbuf(shape, dtype, slot):
+            return keep.tile(shape, dtype, name=slot, align_bytes=64)
 
         idx = keep.tile([P, S // 16], U16, name="idx")
         idx2 = keep.tile([P, S // 16], U16, name="idx2")
         nc.sync.dma_start(idx[:], offs)
 
         def load_rows(src, k0, c0, slot, pieces=1):
-            raw = keep.tile([P, PACK, W], F32, name=slot, align_bytes=64)
+            raw = sbuf([P, PACK, W], F32, slot)
             rows = src[k0 : k0 + W, c0 : c0 + W].rearrange("(p j) c -> p j c", j=PACK)
             step = PACK // pieces
             for j in range(0, PACK, step):
                 nc.sync.dma_start(raw[:, j : j + step, :], rows[:, j : j + step, :])
             return raw
 
-        def grouped_tile():
-            return ring.tile([P, PACK * W], BF16, name="grouped", bufs=6, align_bytes=64)
-
-        def cast_weight(raw, slot=None):
-            grouped = grouped_tile() if slot is None else keep.tile([P, PACK * W], BF16, name=slot, align_bytes=64)
+        def cast_weight(grouped, raw):
             nc.scalar.copy(
-                grouped[:].rearrange("p (t m j) -> p m j t", t=PACK, j=PACK),
+                grouped.rearrange("p (t m j) -> p m j t", t=PACK, j=PACK),
                 raw[:].rearrange("p j (m t) -> p m j t", t=PACK),
             )
-            return grouped
 
-        def interleave_into(copy, grouped, planes, c0, c1):
+        def interleave(copy, grouped, planes):
             copy(
-                grouped[:, PACK * c0 : PACK * c1].rearrange("p (c i t) -> p c t i", i=PACK, t=PACK),
-                planes[:, :, c0:c1].rearrange("p t (c i) -> p c t i", i=PACK),
+                grouped.rearrange("p (c i t) -> p c t i", i=PACK, t=PACK),
+                planes.rearrange("p t (c i) -> p c t i", i=PACK),
             )
 
-        def interleave(copy, planes):
-            grouped = grouped_tile()
-            interleave_into(copy, grouped, planes, 0, W)
-            return grouped
-
-        def quantise(grouped, name, codes=None):
-            if codes is None:
-                codes = keep.tile([P, W], U32, name=name + "_codes", align_bytes=64)[:]
-            scales = keep.tile([P, W], U8, name=name + "_scales", align_bytes=64)
-            nc.vector.quantize_mx(codes.bitcast(FP8X4), scales[:], grouped[:])
+        def quantise(grouped, words, codes_slot, scales_slot):
+            codes = sbuf([P, words], U32, codes_slot)
+            scales = sbuf([P, words], U8, scales_slot)
+            nc.vector.quantize_mx(codes[:].bitcast(FP8X4), scales[:], grouped)
             return codes, scales
 
-        tab_s = keep.tile([P, T], U8, name="tab_s", align_bytes=64)
+        tab_s = sbuf([P, T], U8, "tab_s")
         nc.gpsimd.memset(tab_s[:].bitcast(I32), 0)
-        w4s_raw = keep.tile([P, HB, N], U8, name="w4s_raw", align_bytes=64)
+        w4s_raw = sbuf([P, HB, N], U8, "w4s_raw")
         nc.gpsimd.memset(w4s_raw[:].rearrange("p a n -> p (a n)").bitcast(I32), 0)
         for q in range(4):
             nc.scalar.dma_start(
                 tab_s[32 * q : 32 * q + 4 * KP, :].bitcast(I32), tab_scales[:, 4 * q : 4 * q + 4, :].bitcast(I32)
             )
-        pages = [keep.tile([P, T2], F32, name="page%d" % i) for i in range(PAGES)]
+        pages = [keep.tile([P, T2], F32, name="page%d" % i) for i in range(PACK + 1)]
         for page in pages:
             nc.gpsimd.memset(page[:], 0.0)
+        page_of = [pages[n % PACK] for n in range(PLANES - 1)] + [pages[PACK]]
 
-        tab_w = [keep.tile([P, T], U32, name="tab_w%d" % a, align_bytes=64) for a in range(KP)]
+        tab_w = [sbuf([P, T], U32, "tab_w%d" % a) for a in range(KP)]
 
         def load_table(a):
             nc.sync.dma_start(tab_w[a][:].bitcast(I32), tab_words[a].rearrange("p t i -> p (t i)").bitcast(I32))
@@ -106,58 +101,79 @@ def tile_list_replacement_item_scores_kernel(
             )
         load_table(1)
         load_table(2)
-        w4w_raw = keep.tile([P, HB, 2 * N], U8, name="w4w_raw", align_bytes=64)
+        w4w_raw = sbuf([P, HB, 2 * N], U8, "w4w_raw")
         nc.sync.dma_start(w4w_raw[:].bitcast(I32), w4_words.rearrange("a p c -> p a c").bitcast(I32))
         nc.sync.dma_start(idx2[:], offs2)
-        wg = keep.tile([P, S], F32, name="wg")
+        wg = sbuf([P, S], F32, "wg")
         nc.sync.dma_start(wg[:], wgs)
 
         affs = {}
 
-        def aff_rows(b):
-            return aff[b * W : (b + 1) * W, :].rearrange("(p i) m -> p i m", i=PACK)
+        def load_aff(n, room):
+            b, i = divmod(n, PACK)
+            affs[n] = room
+            nc.sync.dma_start(room, aff[b * W : (b + 1) * W, :].rearrange("(p i) m -> p i m", i=PACK)[:, i, :])
 
-        def load_aff(n0, n1, slot):
-            t = keep.tile([P, (n1 - n0) * T2], F32, name=slot, align_bytes=64)
-            for n in range(n0, n1):
-                b, i = divmod(n, PACK)
-                affs[b, i] = t[:, (n - n0) * T2 : (n - n0 + 1) * T2]
-                nc.sync.dma_start(affs[b, i], aff_rows(b)[:, i, :])
+        aff01 = sbuf([P, 2 * T2], F32, "aff01")
+        aff23 = sbuf([P, 2 * T2], F32, "aff23")
+        aff7 = sbuf([P, T2], F32, "aff7")
+        raw2 = {}
+        raw1[0, 1] = load_rows(w1, 0, W, "raw3")
+        load_aff(0, aff01[:, :T2])
+        raw1[1, 1] = load_rows(w1, W, W, "raw4")
+        raw1[2, 1] = load_rows(w1, 2 * W, W, "raw5")
+        load_aff(1, aff01[:, T2:])
+        raw2[0, 0] = load_rows(w2, 0, 0, "raw6")
+        load_aff(2, aff23[:, :T2])
+        raw2[1, 0] = load_rows(w2, W, 0, "raw7")
+        load_aff(3, aff23[:, T2:])
+        load_aff(7, aff7[:])
 
-        for a in range(KP):
-            raw1[a, 1] = load_rows(w1, a * W, W, "raw%d" % a)
-        load_aff(0, 2, "aff_low")
-        load_aff(2, 4, "aff_high")
-
-        v_s = keep.tile([P, S], U8, name="v_s", align_bytes=64)
-        v_w = [keep.tile([P, S], U32, name="v_w%d" % a, align_bytes=64) for a in range(KP)]
+        v_s = sbuf([P, S], U8, "v_s")
+        v_w = [sbuf([P, S], U32, "v_w%d" % a) for a in range(KP)]
         w1q = {}
 
         def gather_words(a):
             nc.vector.tensor_copy(v_w[a][:], tab_w[a][:].indirect(idx[:]))
 
+        def head_weight(a, slot):
+            grouped = sbuf([P, G], BF16, slot)
+            cast_weight(grouped[:], raw1[a, 0])
+            codes, scales = quantise(grouped[:], W, "w1c%d" % a, "w1s%d" % a)
+            w1q[a, 0] = codes[:], scales[:]
+
         nc.vector.tensor_copy(v_s[:], tab_s[:].indirect(idx[:]))
-        w1q[0, 0] = quantise(cast_weight(raw1[0, 0]), "w1q00")
-        w1q[1, 0] = quantise(cast_weight(raw1[1, 0]), "w1q10")
+        head_weight(0, "ga")
+        head_weight(1, "gb")
         gather_words(0)
-        w4s = keep.tile([P, HB * NG, PACK, P], U8, name="w4s", align_bytes=64)
+        w4s = sbuf([P, HB * NG, PACK, P], U8, "w4s")
         nc.vector.tensor_copy(w4s[:], w4s_raw[:].rearrange("p a (g m t) -> p (a g) t m", g=NG, t=PACK))
-        w1q[2, 0] = quantise(cast_weight(raw1[2, 0]), "w1q20")
+        head_weight(2, "gc")
         gather_words(1)
         gather_words(2)
-        w4w = keep.tile([P, HB * NG, PACK, 2 * P], U8, name="tab_w2", align_bytes=64)
+        w4w = sbuf([P, HB * NG, PACK, 2 * P], U8, "tab_w2")
         nc.vector.tensor_copy(
             w4w[:].bitcast(U16), w4w_raw[:].bitcast(U16).rearrange("p a (g m t) -> p (a g) t m", g=NG, t=PACK)
         )
 
-        hs = {}
+        raw2[0, 1] = load_rows(w2, 0, W, "raw0")
+        aff45 = sbuf([P, 2 * T2], F32, "raw1")
+        load_aff(4, aff45[:, :T2])
+        load_aff(5, aff45[:, T2:])
+        raw2[1, 1] = load_rows(w2, W, W, "tab_w0")
+        falls = {}
+        falls[0, 0] = load_rows(fall, 0, 0, "raw2")
+        aff6 = sbuf([P, T2], F32, "tab_w1")
+        load_aff(6, aff6[:])
 
-        def first_product(b):
-            accs = [psum.tile([P, S], F32, name="acc") for i in range(PACK)]
-            if b == 0:
-                passes = [(a, i) for a in range(KP) for i in range(PACK)]
-            else:
-                passes = [(a, i) for i in range(PACK) for a in reversed(range(KP))]
+        hz = sbuf([P, PLANES * S], F32, "hz")
+        hz16 = hz[:].bitcast(BF16)
+        zplane = [hz16[:, n * T2 : (n + 1) * T2] for n in range(PLANES)]
+        h0 = sbuf([P, S], F32, "h0")
+        h4 = sbuf([P, S], F32, "h4")
+        hs = [h0[:]] + [hz[:, n * S : (n + 1) * S] for n in range(3)] + [h4[:]] + [hz[:, n * S : (n + 1) * S] for n in range(3, 6)]
+
+        def first_passes(accs, b, passes):
             for a, i in passes:
                 codes, scales = w1q[a, b]
                 cols = slice(i * P, (i + 1) * P)
@@ -167,169 +183,237 @@ def tile_list_replacement_item_scores_kernel(
                     lhsT_scale=scales[:, cols],
                     rhs=v_w[a][:].bitcast(FP8X4),
                     rhs_scale=v_s[4 * a :, :],
-                    start=(a == passes[0][0]),
-                    stop=(a == passes[-1][0]),
+                    start=(a == 0),
+                    stop=(a == KP - 1),
                 )
+
+        def silu(accs, b):
             for i in range(PACK):
-                hs[b, i] = keep.tile([P, S], F32, name="h%d%d" % (b, i), align_bytes=64)[:]
-                nc.scalar.activation(hs[b, i], accs[i][:], ACT.Silu)
+                nc.scalar.activation(hs[b * PACK + i], accs[i][:], ACT.Silu)
 
-        zplanes = {}
+        def scatter_fused(n):
+            nc.vector.tensor_tensor(page_of[n][:].indirect(idx2[:]), hs[n], wg[:], ALU.mult)
 
-        def scatter(n):
-            nc.vector.tensor_tensor(pages[n % PAGES][:].indirect(idx2[:]), hs[n // PACK, n % PACK], wg[:], ALU.mult)
+        def scatter(n, hw):
+            nc.vector.tensor_copy(page_of[n][:].indirect(idx2[:]), hw)
 
-        def weigh(n, cols):
-            b, i = divmod(n, PACK)
-            nc.vector.tensor_tensor(zplanes[b][:, i, cols], pages[n % PAGES][:, cols], affs[b, i][:, cols], ALU.mult)
+        def weigh(engine, n, cols):
+            engine.tensor_tensor(zplane[n][:, cols], page_of[n][:, cols], affs[n][:, cols], ALU.mult)
 
         whole = slice(0, T2)
         halves = [slice(mh * W, (mh + 1) * W) for mh in range(MH)]
+
+        accs = [psum.tile([P, S], F32, name="q") for i in range(PACK)]
+        first_passes(accs, 0, [(a, i) for a in range(KP) for i in range(PACK)])
+        silu(accs, 0)
+        w1g = sbuf([P, KP * G], BF16, "w1g")
+        for a in range(KP):
+            cast_weight(w1g[:, a * G : (a + 1) * G], raw1[a, 1])
+        falls[1, 0] = load_rows(fall, W, 0, "raw3")
+        falls[0, 1] = load_rows(fall, 0, W, "raw4")
+        falls[1, 1] = load_rows(fall, W, W, "raw5")
+        w1g32 = w1g[:].bitcast(F32)
+
+        scatter_fused(0)
+        hw1 = sbuf([P, S], F32, "h0")
+        nc.vector.tensor_tensor(hw1[:], hs[1], wg[:], ALU.mult)
+        scatter(1, hw1[:])
+        weigh(nc.gpsimd, 0, whole)
+
+        accs = [psum.tile([P, S], F32, name="gate") for i in range(PACK)]
+        codes, scales = quantise(w1g[:, : 2 * G], 2 * W, "w1c3", "w1s3")
+        for a in range(2):
+            w1q[a, 1] = codes[:, a * W : (a + 1) * W], scales[:, a * W : (a + 1) * W]
+        first_passes(accs, 1, [(a, i) for a in range(2) for i in range(PACK)])
+        hw2 = w1g32[:, 2 * S : 3 * S]
+        nc.vector.tensor_tensor(hw2, hs[2], wg[:], ALU.mult)
+        scatter(2, hw2)
+        weigh(nc.gpsimd, 1, whole)
+
+        codes, scales = quantise(w1g[:, 2 * G :], W, "w1c5", "w1s5")
+        w1q[2, 1] = codes[:], scales[:]
+        first_passes(accs, 1, [(2, i) for i in range(PACK)])
+        hw3 = w1g32[:, 4 * S : 5 * S]
+        nc.vector.tensor_tensor(hw3, hs[3], wg[:], ALU.mult)
+        scatter(3, hw3)
+        weigh(nc.gpsimd, 2, whole)
+        silu(accs, 1)
+
+        w2g = [sbuf([P, HB * G], BF16, slot) for slot in ("ga", "gb")]
+        for g in range(NG):
+            for b in range(HB):
+                cast_weight(w2g[g][:, b * G : (b + 1) * G], raw2[b, g])
+
+        scatter_fused(4)
+        hw567 = sbuf([P, 3, S], F32, "hw567")
+        nc.vector.tensor_tensor(
+            hw567[:],
+            hz[:, 3 * S : 6 * S].rearrange("p (n s) -> p n s", n=3),
+            wg[:].unsqueeze(1).to_broadcast([P, 3, S]),
+            ALU.mult,
+        )
+        for n in range(5, PLANES):
+            scatter(n, hw567[:, n - 5, :])
+        for n in range(3, PLANES - 2):
+            weigh(nc.gpsimd, n, whole)
+        weigh(nc.gpsimd, PLANES - 2, slice(0, GP_LAST_WEIGH))
+        weigh(nc.vector, PLANES - 1, halves[0])
+
+        def zplanes(b, cols):
+            return hz16[:, b * PACK * T2 : (b + 1) * PACK * T2].rearrange("p (t m) -> p t m", t=PACK)[:, :, cols]
+
         zq = {}
         w2q = {}
+        z0g = sbuf([P, MH * G], BF16, "tab_w0")
+        interleave(nc.scalar.copy, z0g[:], zplanes(0, whole))
+        z1g = [sbuf([P, G], BF16, slot) for slot in ("gc", "w1g")]
+        interleave(nc.scalar.copy, z1g[0][:], zplanes(1, halves[0]))
 
-        first_product(0)
-        for n in range(PACK):
-            scatter(n)
-        for a in range(KP):
-            w1q[a, 1] = quantise(cast_weight(raw1[a, 1], "h0%d" % a), "w1q%d1" % a)
-        raw2 = {}
-        for b in range(HB):
-            raw2[b, 0] = load_rows(w2, b * W, 0, "raw%d" % b)
-        w2g = [cast_weight(raw2[b, 0]) for b in range(HB)]
-        first_product(1)
-        zplanes[0] = keep.tile([P, PACK, T2], BF16, name="h02", align_bytes=64)
-        zplanes[1] = keep.tile([P, PACK, T2], BF16, name="tab_w1", align_bytes=64)
-        for n in range(PACK):
-            weigh(n, whole)
-        for b in range(HB):
-            w2q[b, 0] = quantise(w2g[b], "w2q%d0" % b)
-        load_aff(4, 6, "aff_low")
-        load_aff(6, 8, "aff_high")
-        raw2[0, 1] = load_rows(w2, 0, W, "raw2")
-        raw2[1, 1] = load_rows(w2, W, W, "raw0")
-        scatter(4)
-        scatter(5)
-        z0 = []
-        for mh in range(MH):
-            z0.append(keep.tile([P, PACK * W], BF16, name="h1%d" % mh, align_bytes=64))
-            interleave_into(nc.scalar.copy, z0[mh], zplanes[0][:, :, halves[mh]], 0, W)
-        w2g = [cast_weight(raw2[b, 1]) for b in range(HB)]
-        falls = {}
-        falls[0, 0] = load_rows(fall, 0, 0, "raw2")
-        falls[1, 0] = load_rows(fall, W, 0, "raw0")
-        weigh(4, whole)
-        scatter(6)
-        weigh(5, whole)
-        scatter(7)
-        falls[0, 1] = load_rows(fall, 0, W, "aff_low")
-        falls[1, 1] = load_rows(fall, W, W, "h13")
-        weigh(6, whole)
-        weigh(7, halves[0])
-        weigh(7, halves[1])
-        zq[0, 0] = quantise(z0[0], "zq00")
-        zq[0, 1] = quantise(z0[1], "zq01")
-        for b in range(HB):
-            w2q[b, 1] = quantise(w2g[b], "w2q%d1" % b)
-        zq[1, 0] = quantise(interleave(nc.scalar.copy, zplanes[1][:, :, halves[0]]), "zq10")
+        def split(store, pair, keys):
+            codes, scales = pair
+            for j, key in enumerate(keys):
+                store[key] = codes[:, j * W : (j + 1) * W], scales[:, j * W : (j + 1) * W]
 
-        y_s = keep.tile([P, NG, T2], U8, name="y_s", align_bytes=64)
-        groups = [(mh, g) for mh in range(MH) for g in range(NG)]
-        steps = [(mh, g, u, 0, W) for mh, g in groups[:-1] for u in range(2)]
-        steps = steps + [groups[-1] + (u, c0, c0 + W // 2) for c0 in (0, W // 2) for u in range(2)]
-        th = {}
-        dif = {}
+        split(w2q, quantise(w2g[0][:], HB * W, "hw567", "w2s0"), [(0, 0), (1, 0)])
+        split(zq, quantise(z0g[:], MH * W, "w4w_raw", "zs0"), [(0, 0), (0, 1)])
+        split(zq, quantise(z1g[0][:], W, "w1c0", "w1s0"), [(1, 0)])
+        weigh(nc.vector, PLANES - 2, slice(GP_LAST_WEIGH, T2))
+        weigh(nc.vector, PLANES - 1, halves[1])
+        interleave(nc.scalar.copy, z1g[1][:], zplanes(1, halves[1]))
+        split(w2q, quantise(w2g[1][:], HB * W, "gc", "w2s1"), [(0, 1), (1, 1)])
+
+        y_s = sbuf([P, NG, T2], U8, "y_s")
+        units = [(mh, g) for mh in range(MH) for g in range(NG)]
+        gates = {}
+        difs = {}
         q_accs = {}
         ygrouped = {}
 
-        def products(mh, g, u):
-            if (mh, g, u) == (0, 0, 0):
-                th[mh, g, u] = keep.tile([P, 2, W], F32, name="gate_first", align_bytes=64)
+        def q_pass(acc, s, t, b):
+            mh, g = units[s]
+            cols = slice(t * P, (t + 1) * P)
+            nc.tensor.matmul_mx(
+                acc[:],
+                lhsT=w2q[b, g][0][:, cols].bitcast(FP8X4),
+                lhsT_scale=w2q[b, g][1][:, cols],
+                rhs=zq[b, mh][0].bitcast(FP8X4),
+                rhs_scale=zq[b, mh][1],
+                start=(b == 0),
+                stop=(b == HB - 1),
+            )
+
+        def gate_pass(acc, s, t, b):
+            mh, g = units[s]
+            nc.tensor.matmul_mx(
+                acc[:],
+                lhsT=w4w[:, b * NG + g, t, :].bitcast(FP4X4),
+                lhsT_scale=w4s[:, b * NG + g, t, :],
+                rhs=zq[b, mh][0].bitcast(FP8X4),
+                rhs_scale=zq[b, mh][1],
+                start=(b == 0),
+                stop=(b == HB - 1),
+            )
+
+        def products(s):
+            q_accs[s] = [psum.tile([P, W], F32, name="q") for t in range(PACK)]
+            gate_accs = [psum.tile([P, W], F32, name="gate") for t in range(PACK)]
+            work = [(q_pass, q_accs[s][t], t) for t in range(PACK)] + [(gate_pass, gate_accs[t], t) for t in range(PACK)]
+            if s == 0:
+                order = [(w, b) for b in range(HB) for w in work]
             else:
-                th[mh, g, u] = ring.tile([P, 2, W], F32, name="pair", bufs=5)
-            dif[mh, g, u] = ring.tile([P, 2, W], F32, name="pair", bufs=5)
-            for k in range(2):
-                t = 2 * u + k
-                gate_acc = psum.tile([P, W], F32, name="acc")
-                q_acc = psum.tile([P, W], F32, name="acc")
-                cols = slice(t * P, (t + 1) * P)
-                for b in range(HB):
-                    nc.tensor.matmul_mx(
-                        q_acc[:],
-                        lhsT=w2q[b, g][0][:, cols].bitcast(FP8X4),
-                        lhsT_scale=w2q[b, g][1][:, cols],
-                        rhs=zq[b, mh][0].bitcast(FP8X4),
-                        rhs_scale=zq[b, mh][1][:],
-                        start=(b == 0),
-                        stop=(b == HB - 1),
-                    )
-                for b in range(HB):
-                    nc.tensor.matmul_mx(
-                        gate_acc[:],
-                        lhsT=w4w[:, b * NG + g, t, :].bitcast(FP4X4),
-                        lhsT_scale=w4s[:, b * NG + g, t, :],
-                        rhs=zq[b, mh][0].bitcast(FP8X4),
-                        rhs_scale=zq[b, mh][1][:],
-                        start=(b == 0),
-                        stop=(b == HB - 1),
-                    )
-                nc.scalar.activation(th[mh, g, u][:, k, :], gate_acc[:], ACT.Tanh, scale=0.5)
-                q_accs[mh, g, t] = q_acc
+                order = [(w, b) for w in work for b in range(HB)]
+            for (one_pass, acc, t), b in order:
+                one_pass(acc, s, t, b)
+            gates[s] = sbuf([P, PACK, W], F32, ("aff01", "aff23")[s % 2])
+            for t in range(PACK):
+                nc.scalar.activation(gates[s][:, t, :], gate_accs[t][:], ACT.Sigmoid)
+
+        def fall_of(s):
+            mh, g = units[s]
+            return falls[g, mh]
 
         def difference(s):
-            mh, g, u, c0, c1 = steps[s]
-            if c0 == 0:
-                products(mh, g, u)
-            for k in range(2):
-                t = 2 * u + k
-                nc.vector.tensor_tensor(
-                    dif[mh, g, u][:, k, c0:c1], q_accs[mh, g, t][:, c0:c1], falls[g, mh][:, t, c0:c1], ALU.subtract
+            difs[s] = sbuf([P, PACK, W], F32, ("raw6", "raw7")[s % 2])
+            for t in range(PACK):
+                nc.vector.tensor_tensor(difs[s][:, t, :], q_accs[s][t][:], fall_of(s)[:, t, :], ALU.subtract)
+
+        def gate(s, cols):
+            d = difs[s][:, :, cols]
+            nc.vector.tensor_tensor(d, gates[s][:, :, cols], d, ALU.mult)
+
+        def flat(tile):
+            return tile[:].rearrange("p t m -> p (t m)")
+
+        def blend_flat(engine, s, c0, c1):
+            y = flat(fall_of(s))[:, c0:c1]
+            engine.tensor_tensor(y, flat(difs[s])[:, c0:c1], y, ALU.add)
+
+        def store_y(s, cols):
+            mh, g = units[s]
+            rows = out_0[g * W : (g + 1) * W, halves[mh]].rearrange("(p t) m -> p t m", t=PACK)
+            nc.sync.dma_start(rows[:, :, cols], fall_of(s)[:, :, cols])
+
+        def planes_out(s, cols, grouped, slot):
+            mh, g = units[s]
+            out_cols = slice(mh * W + cols.start, mh * W + cols.stop)
+            codes = sbuf([P, cols.stop - cols.start], U32, slot)
+            nc.vector.quantize_mx(codes[:].bitcast(FP8X4), y_s[:, g, out_cols], grouped)
+            nc.sync.dma_start(
+                out_1[g, :, out_cols, :].rearrange("p m t -> p (m t)").bitcast(I32), codes[:].bitcast(I32)
+            )
+
+        def scales_out(mh):
+            for q in range(4):
+                eng = nc.sync if q % 2 == 0 else nc.scalar
+                eng.dma_start(
+                    out_2[:, 4 * q : 4 * q + 4, halves[mh]].rearrange("g r m -> r g m").bitcast(I32),
+                    y_s[32 * q : 32 * q + 4, :, halves[mh]].bitcast(I32),
                 )
 
-        def gate(s):
-            mh, g, u, c0, c1 = steps[s]
-            d = dif[mh, g, u][:, :, c0:c1]
-            nc.vector.scalar_tensor_tensor(d, th[mh, g, u][:, :, c0:c1], 1.0, d, ALU.add, ALU.mult)
+        unit_cols = slice(0, W)
+        last = len(units) - 1
 
-        def blend(s):
-            mh, g, u, c0, c1 = steps[s]
-            y = falls[g, mh][:, 2 * u : 2 * u + 2, c0:c1]
-            nc.vector.scalar_tensor_tensor(y, dif[mh, g, u][:, :, c0:c1], 0.5, y, ALU.mult, ALU.add)
-            rows = out_0[g * W : (g + 1) * W, mh * W + c0 : mh * W + c1].rearrange("(p t) m -> p t m", t=PACK)
-            nc.sync.dma_start(rows[:, 2 * u : 2 * u + 2, :], y)
-            if u == 1:
-                ygrouped[s] = grouped_tile()
-                planes = falls[g, mh][:, :, c0:c1]
-                cut = c1 - c0 if s < len(steps) - 1 else LAST_SCALAR_COLS
-                interleave_into(nc.scalar.copy, ygrouped[s], planes, 0, cut)
-                if cut < c1 - c0:
-                    interleave_into(nc.vector.tensor_copy, ygrouped[s], planes, cut, c1 - c0)
+        def finish(s):
+            blend_flat(nc.vector, s, GP_COLS, G)
+            store_y(s, unit_cols)
+            ygrouped[s] = sbuf([P, G], BF16, ("ga", "gb")[s % 2])
+            interleave(nc.scalar.copy, ygrouped[s][:], fall_of(s)[:])
 
-        def planes_out(s):
-            mh, g, u, c0, c1 = steps[s]
-            cols = slice(mh * W + c0, mh * W + c1)
-            codes = ring.tile([P, c1 - c0], U32, name="y_codes", bufs=2, align_bytes=64)
-            nc.vector.quantize_mx(codes[:].bitcast(FP8X4), y_s[:, g, cols], ygrouped[s][:, : PACK * (c1 - c0)])
-            nc.sync.dma_start(out_1[g, :, cols, :].rearrange("p m t -> p (m t)").bitcast(I32), codes[:].bitcast(I32))
-            if g == NG - 1 and c1 == W:
-                for q in range(4):
-                    eng = nc.sync if q % 2 == 0 else nc.scalar
-                    eng.dma_start(
-                        out_2[:, 4 * q : 4 * q + 4, halves[mh]].rearrange("g r m -> r g m").bitcast(I32),
-                        y_s[32 * q : 32 * q + 4, :, halves[mh]].bitcast(I32),
-                    )
+        def unit_planes(s):
+            planes_out(s, unit_cols, ygrouped[s][:], "y_codes%d" % (s % 2))
+            if units[s][1] == NG - 1:
+                scales_out(units[s][0])
 
-        for s in range(len(steps) + 3):
-            if s < len(steps):
-                difference(s)
-            if 1 <= s <= len(steps):
-                blend(s - 1)
-            if s < len(steps):
-                gate(s)
-            if s == 0:
-                grouped = keep.tile([P, PACK * W], BF16, name="gate_first", align_bytes=64)
-                interleave_into(nc.scalar.copy, grouped, zplanes[1][:, :, halves[1]], 0, W)
-            if s == 1:
-                zq[1, 1] = quantise(grouped, "zq11")
-            if s >= 3 and steps[s - 3][2] == 1:
-                planes_out(s - 3)
+        products(0)
+        difference(0)
+        split(zq, quantise(z1g[1][:], W, "w1c1", "w1s1"), [(1, 1)])
+        for s in range(last):
+            products(s + 1)
+            gate(s, unit_cols)
+            blend_flat(nc.gpsimd, s, 0, GP_COLS)
+            difference(s + 1)
+            finish(s)
+            if s >= 1:
+                unit_planes(s - 1)
+
+        pieces = [slice(0, W // 2), slice(W // 2, W)]
+        for cols in pieces:
+            gate(last, cols)
+        tail = []
+        for j, cols in enumerate(pieces):
+            y = fall_of(last)[:, :, cols]
+            nc.vector.tensor_tensor(y, difs[last][:, :, cols], y, ALU.add)
+            store_y(last, cols)
+            width = cols.stop - cols.start
+            grouped = sbuf([P, PACK * width], BF16, ("w1g", "hw567x")[j])
+            cut = width if j < len(pieces) - 1 else LAST_SCALAR_COLS
+            interleave(nc.scalar.copy, grouped[:, : PACK * cut], y[:, :, :cut])
+            tail.append((grouped, y, cut, width))
+            if j == 0:
+                unit_planes(last - 1)
+        for j, cols in enumerate(pieces):
+            grouped, y, cut, width = tail[j]
+            if cut < width:
+                interleave(nc.vector.tensor_copy, grouped[:, PACK * cut :], y[:, :, cut:])
+            planes_out(last, cols, grouped[:], "y_tail%d" % j)
+        scales_out(MH - 1)

@@ -25,8 +25,7 @@ HB = H // W
 NG = N // W
 MH = T2 // W
 PLANES = HB * PACK
-GP_COLS = 768
-GP_LAST_WEIGH = 640
+GP_COLS = 576
 LAST_SCALAR_COLS = 80
 
 
@@ -104,8 +103,9 @@ def tile_list_replacement_item_scores_kernel(
         w4w_raw = sbuf([P, HB, 2 * N], U8, "w4w_raw")
         nc.sync.dma_start(w4w_raw[:].bitcast(I32), w4_words.rearrange("a p c -> p a c").bitcast(I32))
         nc.sync.dma_start(idx2[:], offs2)
-        wg = sbuf([P, S], F32, "wg")
-        nc.sync.dma_start(wg[:], wgs)
+        hz = sbuf([P, PLANES * S], F32, "hz")
+        wg = hz[:, 3 * S : 4 * S]
+        nc.sync.dma_start(wg, wgs)
 
         affs = {}
 
@@ -124,8 +124,8 @@ def tile_list_replacement_item_scores_kernel(
         raw1[2, 1] = load_rows(w1, 2 * W, W, "raw5")
         load_aff(1, aff01[:, T2:])
         raw2[0, 0] = load_rows(w2, 0, 0, "raw6")
-        load_aff(2, aff23[:, :T2])
         raw2[1, 0] = load_rows(w2, W, 0, "raw7")
+        load_aff(2, aff23[:, :T2])
         load_aff(3, aff23[:, T2:])
         load_aff(7, aff7[:])
 
@@ -166,12 +166,11 @@ def tile_list_replacement_item_scores_kernel(
         aff6 = sbuf([P, T2], F32, "tab_w1")
         load_aff(6, aff6[:])
 
-        hz = sbuf([P, PLANES * S], F32, "hz")
         hz16 = hz[:].bitcast(BF16)
         zplane = [hz16[:, n * T2 : (n + 1) * T2] for n in range(PLANES)]
         h0 = sbuf([P, S], F32, "h0")
-        h4 = sbuf([P, S], F32, "h4")
-        hs = [h0[:]] + [hz[:, n * S : (n + 1) * S] for n in range(3)] + [h4[:]] + [hz[:, n * S : (n + 1) * S] for n in range(3, 6)]
+        h12 = sbuf([P, 2, S], F32, "h12")
+        hs = [h0[:], h12[:, 0, :], h12[:, 1, :], hz[:, 2 * S : 3 * S]]
 
         def first_passes(accs, b, passes):
             for a, i in passes:
@@ -190,9 +189,6 @@ def tile_list_replacement_item_scores_kernel(
         def silu(accs, b):
             for i in range(PACK):
                 nc.scalar.activation(hs[b * PACK + i], accs[i][:], ACT.Silu)
-
-        def scatter_fused(n):
-            nc.vector.tensor_tensor(page_of[n][:].indirect(idx2[:]), hs[n], wg[:], ALU.mult)
 
         def scatter(n, hw):
             nc.vector.tensor_copy(page_of[n][:].indirect(idx2[:]), hw)
@@ -214,49 +210,46 @@ def tile_list_replacement_item_scores_kernel(
         falls[1, 1] = load_rows(fall, W, W, "raw5")
         w1g32 = w1g[:].bitcast(F32)
 
-        scatter_fused(0)
-        hw1 = sbuf([P, S], F32, "h0")
-        nc.vector.tensor_tensor(hw1[:], hs[1], wg[:], ALU.mult)
-        scatter(1, hw1[:])
-        weigh(nc.gpsimd, 0, whole)
+        nc.vector.tensor_tensor(hs[0], hs[0], wg, ALU.mult)
+        for n in (1, 2):
+            nc.gpsimd.tensor_tensor(hs[n], hs[n], wg, ALU.mult)
+        for n in range(3):
+            scatter(n, hs[n])
+        for n in range(2):
+            weigh(nc.gpsimd, n, whole)
 
         accs = [psum.tile([P, S], F32, name="gate") for i in range(PACK)]
         codes, scales = quantise(w1g[:, : 2 * G], 2 * W, "w1c3", "w1s3")
         for a in range(2):
             w1q[a, 1] = codes[:, a * W : (a + 1) * W], scales[:, a * W : (a + 1) * W]
-        first_passes(accs, 1, [(a, i) for a in range(2) for i in range(PACK)])
-        hw2 = w1g32[:, 2 * S : 3 * S]
-        nc.vector.tensor_tensor(hw2, hs[2], wg[:], ALU.mult)
-        scatter(2, hw2)
-        weigh(nc.gpsimd, 1, whole)
-
         codes, scales = quantise(w1g[:, 2 * G :], W, "w1c5", "w1s5")
         w1q[2, 1] = codes[:], scales[:]
-        first_passes(accs, 1, [(2, i) for i in range(PACK)])
+        first_passes(accs, 1, [(a, i) for i in range(PACK) for a in range(KP)])
         hw3 = w1g32[:, 4 * S : 5 * S]
-        nc.vector.tensor_tensor(hw3, hs[3], wg[:], ALU.mult)
+        nc.vector.tensor_tensor(hw3, hs[3], wg, ALU.mult)
         scatter(3, hw3)
         weigh(nc.gpsimd, 2, whole)
-        silu(accs, 1)
-
         w2g = [sbuf([P, HB * G], BF16, slot) for slot in ("ga", "gb")]
-        for g in range(NG):
-            for b in range(HB):
-                cast_weight(w2g[g][:, b * G : (b + 1) * G], raw2[b, g])
+        for b in range(HB):
+            cast_weight(w2g[0][:, b * G : (b + 1) * G], raw2[b, 0])
+        h47 = sbuf([P, PACK, S], F32, "raw7")
+        hs.extend([h47[:, i, :] for i in range(PACK)])
+        silu(accs, 1)
+        warm = sbuf([P, 1], F32, "warm")
+        nc.scalar.activation(warm[:], hs[7][:, :1], ACT.Sigmoid)
+        for b in range(HB):
+            cast_weight(w2g[1][:, b * G : (b + 1) * G], raw2[b, 1])
 
-        scatter_fused(4)
-        hw567 = sbuf([P, 3, S], F32, "hw567")
-        nc.vector.tensor_tensor(
-            hw567[:],
-            hz[:, 3 * S : 6 * S].rearrange("p (n s) -> p n s", n=3),
-            wg[:].unsqueeze(1).to_broadcast([P, 3, S]),
-            ALU.mult,
-        )
-        for n in range(5, PLANES):
-            scatter(n, hw567[:, n - 5, :])
+        hw46 = sbuf([P, 3, S], F32, "hw46")
+        nc.vector.tensor_tensor(hw46[:], h47[:, :3, :], wg.unsqueeze(1).to_broadcast([P, 3, S]), ALU.mult)
+        hw7 = h47[:, 0, :]
+        nc.gpsimd.tensor_tensor(hw7, hs[7], wg, ALU.mult)
+        for n in range(3):
+            scatter(4 + n, hw46[:, n, :])
+        scatter(7, hw7)
         for n in range(3, PLANES - 2):
             weigh(nc.gpsimd, n, whole)
-        weigh(nc.gpsimd, PLANES - 2, slice(0, GP_LAST_WEIGH))
+        weigh(nc.gpsimd, PLANES - 2, halves[0])
         weigh(nc.vector, PLANES - 1, halves[0])
 
         def zplanes(b, cols):
@@ -274,12 +267,12 @@ def tile_list_replacement_item_scores_kernel(
             for j, key in enumerate(keys):
                 store[key] = codes[:, j * W : (j + 1) * W], scales[:, j * W : (j + 1) * W]
 
-        split(w2q, quantise(w2g[0][:], HB * W, "hw567", "w2s0"), [(0, 0), (1, 0)])
-        split(zq, quantise(z0g[:], MH * W, "w4w_raw", "zs0"), [(0, 0), (0, 1)])
-        split(zq, quantise(z1g[0][:], W, "w1c0", "w1s0"), [(1, 0)])
-        weigh(nc.vector, PLANES - 2, slice(GP_LAST_WEIGH, T2))
         weigh(nc.vector, PLANES - 1, halves[1])
+        weigh(nc.vector, PLANES - 2, halves[1])
         interleave(nc.scalar.copy, z1g[1][:], zplanes(1, halves[1]))
+        split(zq, quantise(z0g[:], MH * W, "raw7", "zs0"), [(0, 0), (0, 1)])
+        split(w2q, quantise(w2g[0][:], HB * W, "tab_w0", "w2s0"), [(0, 0), (1, 0)])
+        split(zq, quantise(z1g[0][:], W, "w1c0", "w1s0"), [(1, 0)])
         split(w2q, quantise(w2g[1][:], HB * W, "gc", "w2s1"), [(0, 1), (1, 1)])
 
         y_s = sbuf([P, NG, T2], U8, "y_s")
@@ -319,7 +312,7 @@ def tile_list_replacement_item_scores_kernel(
             gate_accs = [psum.tile([P, W], F32, name="gate") for t in range(PACK)]
             work = [(q_pass, q_accs[s][t], t) for t in range(PACK)] + [(gate_pass, gate_accs[t], t) for t in range(PACK)]
             if s == 0:
-                order = [(w, b) for b in range(HB) for w in work]
+                order = [(w, 0) for w in work[PACK:] + work[:PACK]] + [(w, 1) for w in work]
             else:
                 order = [(w, b) for w in work for b in range(HB)]
             for (one_pass, acc, t), b in order:
@@ -333,7 +326,7 @@ def tile_list_replacement_item_scores_kernel(
             return falls[g, mh]
 
         def difference(s):
-            difs[s] = sbuf([P, PACK, W], F32, ("raw6", "raw7")[s % 2])
+            difs[s] = sbuf([P, PACK, W], F32, ("raw6", "raw0")[s % 2])
             for t in range(PACK):
                 nc.vector.tensor_tensor(difs[s][:, t, :], q_accs[s][t][:], fall_of(s)[:, t, :], ALU.subtract)
 
@@ -385,8 +378,8 @@ def tile_list_replacement_item_scores_kernel(
                 scales_out(units[s][0])
 
         products(0)
-        difference(0)
         split(zq, quantise(z1g[1][:], W, "w1c1", "w1s1"), [(1, 1)])
+        difference(0)
         for s in range(last):
             products(s + 1)
             gate(s, unit_cols)
@@ -405,7 +398,7 @@ def tile_list_replacement_item_scores_kernel(
             nc.vector.tensor_tensor(y, difs[last][:, :, cols], y, ALU.add)
             store_y(last, cols)
             width = cols.stop - cols.start
-            grouped = sbuf([P, PACK * width], BF16, ("w1g", "hw567x")[j])
+            grouped = sbuf([P, PACK * width], BF16, ("w1g", "hw46")[j])
             cut = width if j < len(pieces) - 1 else LAST_SCALAR_COLS
             interleave(nc.scalar.copy, grouped[:, : PACK * cut], y[:, :, :cut])
             tail.append((grouped, y, cut, width))

@@ -26,6 +26,7 @@ NG = N // W
 MH = T2 // W
 PLANES = HB * PACK
 GP_COLS = 576
+TIE_COLS = 16
 LAST_SCALAR_COLS = 80
 
 
@@ -52,11 +53,14 @@ def tile_list_replacement_item_scores_kernel(
                 nc.sync.dma_start(raw[:, j : j + step, :], rows[:, j : j + step, :])
             return raw
 
-        def cast_weight(grouped, raw):
-            nc.scalar.copy(
-                grouped.rearrange("p (t m j) -> p m j t", t=PACK, j=PACK),
-                raw[:].rearrange("p j (m t) -> p m j t", t=PACK),
+        def cast_part(copy, grouped, raw, m0, m1):
+            copy(
+                grouped.rearrange("p (t m j) -> p m j t", t=PACK, j=PACK)[:, m0:m1],
+                raw[:].rearrange("p j (m t) -> p m j t", t=PACK)[:, m0:m1],
             )
+
+        def cast_weight(grouped, raw):
+            cast_part(nc.scalar.copy, grouped, raw, 0, P)
 
         def interleave(copy, grouped, planes):
             copy(
@@ -91,14 +95,14 @@ def tile_list_replacement_item_scores_kernel(
         raw1 = {}
         raw1[0, 0] = load_rows(w1, 0, 0, "raw0", 4)
         raw1[1, 0] = load_rows(w1, W, 0, "raw1", 2)
-        load_table(0)
-        raw1[2, 0] = load_rows(w1, 2 * W, 0, "raw2")
         for q in range(4):
             nc.sync.dma_start(
                 w4s_raw[32 * q : 32 * q + 4, :, :].bitcast(I32),
                 w4_scales[:, 4 * q : 4 * q + 4, :].rearrange("a r n -> r a n").bitcast(I32),
             )
+        load_table(0)
         load_table(1)
+        raw1[2, 0] = load_rows(w1, 2 * W, 0, "raw2")
         load_table(2)
         w4w_raw = sbuf([P, HB, 2 * N], U8, "w4w_raw")
         nc.sync.dma_start(w4w_raw[:].bitcast(I32), w4_words.rearrange("a p c -> p a c").bitcast(I32))
@@ -136,20 +140,22 @@ def tile_list_replacement_item_scores_kernel(
         def gather_words(a):
             nc.vector.tensor_copy(v_w[a][:], tab_w[a][:].indirect(idx[:]))
 
-        def head_weight(a, slot):
+        def head_weight(a, slot, scalar_places):
             grouped = sbuf([P, G], BF16, slot)
-            cast_weight(grouped[:], raw1[a, 0])
+            cast_part(nc.scalar.copy, grouped[:], raw1[a, 0], 0, scalar_places)
+            if scalar_places < P:
+                cast_part(nc.vector.tensor_copy, grouped[:], raw1[a, 0], scalar_places, P)
             codes, scales = quantise(grouped[:], W, "w1c%d" % a, "w1s%d" % a)
             w1q[a, 0] = codes[:], scales[:]
 
         nc.vector.tensor_copy(v_s[:], tab_s[:].indirect(idx[:]))
-        head_weight(0, "ga")
-        head_weight(1, "gb")
+        head_weight(0, "ga", P)
+        head_weight(1, "gb", P)
         gather_words(0)
+        gather_words(1)
         w4s = sbuf([P, HB * NG, PACK, P], U8, "w4s")
         nc.vector.tensor_copy(w4s[:], w4s_raw[:].rearrange("p a (g m t) -> p (a g) t m", g=NG, t=PACK))
-        head_weight(2, "gc")
-        gather_words(1)
+        head_weight(2, "gc", P // 2)
         gather_words(2)
         w4w = sbuf([P, HB * NG, PACK, 2 * P], U8, "tab_w2")
         nc.vector.tensor_copy(
@@ -202,7 +208,7 @@ def tile_list_replacement_item_scores_kernel(
         accs = [psum.tile([P, S], F32, name="q") for i in range(PACK)]
         first_passes(accs, 0, [(a, i) for a in range(KP) for i in range(PACK)])
         silu(accs, 0)
-        w1g = sbuf([P, KP * G], BF16, "w1g")
+        w1g = sbuf([P, KP * G + 2 * (S - TIE_COLS)], BF16, "w1g")
         for a in range(KP):
             cast_weight(w1g[:, a * G : (a + 1) * G], raw1[a, 1])
         falls[1, 0] = load_rows(fall, W, 0, "raw3")
@@ -213,20 +219,22 @@ def tile_list_replacement_item_scores_kernel(
         nc.vector.tensor_tensor(hs[0], hs[0], wg, ALU.mult)
         for n in (1, 2):
             nc.gpsimd.tensor_tensor(hs[n], hs[n], wg, ALU.mult)
+        hw3 = w1g32[:, KP * G // 2 - TIE_COLS :]
+        nc.gpsimd.tensor_tensor(hw3[:, TIE_COLS:], hs[3][:, TIE_COLS:], wg[:, TIE_COLS:], ALU.mult)
         for n in range(3):
             scatter(n, hs[n])
         for n in range(2):
             weigh(nc.gpsimd, n, whole)
 
         accs = [psum.tile([P, S], F32, name="gate") for i in range(PACK)]
-        codes, scales = quantise(w1g[:, : 2 * G], 2 * W, "w1c3", "w1s3")
-        for a in range(2):
-            w1q[a, 1] = codes[:, a * W : (a + 1) * W], scales[:, a * W : (a + 1) * W]
-        codes, scales = quantise(w1g[:, 2 * G :], W, "w1c5", "w1s5")
-        w1q[2, 1] = codes[:], scales[:]
-        first_passes(accs, 1, [(a, i) for i in range(PACK) for a in range(KP)])
-        hw3 = w1g32[:, 4 * S : 5 * S]
-        nc.vector.tensor_tensor(hw3, hs[3], wg, ALU.mult)
+        codes, scales = quantise(w1g[:, :G], W, "h12", "w1s5")
+        w1q[0, 1] = codes[:], scales[:]
+        first_passes(accs, 1, [(0, i) for i in range(PACK)])
+        codes, scales = quantise(w1g[:, G : KP * G], 2 * W, "w1c3", "w1s3")
+        for a in range(1, KP):
+            w1q[a, 1] = codes[:, (a - 1) * W : a * W], scales[:, (a - 1) * W : a * W]
+        first_passes(accs, 1, [(a, i) for i in range(PACK) for a in range(1, KP)])
+        nc.vector.tensor_tensor(hw3[:, :TIE_COLS], hs[3][:, :TIE_COLS], wg[:, :TIE_COLS], ALU.mult)
         scatter(3, hw3)
         weigh(nc.gpsimd, 2, whole)
         w2g = [sbuf([P, HB * G], BF16, slot) for slot in ("ga", "gb")]
@@ -240,16 +248,17 @@ def tile_list_replacement_item_scores_kernel(
         for b in range(HB):
             cast_weight(w2g[1][:, b * G : (b + 1) * G], raw2[b, 1])
 
-        hw46 = sbuf([P, 3, S], F32, "hw46")
-        nc.vector.tensor_tensor(hw46[:], h47[:, :3, :], wg.unsqueeze(1).to_broadcast([P, 3, S]), ALU.mult)
-        hw7 = h47[:, 0, :]
-        nc.gpsimd.tensor_tensor(hw7, hs[7], wg, ALU.mult)
-        for n in range(3):
-            scatter(4 + n, hw46[:, n, :])
-        scatter(7, hw7)
-        for n in range(3, PLANES - 2):
+        wg2 = wg.unsqueeze(1).to_broadcast([P, 2, S])
+        hw45 = sbuf([P, 2, S], F32, "hw45")
+        nc.vector.tensor_tensor(hw45[:], h47[:, :2, :], wg2, ALU.mult)
+        hw67 = h47[:, :2, :]
+        nc.gpsimd.tensor_tensor(hw67, h47[:, 2:, :], wg2, ALU.mult)
+        for n in range(2):
+            scatter(4 + n, hw45[:, n, :])
+        for n in range(2):
+            scatter(6 + n, hw67[:, n, :])
+        for n in range(3, PLANES - 1):
             weigh(nc.gpsimd, n, whole)
-        weigh(nc.gpsimd, PLANES - 2, halves[0])
         weigh(nc.vector, PLANES - 1, halves[0])
 
         def zplanes(b, cols):
@@ -268,7 +277,6 @@ def tile_list_replacement_item_scores_kernel(
                 store[key] = codes[:, j * W : (j + 1) * W], scales[:, j * W : (j + 1) * W]
 
         weigh(nc.vector, PLANES - 1, halves[1])
-        weigh(nc.vector, PLANES - 2, halves[1])
         interleave(nc.scalar.copy, z1g[1][:], zplanes(1, halves[1]))
         split(zq, quantise(z0g[:], MH * W, "raw7", "zs0"), [(0, 0), (0, 1)])
         split(w2q, quantise(w2g[0][:], HB * W, "tab_w0", "w2s0"), [(0, 0), (1, 0)])
@@ -277,7 +285,8 @@ def tile_list_replacement_item_scores_kernel(
 
         y_s = sbuf([P, NG, T2], U8, "y_s")
         units = [(mh, g) for mh in range(MH) for g in range(NG)]
-        gates = {}
+        rests = {}
+        kept = {}
         difs = {}
         q_accs = {}
         ygrouped = {}
@@ -310,41 +319,45 @@ def tile_list_replacement_item_scores_kernel(
         def products(s):
             q_accs[s] = [psum.tile([P, W], F32, name="q") for t in range(PACK)]
             gate_accs = [psum.tile([P, W], F32, name="gate") for t in range(PACK)]
-            work = [(q_pass, q_accs[s][t], t) for t in range(PACK)] + [(gate_pass, gate_accs[t], t) for t in range(PACK)]
+            work = [w for t in range(PACK) for w in ((gate_pass, gate_accs[t], t), (q_pass, q_accs[s][t], t))]
             if s == 0:
-                order = [(w, 0) for w in work[PACK:] + work[:PACK]] + [(w, 1) for w in work]
+                order = [(w, 0) for w in work[0::2] + work[1::2]] + [(w, 1) for w in work]
             else:
-                order = [(w, b) for w in work for b in range(HB)]
+                order = [(w, b) for w in work[0::2] + work[1::2] for b in range(HB)]
             for (one_pass, acc, t), b in order:
                 one_pass(acc, s, t, b)
-            gates[s] = sbuf([P, PACK, W], F32, ("aff01", "aff23")[s % 2])
+            rests[s] = sbuf([P, PACK, W], F32, ("aff01", "aff23")[s % 2])
             for t in range(PACK):
-                nc.scalar.activation(gates[s][:, t, :], gate_accs[t][:], ACT.Sigmoid)
+                nc.scalar.activation(rests[s][:, t, :], gate_accs[t][:], ACT.Sigmoid, scale=-1.0)
 
         def fall_of(s):
             mh, g = units[s]
             return falls[g, mh]
 
-        def difference(s):
-            difs[s] = sbuf([P, PACK, W], F32, ("raw6", "raw0")[s % 2])
-            for t in range(PACK):
-                nc.vector.tensor_tensor(difs[s][:, t, :], q_accs[s][t][:], fall_of(s)[:, t, :], ALU.subtract)
-
-        def gate(s, cols):
-            d = difs[s][:, :, cols]
-            nc.vector.tensor_tensor(d, gates[s][:, :, cols], d, ALU.mult)
-
         def flat(tile):
             return tile[:].rearrange("p t m -> p (t m)")
 
-        def blend_flat(engine, s, c0, c1):
-            y = flat(fall_of(s))[:, c0:c1]
-            engine.tensor_tensor(y, flat(difs[s])[:, c0:c1], y, ALU.add)
+        def gated(s):
+            kept[s] = sbuf([P, PACK, W], F32, "gb")
+            nc.gpsimd.tensor_tensor(
+                flat(kept[s])[:, :GP_COLS], flat(rests[s])[:, :GP_COLS], flat(fall_of(s))[:, :GP_COLS], ALU.mult
+            )
+            difs[s] = sbuf([P, PACK, W], F32, ("raw6", "raw1")[s % 2])
+            for t in range(PACK):
+                nc.vector.scalar_tensor_tensor(
+                    difs[s][:, t, :], rests[s][:, t, :], 1.0, q_accs[s][t][:], ALU.subtract, ALU.mult
+                )
+            nc.vector.tensor_tensor(
+                flat(kept[s])[:, GP_COLS:], flat(rests[s])[:, GP_COLS:], flat(fall_of(s))[:, GP_COLS:], ALU.mult
+            )
 
-        def store_y(s, cols):
+        def blend(s, cols):
             mh, g = units[s]
+            y = fall_of(s)[:, :, cols]
+            nc.vector.tensor_tensor(y, kept[s][:, :, cols], difs[s][:, :, cols], ALU.subtract)
             rows = out_0[g * W : (g + 1) * W, halves[mh]].rearrange("(p t) m -> p t m", t=PACK)
-            nc.sync.dma_start(rows[:, :, cols], fall_of(s)[:, :, cols])
+            nc.sync.dma_start(rows[:, :, cols], y)
+            return y
 
         def planes_out(s, cols, grouped, slot):
             mh, g = units[s]
@@ -366,44 +379,35 @@ def tile_list_replacement_item_scores_kernel(
         unit_cols = slice(0, W)
         last = len(units) - 1
 
-        def finish(s):
-            blend_flat(nc.vector, s, GP_COLS, G)
-            store_y(s, unit_cols)
-            ygrouped[s] = sbuf([P, G], BF16, ("ga", "gb")[s % 2])
-            interleave(nc.scalar.copy, ygrouped[s][:], fall_of(s)[:])
-
         def unit_planes(s):
             planes_out(s, unit_cols, ygrouped[s][:], "y_codes%d" % (s % 2))
             if units[s][1] == NG - 1:
                 scales_out(units[s][0])
 
         products(0)
-        split(zq, quantise(z1g[1][:], W, "w1c1", "w1s1"), [(1, 1)])
-        difference(0)
         for s in range(last):
+            gated(s)
             products(s + 1)
-            gate(s, unit_cols)
-            blend_flat(nc.gpsimd, s, 0, GP_COLS)
-            difference(s + 1)
-            finish(s)
-            if s >= 1:
+            if s == 0:
+                split(zq, quantise(z1g[1][:], W, "w1c1", "w1s1"), [(1, 1)])
+            else:
                 unit_planes(s - 1)
+            y = blend(s, unit_cols)
+            ygrouped[s] = sbuf([P, G], BF16, ("ga", "raw0")[s % 2])
+            interleave(nc.scalar.copy, ygrouped[s][:], y)
+        gated(last)
 
         pieces = [slice(0, W // 2), slice(W // 2, W)]
-        for cols in pieces:
-            gate(last, cols)
         tail = []
         for j, cols in enumerate(pieces):
-            y = fall_of(last)[:, :, cols]
-            nc.vector.tensor_tensor(y, difs[last][:, :, cols], y, ALU.add)
-            store_y(last, cols)
+            if j == 0:
+                unit_planes(last - 1)
+            y = blend(last, cols)
             width = cols.stop - cols.start
-            grouped = sbuf([P, PACK * width], BF16, ("w1g", "hw46")[j])
+            grouped = sbuf([P, PACK * width], BF16, ("w1g", "hw45")[j])
             cut = width if j < len(pieces) - 1 else LAST_SCALAR_COLS
             interleave(nc.scalar.copy, grouped[:, : PACK * cut], y[:, :, :cut])
             tail.append((grouped, y, cut, width))
-            if j == 0:
-                unit_planes(last - 1)
         for j, cols in enumerate(pieces):
             grouped, y, cut, width = tail[j]
             if cut < width:

@@ -25,8 +25,10 @@ HB = H // W
 NG = N // W
 MH = T2 // W
 PLANES = HB * PACK
-GP_COLS = 576
+GP_FIRST_COLS = 576
+GP_COLS = 704
 TIE_COLS = 16
+EARLY_GATES, EARLY_QS = 2, 1
 LAST_SCALAR_COLS = 80
 
 
@@ -268,19 +270,18 @@ def tile_list_replacement_item_scores_kernel(
         w2q = {}
         z0g = sbuf([P, MH * G], BF16, "tab_w0")
         interleave(nc.scalar.copy, z0g[:], zplanes(0, whole))
-        z1g = [sbuf([P, G], BF16, slot) for slot in ("gc", "w1g")]
-        interleave(nc.scalar.copy, z1g[0][:], zplanes(1, halves[0]))
+        z1g = sbuf([P, G], BF16, "gc")
+        interleave(nc.scalar.copy, z1g[:], zplanes(1, halves[0]))
 
         def split(store, pair, keys):
             codes, scales = pair
             for j, key in enumerate(keys):
                 store[key] = codes[:, j * W : (j + 1) * W], scales[:, j * W : (j + 1) * W]
 
-        weigh(nc.vector, PLANES - 1, halves[1])
-        interleave(nc.scalar.copy, z1g[1][:], zplanes(1, halves[1]))
         split(zq, quantise(z0g[:], MH * W, "raw7", "zs0"), [(0, 0), (0, 1)])
         split(w2q, quantise(w2g[0][:], HB * W, "tab_w0", "w2s0"), [(0, 0), (1, 0)])
-        split(zq, quantise(z1g[0][:], W, "w1c0", "w1s0"), [(1, 0)])
+        weigh(nc.vector, PLANES - 1, halves[1])
+        split(zq, quantise(z1g[:], W, "w1c0", "w1s0"), [(1, 0)])
         split(w2q, quantise(w2g[1][:], HB * W, "gc", "w2s1"), [(0, 1), (1, 1)])
 
         y_s = sbuf([P, NG, T2], U8, "y_s")
@@ -291,7 +292,7 @@ def tile_list_replacement_item_scores_kernel(
         q_accs = {}
         ygrouped = {}
 
-        def q_pass(acc, s, t, b):
+        def q_pass(acc, s, t, b, first):
             mh, g = units[s]
             cols = slice(t * P, (t + 1) * P)
             nc.tensor.matmul_mx(
@@ -300,11 +301,11 @@ def tile_list_replacement_item_scores_kernel(
                 lhsT_scale=w2q[b, g][1][:, cols],
                 rhs=zq[b, mh][0].bitcast(FP8X4),
                 rhs_scale=zq[b, mh][1],
-                start=(b == 0),
-                stop=(b == HB - 1),
+                start=first,
+                stop=not first,
             )
 
-        def gate_pass(acc, s, t, b):
+        def gate_pass(acc, s, t, b, first):
             mh, g = units[s]
             nc.tensor.matmul_mx(
                 acc[:],
@@ -312,20 +313,27 @@ def tile_list_replacement_item_scores_kernel(
                 lhsT_scale=w4s[:, b * NG + g, t, :],
                 rhs=zq[b, mh][0].bitcast(FP8X4),
                 rhs_scale=zq[b, mh][1],
-                start=(b == 0),
-                stop=(b == HB - 1),
+                start=first,
+                stop=not first,
             )
 
         def products(s):
             q_accs[s] = [psum.tile([P, W], F32, name="q") for t in range(PACK)]
             gate_accs = [psum.tile([P, W], F32, name="gate") for t in range(PACK)]
-            work = [w for t in range(PACK) for w in ((gate_pass, gate_accs[t], t), (q_pass, q_accs[s][t], t))]
+            gate_work = [(gate_pass, gate_accs[t], t) for t in range(PACK)]
+            q_work = [(q_pass, q_accs[s][t], t) for t in range(PACK)]
             if s == 0:
-                order = [(w, 0) for w in work[0::2] + work[1::2]] + [(w, 1) for w in work]
+                for one_pass, acc, t in gate_work[:EARLY_GATES] + q_work[:EARLY_QS]:
+                    one_pass(acc, s, t, 0, True)
+                for t in range(PACK):
+                    for (one_pass, acc, t), late in ((gate_work[t], t >= EARLY_GATES), (q_work[t], t >= EARLY_QS)):
+                        one_pass(acc, s, t, 1, late)
+                        if late:
+                            one_pass(acc, s, t, 0, False)
             else:
-                order = [(w, b) for w in work[0::2] + work[1::2] for b in range(HB)]
-            for (one_pass, acc, t), b in order:
-                one_pass(acc, s, t, b)
+                for one_pass, acc, t in gate_work + q_work:
+                    for b in range(HB):
+                        one_pass(acc, s, t, b, b == 0)
             rests[s] = sbuf([P, PACK, W], F32, ("aff01", "aff23")[s % 2])
             for t in range(PACK):
                 nc.scalar.activation(rests[s][:, t, :], gate_accs[t][:], ACT.Sigmoid, scale=-1.0)
@@ -337,19 +345,21 @@ def tile_list_replacement_item_scores_kernel(
         def flat(tile):
             return tile[:].rearrange("p t m -> p (t m)")
 
-        def gated(s):
-            kept[s] = sbuf([P, PACK, W], F32, "gb")
-            nc.gpsimd.tensor_tensor(
-                flat(kept[s])[:, :GP_COLS], flat(rests[s])[:, :GP_COLS], flat(fall_of(s))[:, :GP_COLS], ALU.mult
+        def times_q(s, t):
+            nc.vector.scalar_tensor_tensor(
+                difs[s][:, t, :], rests[s][:, t, :], 1.0, q_accs[s][t][:], ALU.subtract, ALU.mult
             )
-            difs[s] = sbuf([P, PACK, W], F32, ("raw6", "raw1")[s % 2])
-            for t in range(PACK):
-                nc.vector.scalar_tensor_tensor(
-                    difs[s][:, t, :], rests[s][:, t, :], 1.0, q_accs[s][t][:], ALU.subtract, ALU.mult
-                )
-            nc.vector.tensor_tensor(
-                flat(kept[s])[:, GP_COLS:], flat(rests[s])[:, GP_COLS:], flat(fall_of(s))[:, GP_COLS:], ALU.mult
+
+        def times_fall(engine, s, c0, c1):
+            engine.tensor_tensor(
+                flat(kept[s])[:, c0:c1], flat(rests[s])[:, c0:c1], flat(fall_of(s))[:, c0:c1], ALU.mult
             )
+
+        def open_unit(s):
+            difs[s] = sbuf([P, PACK, W], F32, ("raw6", "raw1", "raw0", "raw1")[s])
+            kept[s] = sbuf([P, PACK, W], F32, unit_slots[s % 2])
+
+        unit_slots = ("ga", "raw6")
 
         def blend(s, cols):
             mh, g = units[s]
@@ -359,12 +369,12 @@ def tile_list_replacement_item_scores_kernel(
             nc.sync.dma_start(rows[:, :, cols], y)
             return y
 
-        def planes_out(s, cols, grouped, slot):
+        def planes_out(s, cols, grouped, slot, queue):
             mh, g = units[s]
             out_cols = slice(mh * W + cols.start, mh * W + cols.stop)
             codes = sbuf([P, cols.stop - cols.start], U32, slot)
             nc.vector.quantize_mx(codes[:].bitcast(FP8X4), y_s[:, g, out_cols], grouped)
-            nc.sync.dma_start(
+            queue.dma_start(
                 out_1[g, :, out_cols, :].rearrange("p m t -> p (m t)").bitcast(I32), codes[:].bitcast(I32)
             )
 
@@ -380,22 +390,34 @@ def tile_list_replacement_item_scores_kernel(
         last = len(units) - 1
 
         def unit_planes(s):
-            planes_out(s, unit_cols, ygrouped[s][:], "y_codes%d" % (s % 2))
+            planes_out(s, unit_cols, ygrouped[s][:], "y_codes%d" % (s % 2), nc.sync)
             if units[s][1] == NG - 1:
                 scales_out(units[s][0])
 
         products(0)
-        for s in range(last):
-            gated(s)
-            products(s + 1)
-            if s == 0:
-                split(zq, quantise(z1g[1][:], W, "w1c1", "w1s1"), [(1, 1)])
-            else:
+        open_unit(0)
+        for t in range(PACK):
+            times_fall(nc.vector, 0, t * W, (t + 1) * W)
+            times_q(0, t)
+        products(1)
+        z1g = sbuf([P, G], BF16, "aff01")
+        interleave(nc.scalar.copy, z1g[:], zplanes(1, halves[1]))
+        for s in range(1, len(units)):
+            y = blend(s - 1, unit_cols)
+            open_unit(s)
+            ygrouped[s - 1] = sbuf([P, G], BF16, unit_slots[(s - 1) % 2])
+            interleave(nc.scalar.copy, ygrouped[s - 1][:], y)
+            share = GP_FIRST_COLS if s == 1 else GP_COLS
+            times_fall(nc.gpsimd, s, 0, share)
+            for t in range(PACK):
+                times_q(s, t)
+            if s == 1:
+                split(zq, quantise(z1g[:], W, "w1c1", "w1s1"), [(1, 1)])
+            if s < last:
+                products(s + 1)
+            times_fall(nc.vector, s, share, G)
+            if s < last:
                 unit_planes(s - 1)
-            y = blend(s, unit_cols)
-            ygrouped[s] = sbuf([P, G], BF16, ("ga", "raw0")[s % 2])
-            interleave(nc.scalar.copy, ygrouped[s][:], y)
-        gated(last)
 
         pieces = [slice(0, W // 2), slice(W // 2, W)]
         tail = []
@@ -412,5 +434,5 @@ def tile_list_replacement_item_scores_kernel(
             grouped, y, cut, width = tail[j]
             if cut < width:
                 interleave(nc.vector.tensor_copy, grouped[:, PACK * cut :], y[:, :, cut:])
-            planes_out(last, cols, grouped[:], "y_tail%d" % j)
+            planes_out(last, cols, grouped[:], "y_tail%d" % j, nc.scalar)
         scales_out(MH - 1)

@@ -25,10 +25,11 @@ HB = H // W
 NG = N // W
 MH = T2 // W
 PLANES = HB * PACK
-GP_FIRST_COLS = 576
-GP_COLS = 704
+C = 256
+GP_COLS = 752
+GP_END_COLS = 320
+PLANES_LAG = 3
 TIE_COLS = 16
-EARLY_GATES, EARLY_QS = 2, 1
 LAST_SCALAR_COLS = 80
 
 
@@ -38,7 +39,7 @@ def tile_list_replacement_item_scores_kernel(
     nc = tc.nc
     with ExitStack() as ctx:
         keep = ctx.enter_context(tc.tile_pool(name="keep", bufs=1))
-        psum = ctx.enter_context(tc.psum_pool(name="psum", bufs=4))
+        psum = ctx.enter_context(tc.psum_pool(name="psum", bufs=1))
 
         def sbuf(shape, dtype, slot):
             return keep.tile(shape, dtype, name=slot, align_bytes=64)
@@ -207,7 +208,7 @@ def tile_list_replacement_item_scores_kernel(
         whole = slice(0, T2)
         halves = [slice(mh * W, (mh + 1) * W) for mh in range(MH)]
 
-        accs = [psum.tile([P, S], F32, name="q") for i in range(PACK)]
+        accs = [psum.tile([P, S], F32, name="q", bufs=6) for i in range(PACK)]
         first_passes(accs, 0, [(a, i) for a in range(KP) for i in range(PACK)])
         silu(accs, 0)
         w1g = sbuf([P, KP * G + 2 * (S - TIE_COLS)], BF16, "w1g")
@@ -228,7 +229,8 @@ def tile_list_replacement_item_scores_kernel(
         for n in range(2):
             weigh(nc.gpsimd, n, whole)
 
-        accs = [psum.tile([P, S], F32, name="gate") for i in range(PACK)]
+        accs = [psum.tile([P, S], F32, name="q", bufs=6) for i in range(2)]
+        accs = accs + [psum.tile([P, S], F32, name="gate", bufs=2) for i in range(2)]
         codes, scales = quantise(w1g[:, :G], W, "h12", "w1s5")
         w1q[0, 1] = codes[:], scales[:]
         first_passes(accs, 1, [(0, i) for i in range(PACK)])
@@ -261,118 +263,109 @@ def tile_list_replacement_item_scores_kernel(
             scatter(6 + n, hw67[:, n, :])
         for n in range(3, PLANES - 1):
             weigh(nc.gpsimd, n, whole)
-        weigh(nc.vector, PLANES - 1, halves[0])
+        quarters = [slice(j * C, (j + 1) * C) for j in range(T2 // C)]
+        weigh(nc.vector, PLANES - 1, quarters[0])
 
         def zplanes(b, cols):
             return hz16[:, b * PACK * T2 : (b + 1) * PACK * T2].rearrange("p (t m) -> p t m", t=PACK)[:, :, cols]
 
-        zq = {}
-        w2q = {}
-        z0g = sbuf([P, MH * G], BF16, "tab_w0")
-        interleave(nc.scalar.copy, z0g[:], zplanes(0, whole))
-        z1g = sbuf([P, G], BF16, "gc")
-        interleave(nc.scalar.copy, z1g[:], zplanes(1, halves[0]))
-
-        def split(store, pair, keys):
+        def split(store, pair, keys, width):
             codes, scales = pair
             for j, key in enumerate(keys):
-                store[key] = codes[:, j * W : (j + 1) * W], scales[:, j * W : (j + 1) * W]
+                store[key] = codes[:, j * width : (j + 1) * width], scales[:, j * width : (j + 1) * width]
 
-        split(zq, quantise(z0g[:], MH * W, "raw7", "zs0"), [(0, 0), (0, 1)])
-        split(w2q, quantise(w2g[0][:], HB * W, "tab_w0", "w2s0"), [(0, 0), (1, 0)])
+        zq = {}
+        w2q = {}
+        z0g = sbuf([P, PACK * T2], BF16, "tab_w0")
+        interleave(nc.scalar.copy, z0g[:], zplanes(0, whole))
+        z1g = [sbuf([P, PACK * C], BF16, slot) for slot in ("h0", "gc")]
+        interleave(nc.scalar.copy, z1g[0][:], zplanes(1, quarters[0]))
+        split(zq, quantise(z0g[:], T2, "raw7", "zs0"), [(0, j) for j in range(4)], C)
+        weigh(nc.vector, PLANES - 1, quarters[1])
+        interleave(nc.scalar.copy, z1g[1][:], zplanes(1, quarters[1]))
+        split(zq, quantise(z1g[0][:], C, "w1c0", "w1s0"), [(1, 0)], C)
+        split(w2q, quantise(w2g[0][:], HB * W, "tab_w0", "w2s0"), [(0, 0), (1, 0)], W)
         weigh(nc.vector, PLANES - 1, halves[1])
-        split(zq, quantise(z1g[:], W, "w1c0", "w1s0"), [(1, 0)])
-        split(w2q, quantise(w2g[1][:], HB * W, "gc", "w2s1"), [(0, 1), (1, 1)])
+        split(zq, quantise(z1g[1][:], C, "w1c2", "w1s2"), [(1, 1)], C)
+        split(w2q, quantise(w2g[1][:], HB * W, "gc", "w2s1"), [(0, 1), (1, 1)], W)
 
         y_s = sbuf([P, NG, T2], U8, "y_s")
-        units = [(mh, g) for mh in range(MH) for g in range(NG)]
+        steps = [(mh, g, j) for mh in range(MH) for g in range(NG) for j in range(W // C)]
+        last = len(steps) - 1
         rests = {}
-        kept = {}
         difs = {}
-        q_accs = {}
+        pulls = {}
+        q_banks = {}
         ygrouped = {}
 
-        def q_pass(acc, s, t, b, first):
-            mh, g = units[s]
+        def fill_bank(bank, k, pair, stationary):
+            mh, g, j = steps[k]
+            for b in range(HB):
+                for e in range(2):
+                    words, scales = stationary(b, g, 2 * pair + e)
+                    nc.tensor.matmul_mx(
+                        bank[:, e, :],
+                        lhsT=words,
+                        lhsT_scale=scales,
+                        rhs=zq[b, 2 * mh + j][0].bitcast(FP8X4),
+                        rhs_scale=zq[b, 2 * mh + j][1],
+                        start=(b == 0 and e == 0),
+                        stop=(b == HB - 1 and e == 1),
+                    )
+
+        def w2_columns(b, g, t):
             cols = slice(t * P, (t + 1) * P)
-            nc.tensor.matmul_mx(
-                acc[:],
-                lhsT=w2q[b, g][0][:, cols].bitcast(FP8X4),
-                lhsT_scale=w2q[b, g][1][:, cols],
-                rhs=zq[b, mh][0].bitcast(FP8X4),
-                rhs_scale=zq[b, mh][1],
-                start=first,
-                stop=not first,
-            )
+            return w2q[b, g][0][:, cols].bitcast(FP8X4), w2q[b, g][1][:, cols]
 
-        def gate_pass(acc, s, t, b, first):
-            mh, g = units[s]
-            nc.tensor.matmul_mx(
-                acc[:],
-                lhsT=w4w[:, b * NG + g, t, :].bitcast(FP4X4),
-                lhsT_scale=w4s[:, b * NG + g, t, :],
-                rhs=zq[b, mh][0].bitcast(FP8X4),
-                rhs_scale=zq[b, mh][1],
-                start=first,
-                stop=not first,
-            )
+        def w4_columns(b, g, t):
+            return w4w[:, b * NG + g, t, :].bitcast(FP4X4), w4s[:, b * NG + g, t, :]
 
-        def products(s):
-            q_accs[s] = [psum.tile([P, W], F32, name="q") for t in range(PACK)]
-            gate_accs = [psum.tile([P, W], F32, name="gate") for t in range(PACK)]
-            gate_work = [(gate_pass, gate_accs[t], t) for t in range(PACK)]
-            q_work = [(q_pass, q_accs[s][t], t) for t in range(PACK)]
-            if s == 0:
-                for one_pass, acc, t in gate_work[:EARLY_GATES] + q_work[:EARLY_QS]:
-                    one_pass(acc, s, t, 0, True)
-                for t in range(PACK):
-                    for (one_pass, acc, t), late in ((gate_work[t], t >= EARLY_GATES), (q_work[t], t >= EARLY_QS)):
-                        one_pass(acc, s, t, 1, late)
-                        if late:
-                            one_pass(acc, s, t, 0, False)
-            else:
-                for one_pass, acc, t in gate_work + q_work:
-                    for b in range(HB):
-                        one_pass(acc, s, t, b, b == 0)
-            rests[s] = sbuf([P, PACK, W], F32, ("aff01", "aff23")[s % 2])
-            for t in range(PACK):
-                nc.scalar.activation(rests[s][:, t, :], gate_accs[t][:], ACT.Sigmoid, scale=-1.0)
+        def products(k):
+            rests[k] = sbuf([P, PACK, C], F32, ("aff01", "aff23", "raw0")[k % 3])
+            for pair in range(2):
+                bank = psum.tile([P, 2, C], F32, name="gate", bufs=2)
+                fill_bank(bank, k, pair, w4_columns)
+                nc.scalar.activation(rests[k][:, 2 * pair : 2 * pair + 2, :], bank[:], ACT.Sigmoid, scale=-1.0)
+            q_banks[k] = [psum.tile([P, 2, C], F32, name="q", bufs=6) for pair in range(2)]
+            for pair in range(2):
+                fill_bank(q_banks[k][pair], k, pair, w2_columns)
 
-        def fall_of(s):
-            mh, g = units[s]
-            return falls[g, mh]
+        def fall_of(k):
+            mh, g, j = steps[k]
+            return falls[g, mh][:, :, j * C : (j + 1) * C]
 
         def flat(tile):
             return tile[:].rearrange("p t m -> p (t m)")
 
-        def times_q(s, t):
-            nc.vector.scalar_tensor_tensor(
-                difs[s][:, t, :], rests[s][:, t, :], 1.0, q_accs[s][t][:], ALU.subtract, ALU.mult
-            )
+        def difference(k):
+            share = GP_END_COLS if k in (0, last) else GP_COLS
+            cut = PACK * C - share
+            shift = max(share, cut)
+            room = sbuf([P, shift + PACK * C], F32, ("raw6", "raw1", "w1g")[k % 3])
+            pulls[k] = room[:, : PACK * C]
+            difs[k] = room[:, shift:]
+            for pair in range(2):
+                nc.vector.tensor_tensor(
+                    bank_view(difs[k], pair), fall_of(k)[:, 2 * pair : 2 * pair + 2, :], q_banks[k][pair][:], ALU.subtract
+                )
+            for engine, cols in ((nc.vector, slice(0, cut)), (nc.gpsimd, slice(cut, PACK * C))):
+                engine.tensor_tensor(pulls[k][:, cols], flat(rests[k])[:, cols], difs[k][:, cols], ALU.mult)
 
-        def times_fall(engine, s, c0, c1):
-            engine.tensor_tensor(
-                flat(kept[s])[:, c0:c1], flat(rests[s])[:, c0:c1], flat(fall_of(s))[:, c0:c1], ALU.mult
-            )
+        def bank_view(room, pair):
+            return room[:, pair * W : (pair + 1) * W].rearrange("p (e m) -> p e m", e=2)
 
-        def open_unit(s):
-            difs[s] = sbuf([P, PACK, W], F32, ("raw6", "raw1", "raw0", "raw1")[s])
-            kept[s] = sbuf([P, PACK, W], F32, unit_slots[s % 2])
+        def blend(k):
+            mh, g, j = steps[k]
+            for pair in range(2):
+                planes = slice(2 * pair, 2 * pair + 2)
+                nc.vector.tensor_tensor(
+                    fall_of(k)[:, planes, :], q_banks[k][pair][:], bank_view(pulls[k], pair), ALU.add
+                )
+            rows = out_0[g * W : (g + 1) * W, quarters[2 * mh + j]].rearrange("(p t) m -> p t m", t=PACK)
+            nc.sync.dma_start(rows, fall_of(k))
 
-        unit_slots = ("ga", "raw6")
-
-        def blend(s, cols):
-            mh, g = units[s]
-            y = fall_of(s)[:, :, cols]
-            nc.vector.tensor_tensor(y, kept[s][:, :, cols], difs[s][:, :, cols], ALU.subtract)
-            rows = out_0[g * W : (g + 1) * W, halves[mh]].rearrange("(p t) m -> p t m", t=PACK)
-            nc.sync.dma_start(rows[:, :, cols], y)
-            return y
-
-        def planes_out(s, cols, grouped, slot, queue):
-            mh, g = units[s]
-            out_cols = slice(mh * W + cols.start, mh * W + cols.stop)
-            codes = sbuf([P, cols.stop - cols.start], U32, slot)
+        def planes_out(g, out_cols, grouped, slot, queue):
+            codes = sbuf([P, out_cols.stop - out_cols.start], U32, slot)
             nc.vector.quantize_mx(codes[:].bitcast(FP8X4), y_s[:, g, out_cols], grouped)
             queue.dma_start(
                 out_1[g, :, out_cols, :].rearrange("p m t -> p (m t)").bitcast(I32), codes[:].bitcast(I32)
@@ -386,53 +379,38 @@ def tile_list_replacement_item_scores_kernel(
                     y_s[32 * q : 32 * q + 4, :, halves[mh]].bitcast(I32),
                 )
 
-        unit_cols = slice(0, W)
-        last = len(units) - 1
+        def regroup(k):
+            ygrouped[k] = sbuf([P, PACK * C], BF16, ("ga", "gb", "hw45")[k % 3])
+            cut = C if k < last else LAST_SCALAR_COLS
+            interleave(nc.scalar.copy, ygrouped[k][:, : PACK * cut], fall_of(k)[:, :, :cut])
+            if cut < C:
+                interleave(nc.vector.tensor_copy, ygrouped[k][:, PACK * cut :], fall_of(k)[:, :, cut:])
 
-        def unit_planes(s):
-            planes_out(s, unit_cols, ygrouped[s][:], "y_codes%d" % (s % 2), nc.sync)
-            if units[s][1] == NG - 1:
-                scales_out(units[s][0])
+        def step_planes(k):
+            mh, g, j = steps[k]
+            queue = nc.sync if k < last - 1 else nc.scalar
+            planes_out(g, quarters[2 * mh + j], ygrouped[k][:], "y_codes%d" % (k % 3), queue)
+            if g == NG - 1 and j == W // C - 1:
+                scales_out(mh)
 
+        z1late = {}
         products(0)
-        open_unit(0)
-        for t in range(PACK):
-            times_fall(nc.vector, 0, t * W, (t + 1) * W)
-            times_q(0, t)
-        products(1)
-        z1g = sbuf([P, G], BF16, "aff01")
-        interleave(nc.scalar.copy, z1g[:], zplanes(1, halves[1]))
-        for s in range(1, len(units)):
-            y = blend(s - 1, unit_cols)
-            open_unit(s)
-            ygrouped[s - 1] = sbuf([P, G], BF16, unit_slots[(s - 1) % 2])
-            interleave(nc.scalar.copy, ygrouped[s - 1][:], y)
-            share = GP_FIRST_COLS if s == 1 else GP_COLS
-            times_fall(nc.gpsimd, s, 0, share)
-            for t in range(PACK):
-                times_q(s, t)
-            if s == 1:
-                split(zq, quantise(z1g[:], W, "w1c1", "w1s1"), [(1, 1)])
-            if s < last:
-                products(s + 1)
-            times_fall(nc.vector, s, share, G)
-            if s < last:
-                unit_planes(s - 1)
-
-        pieces = [slice(0, W // 2), slice(W // 2, W)]
-        tail = []
-        for j, cols in enumerate(pieces):
-            if j == 0:
-                unit_planes(last - 1)
-            y = blend(last, cols)
-            width = cols.stop - cols.start
-            grouped = sbuf([P, PACK * width], BF16, ("w1g", "hw45")[j])
-            cut = width if j < len(pieces) - 1 else LAST_SCALAR_COLS
-            interleave(nc.scalar.copy, grouped[:, : PACK * cut], y[:, :, :cut])
-            tail.append((grouped, y, cut, width))
-        for j, cols in enumerate(pieces):
-            grouped, y, cut, width = tail[j]
-            if cut < width:
-                interleave(nc.vector.tensor_copy, grouped[:, PACK * cut :], y[:, :, cut:])
-            planes_out(last, cols, grouped[:], "y_tail%d" % j, nc.scalar)
-        scales_out(MH - 1)
+        for k in range(len(steps)):
+            if k < 2:
+                z1late[k] = sbuf([P, PACK * C], BF16, ("h12", "aff7")[k])
+                interleave(nc.scalar.copy, z1late[k][:], zplanes(1, quarters[2 + k]))
+            difference(k)
+            if k in (1, 2):
+                split(zq, quantise(z1late[k - 1][:], C, "w1c%d" % (2 * k - 1), "w1s%d" % (2 * k - 1)), [(1, 1 + k)], C)
+            if k >= PLANES_LAG:
+                step_planes(k - PLANES_LAG)
+            if k < last:
+                products(k + 1)
+            if k >= 1:
+                blend(k - 1)
+                regroup(k - 1)
+        step_planes(last - 2)
+        blend(last)
+        regroup(last)
+        step_planes(last - 1)
+        step_planes(last)

@@ -26,7 +26,7 @@ NG = N // W
 MH = T2 // W
 PLANES = HB * PACK
 C = 256
-GP_COLS = 752
+GP_COLS = 864
 GP_END_COLS = 320
 PLANES_LAG = 3
 TIE_COLS = 16
@@ -247,14 +247,13 @@ def tile_list_replacement_item_scores_kernel(
         h47 = sbuf([P, PACK, S], F32, "raw7")
         hs.extend([h47[:, i, :] for i in range(PACK)])
         silu(accs, 1)
-        warm = sbuf([P, 1], F32, "warm")
-        nc.scalar.activation(warm[:], hs[7][:, :1], ACT.Sigmoid)
         for b in range(HB):
             cast_weight(w2g[1][:, b * G : (b + 1) * G], raw2[b, 1])
 
         wg2 = wg.unsqueeze(1).to_broadcast([P, 2, S])
         hw45 = sbuf([P, 2, S], F32, "hw45")
-        nc.vector.tensor_tensor(hw45[:], h47[:, :2, :], wg2, ALU.mult)
+        for n in range(2):
+            nc.vector.tensor_tensor(hw45[:, n, :], h47[:, n, :], wg, ALU.mult)
         hw67 = h47[:, :2, :]
         nc.gpsimd.tensor_tensor(hw67, h47[:, 2:, :], wg2, ALU.mult)
         for n in range(2):
@@ -264,7 +263,6 @@ def tile_list_replacement_item_scores_kernel(
         for n in range(3, PLANES - 1):
             weigh(nc.gpsimd, n, whole)
         quarters = [slice(j * C, (j + 1) * C) for j in range(T2 // C)]
-        weigh(nc.vector, PLANES - 1, quarters[0])
 
         def zplanes(b, cols):
             return hz16[:, b * PACK * T2 : (b + 1) * PACK * T2].rearrange("p (t m) -> p t m", t=PACK)[:, :, cols]
@@ -278,9 +276,10 @@ def tile_list_replacement_item_scores_kernel(
         w2q = {}
         z0g = sbuf([P, PACK * T2], BF16, "tab_w0")
         interleave(nc.scalar.copy, z0g[:], zplanes(0, whole))
+        split(zq, quantise(z0g[:], T2, "raw7", "zs0"), [(0, j) for j in range(4)], C)
+        weigh(nc.vector, PLANES - 1, quarters[0])
         z1g = [sbuf([P, PACK * C], BF16, slot) for slot in ("h0", "gc")]
         interleave(nc.scalar.copy, z1g[0][:], zplanes(1, quarters[0]))
-        split(zq, quantise(z0g[:], T2, "raw7", "zs0"), [(0, j) for j in range(4)], C)
         weigh(nc.vector, PLANES - 1, quarters[1])
         interleave(nc.scalar.copy, z1g[1][:], zplanes(1, quarters[1]))
         split(zq, quantise(z1g[0][:], C, "w1c0", "w1s0"), [(1, 0)], C)

@@ -26,8 +26,9 @@ NG = N // W
 MH = T2 // W
 PLANES = HB * PACK
 C = 256
-GP_COLS = 864
-GP_END_COLS = 320
+GP_COLS = 928
+GP_FIRST_COLS = 320
+GP_LAST_COLS = 416
 PLANES_LAG = 3
 TIE_COLS = 16
 LAST_SCALAR_COLS = 80
@@ -337,7 +338,7 @@ def tile_list_replacement_item_scores_kernel(
             return tile[:].rearrange("p t m -> p (t m)")
 
         def difference(k):
-            share = GP_END_COLS if k in (0, last) else GP_COLS
+            share = {0: GP_FIRST_COLS, last: GP_LAST_COLS}.get(k, GP_COLS)
             cut = PACK * C - share
             shift = max(share, cut)
             room = sbuf([P, shift + PACK * C], F32, ("raw6", "raw1", "w1g")[k % 3])

@@ -251,16 +251,12 @@ def tile_list_replacement_item_scores_kernel(
         for b in range(HB):
             cast_weight(w2g[1][:, b * G : (b + 1) * G], raw2[b, 1])
 
-        wg2 = wg.unsqueeze(1).to_broadcast([P, 2, S])
-        hw45 = sbuf([P, 2, S], F32, "hw45")
-        for n in range(2):
-            nc.vector.tensor_tensor(hw45[:, n, :], h47[:, n, :], wg, ALU.mult)
-        hw67 = h47[:, :2, :]
-        nc.gpsimd.tensor_tensor(hw67, h47[:, 2:, :], wg2, ALU.mult)
-        for n in range(2):
-            scatter(4 + n, hw45[:, n, :])
-        for n in range(2):
-            scatter(6 + n, hw67[:, n, :])
+        hw4 = sbuf([P, S], F32, "hw45")
+        nc.vector.tensor_tensor(hw4[:], hs[4], wg, ALU.mult)
+        nc.gpsimd.tensor_tensor(hs[4], hs[5], wg, ALU.mult)
+        nc.gpsimd.tensor_tensor(h47[:, 2:, :], h47[:, 2:, :], wg.unsqueeze(1).to_broadcast([P, 2, S]), ALU.mult)
+        for n, hw in ((4, hw4[:]), (5, hs[4]), (6, hs[6]), (7, hs[7])):
+            scatter(n, hw)
         for n in range(3, PLANES - 1):
             weigh(nc.gpsimd, n, whole)
         quarters = [slice(j * C, (j + 1) * C) for j in range(T2 // C)]

@@ -32,6 +32,8 @@ GP_LAST_COLS = 416
 PLANES_LAG = 3
 TIE_COLS = 16
 LAST_SCALAR_COLS = 80
+EARLY = 128
+HEAD_SCALAR_PLACES = 48
 
 
 def tile_list_replacement_item_scores_kernel(
@@ -107,10 +109,8 @@ def tile_list_replacement_item_scores_kernel(
         load_table(0)
         load_table(1)
         raw1[2, 0] = load_rows(w1, 2 * W, 0, "raw2")
-        load_table(2)
-        w4w_raw = sbuf([P, HB, 2 * N], U8, "w4w_raw")
-        nc.sync.dma_start(w4w_raw[:].bitcast(I32), w4_words.rearrange("a p c -> p a c").bitcast(I32))
         nc.sync.dma_start(idx2[:], offs2)
+        load_table(2)
         hz = sbuf([P, PLANES * S], F32, "hz")
         wg = hz[:, 3 * S : 4 * S]
         nc.sync.dma_start(wg, wgs)
@@ -129,20 +129,25 @@ def tile_list_replacement_item_scores_kernel(
         raw1[0, 1] = load_rows(w1, 0, W, "raw3")
         load_aff(0, aff01[:, :T2])
         raw1[1, 1] = load_rows(w1, W, W, "raw4")
-        raw1[2, 1] = load_rows(w1, 2 * W, W, "raw5")
         load_aff(1, aff01[:, T2:])
+        raw1[2, 1] = load_rows(w1, 2 * W, W, "raw5")
+        load_aff(2, aff23[:, :T2])
         raw2[0, 0] = load_rows(w2, 0, 0, "raw6")
         raw2[1, 0] = load_rows(w2, W, 0, "raw7")
-        load_aff(2, aff23[:, :T2])
         load_aff(3, aff23[:, T2:])
+        w4w_raw = sbuf([P, HB, 2 * N], U8, "w4w_raw")
+        nc.sync.dma_start(w4w_raw[:].bitcast(I32), w4_words.rearrange("a p c -> p a c").bitcast(I32))
         load_aff(7, aff7[:])
 
         v_s = sbuf([P, S], U8, "v_s")
         v_w = [sbuf([P, S], U32, "v_w%d" % a) for a in range(KP)]
         w1q = {}
 
-        def gather_words(a):
-            nc.vector.tensor_copy(v_w[a][:], tab_w[a][:].indirect(idx[:]))
+        def entries(offsets, cols):
+            return offsets[:, cols.start // 16 : cols.stop // 16]
+
+        def gather_words(a, cols):
+            nc.vector.tensor_copy(v_w[a][:, cols], tab_w[a][:].indirect(entries(idx, cols)))
 
         def head_weight(a, slot, scalar_places):
             grouped = sbuf([P, G], BF16, slot)
@@ -153,28 +158,28 @@ def tile_list_replacement_item_scores_kernel(
             w1q[a, 0] = codes[:], scales[:]
 
         nc.vector.tensor_copy(v_s[:], tab_s[:].indirect(idx[:]))
+        listed = slice(0, S)
+        early = slice(0, EARLY)
+        later = slice(EARLY, S)
         head_weight(0, "ga", P)
         head_weight(1, "gb", P)
-        gather_words(0)
-        gather_words(1)
+        gather_words(0, listed)
+        gather_words(1, listed)
         w4s = sbuf([P, HB * NG, PACK, P], U8, "w4s")
         nc.vector.tensor_copy(w4s[:], w4s_raw[:].rearrange("p a (g m t) -> p (a g) t m", g=NG, t=PACK))
-        head_weight(2, "gc", P // 2)
-        gather_words(2)
-        w4w = sbuf([P, HB * NG, PACK, 2 * P], U8, "tab_w2")
-        nc.vector.tensor_copy(
-            w4w[:].bitcast(U16), w4w_raw[:].bitcast(U16).rearrange("p a (g m t) -> p (a g) t m", g=NG, t=PACK)
-        )
+        head_weight(2, "gc", HEAD_SCALAR_PLACES)
+        gather_words(2, early)
+        gather_words(2, later)
 
         raw2[0, 1] = load_rows(w2, 0, W, "raw0")
         aff45 = sbuf([P, 2 * T2], F32, "raw1")
         load_aff(4, aff45[:, :T2])
         load_aff(5, aff45[:, T2:])
         raw2[1, 1] = load_rows(w2, W, W, "tab_w0")
-        falls = {}
-        falls[0, 0] = load_rows(fall, 0, 0, "raw2")
         aff6 = sbuf([P, T2], F32, "tab_w1")
         load_aff(6, aff6[:])
+        falls = {}
+        falls[0, 0] = load_rows(fall, 0, 0, "raw2")
 
         hz16 = hz[:].bitcast(BF16)
         zplane = [hz16[:, n * T2 : (n + 1) * T2] for n in range(PLANES)]
@@ -182,22 +187,25 @@ def tile_list_replacement_item_scores_kernel(
         h12 = sbuf([P, 2, S], F32, "h12")
         hs = [h0[:], h12[:, 0, :], h12[:, 1, :], hz[:, 2 * S : 3 * S]]
 
+        def first_pass(out, a, b, i, moving, start, stop):
+            codes, scales = w1q[a, b]
+            cols = slice(i * P, (i + 1) * P)
+            nc.tensor.matmul_mx(
+                out,
+                lhsT=codes[:, cols].bitcast(FP8X4),
+                lhsT_scale=scales[:, cols],
+                rhs=v_w[a][:, moving].bitcast(FP8X4),
+                rhs_scale=v_s[4 * a :, moving],
+                start=start,
+                stop=stop,
+            )
+
         def first_passes(accs, b, passes):
             for a, i in passes:
-                codes, scales = w1q[a, b]
-                cols = slice(i * P, (i + 1) * P)
-                nc.tensor.matmul_mx(
-                    accs[i][:],
-                    lhsT=codes[:, cols].bitcast(FP8X4),
-                    lhsT_scale=scales[:, cols],
-                    rhs=v_w[a][:].bitcast(FP8X4),
-                    rhs_scale=v_s[4 * a :, :],
-                    start=(a == 0),
-                    stop=(a == KP - 1),
-                )
+                first_pass(accs[i][:], a, b, i, listed, a == 0, a == KP - 1)
 
-        def silu(accs, b):
-            for i in range(PACK):
+        def silu(accs, b, planes):
+            for i in planes:
                 nc.scalar.activation(hs[b * PACK + i], accs[i][:], ACT.Silu)
 
         def scatter(n, hw):
@@ -209,9 +217,16 @@ def tile_list_replacement_item_scores_kernel(
         whole = slice(0, T2)
         halves = [slice(mh * W, (mh + 1) * W) for mh in range(MH)]
 
+        acc_early = psum.tile([P, S], F32, name="q", bufs=6)
         accs = [psum.tile([P, S], F32, name="q", bufs=6) for i in range(PACK)]
-        first_passes(accs, 0, [(a, i) for a in range(KP) for i in range(PACK)])
-        silu(accs, 0)
+        for a in range(KP):
+            first_pass(acc_early[:, early], a, 0, 0, early, a == 0, a == KP - 1)
+            first_pass(accs[0][:, EARLY:C], a, 0, 0, slice(EARLY, C), a == 0, False)
+            first_pass(accs[0][:, C:], a, 0, 0, slice(C, S), False, a == KP - 1)
+            first_passes(accs, 0, [(a, i) for i in range(1, PACK)])
+        nc.scalar.activation(hs[0][:, early], acc_early[:, early], ACT.Silu)
+        nc.scalar.activation(hs[0][:, later], accs[0][:, later], ACT.Silu)
+        silu(accs, 0, range(1, PACK))
         w1g = sbuf([P, KP * G + 2 * (S - TIE_COLS)], BF16, "w1g")
         for a in range(KP):
             cast_weight(w1g[:, a * G : (a + 1) * G], raw1[a, 1])
@@ -220,12 +235,14 @@ def tile_list_replacement_item_scores_kernel(
         falls[1, 1] = load_rows(fall, W, W, "raw5")
         w1g32 = w1g[:].bitcast(F32)
 
-        nc.vector.tensor_tensor(hs[0], hs[0], wg, ALU.mult)
+        nc.vector.tensor_tensor(page_of[0][:].indirect(entries(idx2, early)), hs[0][:, early], wg[:, early], ALU.mult)
+        nc.vector.tensor_tensor(hs[0][:, later], hs[0][:, later], wg[:, later], ALU.mult)
         for n in (1, 2):
             nc.gpsimd.tensor_tensor(hs[n], hs[n], wg, ALU.mult)
         hw3 = w1g32[:, KP * G // 2 - TIE_COLS :]
         nc.gpsimd.tensor_tensor(hw3[:, TIE_COLS:], hs[3][:, TIE_COLS:], wg[:, TIE_COLS:], ALU.mult)
-        for n in range(3):
+        nc.vector.tensor_copy(page_of[0][:].indirect(entries(idx2, later)), hs[0][:, later])
+        for n in (1, 2):
             scatter(n, hs[n])
         for n in range(2):
             weigh(nc.gpsimd, n, whole)
@@ -242,17 +259,22 @@ def tile_list_replacement_item_scores_kernel(
         nc.vector.tensor_tensor(hw3[:, :TIE_COLS], hs[3][:, :TIE_COLS], wg[:, :TIE_COLS], ALU.mult)
         scatter(3, hw3)
         weigh(nc.gpsimd, 2, whole)
-        w2g = [sbuf([P, HB * G], BF16, slot) for slot in ("ga", "gb")]
-        for b in range(HB):
-            cast_weight(w2g[0][:, b * G : (b + 1) * G], raw2[b, 0])
-        h47 = sbuf([P, PACK, S], F32, "raw7")
+        w2g0 = [sbuf([P, G], BF16, slot) for slot in ("ga", "w1c3")]
+        w2g1 = sbuf([P, HB * G], BF16, "gb")
+        cast_weight(w2g0[0][:], raw2[0, 0])
+        h47 = sbuf([P, PACK, S], F32, "raw6")
         hs.extend([h47[:, i, :] for i in range(PACK)])
-        silu(accs, 1)
+        silu(accs, 1, range(PACK))
+        cast_weight(w2g0[1][:], raw2[1, 0])
+        w4w = sbuf([P, HB * NG, PACK, 2 * P], U8, "w1s3")
+        nc.scalar.copy(
+            w4w[:].bitcast(U16), w4w_raw[:].bitcast(U16).rearrange("p a (g m t) -> p (a g) t m", g=NG, t=PACK)
+        )
         for b in range(HB):
-            cast_weight(w2g[1][:, b * G : (b + 1) * G], raw2[b, 1])
+            cast_weight(w2g1[:, b * G : (b + 1) * G], raw2[b, 1])
 
         hw4 = sbuf([P, S], F32, "hw45")
-        nc.vector.tensor_tensor(hw4[:], hs[4], wg, ALU.mult)
+        nc.gpsimd.tensor_tensor(hw4[:], hs[4], wg, ALU.mult)
         nc.gpsimd.tensor_tensor(hs[4], hs[5], wg, ALU.mult)
         nc.gpsimd.tensor_tensor(h47[:, 2:, :], h47[:, 2:, :], wg.unsqueeze(1).to_broadcast([P, 2, S]), ALU.mult)
         for n, hw in ((4, hw4[:]), (5, hs[4]), (6, hs[6]), (7, hs[7])):
@@ -273,17 +295,21 @@ def tile_list_replacement_item_scores_kernel(
         w2q = {}
         z0g = sbuf([P, PACK * T2], BF16, "tab_w0")
         interleave(nc.scalar.copy, z0g[:], zplanes(0, whole))
-        split(zq, quantise(z0g[:], T2, "raw7", "zs0"), [(0, j) for j in range(4)], C)
+        split(zq, quantise(z0g[:], T2, "raw6", "zs0"), [(0, j) for j in range(4)], C)
         weigh(nc.vector, PLANES - 1, quarters[0])
         z1g = [sbuf([P, PACK * C], BF16, slot) for slot in ("h0", "gc")]
         interleave(nc.scalar.copy, z1g[0][:], zplanes(1, quarters[0]))
         weigh(nc.vector, PLANES - 1, quarters[1])
         interleave(nc.scalar.copy, z1g[1][:], zplanes(1, quarters[1]))
         split(zq, quantise(z1g[0][:], C, "w1c0", "w1s0"), [(1, 0)], C)
-        split(w2q, quantise(w2g[0][:], HB * W, "tab_w0", "w2s0"), [(0, 0), (1, 0)], W)
+        codes = sbuf([P, HB * W], U32, "tab_w0")
+        scales = sbuf([P, HB * W], U8, "w2s0")
+        split(w2q, (codes, scales), [(0, 0), (1, 0)], W)
+        for b in range(HB):
+            nc.vector.quantize_mx(w2q[b, 0][0].bitcast(FP8X4), w2q[b, 0][1], w2g0[b][:])
         weigh(nc.vector, PLANES - 1, halves[1])
         split(zq, quantise(z1g[1][:], C, "w1c2", "w1s2"), [(1, 1)], C)
-        split(w2q, quantise(w2g[1][:], HB * W, "gc", "w2s1"), [(0, 1), (1, 1)], W)
+        split(w2q, quantise(w2g1[:], HB * W, "gc", "w2s1"), [(0, 1), (1, 1)], W)
 
         y_s = sbuf([P, NG, T2], U8, "y_s")
         steps = [(mh, g, j) for mh in range(MH) for g in range(NG) for j in range(W // C)]
@@ -337,7 +363,7 @@ def tile_list_replacement_item_scores_kernel(
             share = {0: GP_FIRST_COLS, last: GP_LAST_COLS}.get(k, GP_COLS)
             cut = PACK * C - share
             shift = max(share, cut)
-            room = sbuf([P, shift + PACK * C], F32, ("raw6", "raw1", "w1g")[k % 3])
+            room = sbuf([P, shift + PACK * C], F32, ("raw7", "raw1", "w1g")[k % 3])
             pulls[k] = room[:, : PACK * C]
             difs[k] = room[:, shift:]
             for pair in range(2):
@@ -397,7 +423,7 @@ def tile_list_replacement_item_scores_kernel(
                 interleave(nc.scalar.copy, z1late[k][:], zplanes(1, quarters[2 + k]))
             difference(k)
             if k in (1, 2):
-                split(zq, quantise(z1late[k - 1][:], C, "w1c%d" % (2 * k - 1), "w1s%d" % (2 * k - 1)), [(1, 1 + k)], C)
+                split(zq, quantise(z1late[k - 1][:], C, "w1c%d" % (2 * k - 1), "zs%d" % k), [(1, 1 + k)], C)
             if k >= PLANES_LAG:
                 step_planes(k - PLANES_LAG)
             if k < last:

@@ -101,10 +101,10 @@ def tile_list_replacement_item_scores_kernel(
         raw1 = {}
         raw1[0, 0] = load_rows(w1, 0, 0, "raw0", 4)
         raw1[1, 0] = load_rows(w1, W, 0, "raw1", 2)
-        for q in range(4):
+        for r in range(4):
             nc.sync.dma_start(
-                w4s_raw[32 * q : 32 * q + 4, :, :].bitcast(I32),
-                w4_scales[:, 4 * q : 4 * q + 4, :].rearrange("a r n -> r a n").bitcast(I32),
+                w4s_raw[r:P:32, :, :].bitcast(I32),
+                w4_scales[:, r:16:4, :].rearrange("a q n -> q a n").bitcast(I32),
             )
         load_table(0)
         load_table(1)
@@ -394,11 +394,11 @@ def tile_list_replacement_item_scores_kernel(
             )
 
         def scales_out(mh):
-            for q in range(4):
-                eng = nc.sync if q % 2 == 0 else nc.scalar
+            for r in range(4):
+                eng = nc.sync if r % 2 == 0 else nc.scalar
                 eng.dma_start(
-                    out_2[:, 4 * q : 4 * q + 4, halves[mh]].rearrange("g r m -> r g m").bitcast(I32),
-                    y_s[32 * q : 32 * q + 4, :, halves[mh]].bitcast(I32),
+                    out_2[:, r:16:4, halves[mh]].rearrange("g q m -> q g m").bitcast(I32),
+                    y_s[r:P:32, :, halves[mh]].bitcast(I32),
                 )
 
         def regroup(k):

@@ -27,7 +27,7 @@ MH = T2 // W
 PLANES = HB * PACK
 C = 256
 GP_COLS = 928
-GP_FIRST_COLS = 320
+GP_FIRST_COLS = 384
 GP_LAST_COLS = 416
 PLANES_LAG = 3
 TIE_COLS = 16
@@ -111,8 +111,13 @@ def tile_list_replacement_item_scores_kernel(
         raw1[2, 0] = load_rows(w1, 2 * W, 0, "raw2")
         nc.sync.dma_start(idx2[:], offs2)
         load_table(2)
-        hz = sbuf([P, PLANES * S], F32, "hz")
-        wg = hz[:, 3 * S : 4 * S]
+        w1_at = T2
+        hw3_at = w1_at + KP * G // 2 - TIE_COLS
+        pair_step = hw3_at - T2
+        wg_at = hw3_at + S
+        work = sbuf([P, max(2 * pair_step, wg_at + 3 * S)], F32, "work")
+        work16 = work[:].bitcast(BF16)
+        wg = work[:, wg_at : wg_at + S]
         nc.sync.dma_start(wg, wgs)
 
         affs = {}
@@ -131,13 +136,12 @@ def tile_list_replacement_item_scores_kernel(
         raw1[1, 1] = load_rows(w1, W, W, "raw4")
         load_aff(1, aff01[:, T2:])
         raw1[2, 1] = load_rows(w1, 2 * W, W, "raw5")
+        w4w_raw = sbuf([P, HB, 2 * N], U8, "w4w_raw")
+        nc.sync.dma_start(w4w_raw[:].bitcast(I32), w4_words.rearrange("a p c -> p a c").bitcast(I32))
         load_aff(2, aff23[:, :T2])
         raw2[0, 0] = load_rows(w2, 0, 0, "raw6")
         raw2[1, 0] = load_rows(w2, W, 0, "raw7")
         load_aff(3, aff23[:, T2:])
-        w4w_raw = sbuf([P, HB, 2 * N], U8, "w4w_raw")
-        nc.sync.dma_start(w4w_raw[:].bitcast(I32), w4_words.rearrange("a p c -> p a c").bitcast(I32))
-        load_aff(7, aff7[:])
 
         v_s = sbuf([P, S], U8, "v_s")
         v_w = [sbuf([P, S], U32, "v_w%d" % a) for a in range(KP)]
@@ -155,7 +159,8 @@ def tile_list_replacement_item_scores_kernel(
             if scalar_places < P:
                 cast_part(nc.vector.tensor_copy, grouped[:], raw1[a, 0], scalar_places, P)
             codes, scales = quantise(grouped[:], W, "w1c%d" % a, "w1s%d" % a)
-            w1q[a, 0] = codes[:], scales[:]
+            for i in range(PACK):
+                w1q[a, i] = codes[:, i * P : (i + 1) * P], scales[:, i * P : (i + 1) * P]
 
         nc.vector.tensor_copy(v_s[:], tab_s[:].indirect(idx[:]))
         listed = slice(0, S)
@@ -174,72 +179,83 @@ def tile_list_replacement_item_scores_kernel(
         raw2[0, 1] = load_rows(w2, 0, W, "raw0")
         aff45 = sbuf([P, 2 * T2], F32, "raw1")
         load_aff(4, aff45[:, :T2])
-        load_aff(5, aff45[:, T2:])
         raw2[1, 1] = load_rows(w2, W, W, "tab_w0")
+        load_aff(5, aff45[:, T2:])
         aff6 = sbuf([P, T2], F32, "tab_w1")
         load_aff(6, aff6[:])
+        load_aff(7, aff7[:])
         falls = {}
         falls[0, 0] = load_rows(fall, 0, 0, "raw2")
 
-        hz16 = hz[:].bitcast(BF16)
-        zplane = [hz16[:, n * T2 : (n + 1) * T2] for n in range(PLANES)]
         h0 = sbuf([P, S], F32, "h0")
-        h12 = sbuf([P, 2, S], F32, "h12")
-        hs = [h0[:], h12[:, 0, :], h12[:, 1, :], hz[:, 2 * S : 3 * S]]
+        h3 = sbuf([P, S], F32, "h3")
+        hs = [h0[:], work[:, wg_at + S : wg_at + 2 * S], work[:, wg_at + 2 * S : wg_at + 3 * S], h3[:]]
 
-        def first_pass(out, a, b, i, moving, start, stop):
-            codes, scales = w1q[a, b]
-            cols = slice(i * P, (i + 1) * P)
+        def first_pass(out, a, n, moving, start, stop):
+            codes, scales = w1q[a, n]
             nc.tensor.matmul_mx(
                 out,
-                lhsT=codes[:, cols].bitcast(FP8X4),
-                lhsT_scale=scales[:, cols],
+                lhsT=codes.bitcast(FP8X4),
+                lhsT_scale=scales,
                 rhs=v_w[a][:, moving].bitcast(FP8X4),
                 rhs_scale=v_s[4 * a :, moving],
                 start=start,
                 stop=stop,
             )
 
-        def first_passes(accs, b, passes):
-            for a, i in passes:
-                first_pass(accs[i][:], a, b, i, listed, a == 0, a == KP - 1)
-
-        def silu(accs, b, planes):
-            for i in planes:
-                nc.scalar.activation(hs[b * PACK + i], accs[i][:], ACT.Silu)
-
         def scatter(n, hw):
             nc.vector.tensor_copy(page_of[n][:].indirect(idx2[:]), hw)
+
+        zplane = {}
+        for n in range(PACK):
+            at = 2 * pair_step * (n // 2)
+            zplane[n] = work16[:, at : at + 2 * T2].rearrange("p (m e) -> p m e", e=2)[:, :, n % 2]
 
         def weigh(engine, n, cols):
             engine.tensor_tensor(zplane[n][:, cols], page_of[n][:, cols], affs[n][:, cols], ALU.mult)
 
         whole = slice(0, T2)
         halves = [slice(mh * W, (mh + 1) * W) for mh in range(MH)]
+        quarters = [slice(j * C, (j + 1) * C) for j in range(T2 // C)]
 
         acc_early = psum.tile([P, S], F32, name="q", bufs=6)
         accs = [psum.tile([P, S], F32, name="q", bufs=6) for i in range(PACK)]
         for a in range(KP):
-            first_pass(acc_early[:, early], a, 0, 0, early, a == 0, a == KP - 1)
-            first_pass(accs[0][:, EARLY:C], a, 0, 0, slice(EARLY, C), a == 0, False)
-            first_pass(accs[0][:, C:], a, 0, 0, slice(C, S), False, a == KP - 1)
-            first_passes(accs, 0, [(a, i) for i in range(1, PACK)])
+            first_pass(acc_early[:, early], a, 0, early, a == 0, a == KP - 1)
+            first_pass(accs[0][:, EARLY:C], a, 0, slice(EARLY, C), a == 0, False)
+            first_pass(accs[0][:, C:], a, 0, slice(C, S), False, a == KP - 1)
+            for i in range(1, PACK):
+                first_pass(accs[i][:], a, i, listed, a == 0, a == KP - 1)
         nc.scalar.activation(hs[0][:, early], acc_early[:, early], ACT.Silu)
         nc.scalar.activation(hs[0][:, later], accs[0][:, later], ACT.Silu)
-        silu(accs, 0, range(1, PACK))
-        w1g = sbuf([P, KP * G + 2 * (S - TIE_COLS)], BF16, "w1g")
-        for a in range(KP):
-            cast_weight(w1g[:, a * G : (a + 1) * G], raw1[a, 1])
+        for i in range(1, PACK):
+            nc.scalar.activation(hs[i], accs[i][:], ACT.Silu)
+
+        w1g = work16[:, 2 * w1_at : 2 * w1_at + KP * G]
+
+        def cast_planes(a, t0, t1):
+            nc.scalar.copy(
+                w1g.rearrange("p (t a m j) -> p a m j t", t=PACK, a=KP, j=PACK)[:, a, :, :, t0:t1],
+                raw1[a, 1][:].rearrange("p j (m t) -> p m j t", t=PACK)[:, :, :, t0:t1],
+            )
+
+        for a in range(KP - 1):
+            cast_planes(a, 0, PACK)
+        cast_planes(KP - 1, 0, 2)
+        cast_planes(KP - 1, 2, PACK)
         falls[1, 0] = load_rows(fall, W, 0, "raw3")
         falls[0, 1] = load_rows(fall, 0, W, "raw4")
         falls[1, 1] = load_rows(fall, W, W, "raw5")
-        w1g32 = w1g[:].bitcast(F32)
+        w4w = sbuf([P, HB * NG, PACK, 2 * P], U8, "w4w")
+        nc.scalar.copy(
+            w4w[:].bitcast(U16), w4w_raw[:].bitcast(U16).rearrange("p a (g m t) -> p (a g) t m", g=NG, t=PACK)
+        )
 
         nc.vector.tensor_tensor(page_of[0][:].indirect(entries(idx2, early)), hs[0][:, early], wg[:, early], ALU.mult)
         nc.vector.tensor_tensor(hs[0][:, later], hs[0][:, later], wg[:, later], ALU.mult)
         for n in (1, 2):
             nc.gpsimd.tensor_tensor(hs[n], hs[n], wg, ALU.mult)
-        hw3 = w1g32[:, KP * G // 2 - TIE_COLS :]
+        hw3 = work[:, hw3_at : hw3_at + S]
         nc.gpsimd.tensor_tensor(hw3[:, TIE_COLS:], hs[3][:, TIE_COLS:], wg[:, TIE_COLS:], ALU.mult)
         nc.vector.tensor_copy(page_of[0][:].indirect(entries(idx2, later)), hs[0][:, later])
         for n in (1, 2):
@@ -249,42 +265,51 @@ def tile_list_replacement_item_scores_kernel(
 
         accs = [psum.tile([P, S], F32, name="q", bufs=6) for i in range(2)]
         accs = accs + [psum.tile([P, S], F32, name="gate", bufs=2) for i in range(2)]
-        codes, scales = quantise(w1g[:, :G], W, "h12", "w1s5")
-        w1q[0, 1] = codes[:], scales[:]
-        first_passes(accs, 1, [(0, i) for i in range(PACK)])
-        codes, scales = quantise(w1g[:, G : KP * G], 2 * W, "w1c3", "w1s3")
-        for a in range(1, KP):
-            w1q[a, 1] = codes[:, (a - 1) * W : a * W], scales[:, (a - 1) * W : a * W]
-        first_passes(accs, 1, [(a, i) for i in range(PACK) for a in range(1, KP)])
+        h47 = sbuf([P, PACK, S], F32, "tab_w2")
+        hs.extend([h47[:, i, :] for i in range(PACK)])
+        codes = sbuf([P, PACK, KP * P], U32, "w1c3")
+        scales = sbuf([P, PACK * KP * P], U8, "w1s3")
+        for i in range(PACK):
+            plane_scales = scales[:, i * KP * P : (i + 1) * KP * P]
+            nc.vector.quantize_mx(codes[:, i, :].bitcast(FP8X4), plane_scales, w1g[:, i * KP * W : (i + 1) * KP * W])
+            for a in range(KP):
+                w1q[a, PACK + i] = codes[:, i, a * P : (a + 1) * P], plane_scales[:, a * P : (a + 1) * P]
+                first_pass(accs[i][:], a, PACK + i, listed, a == 0, a == KP - 1)
+            nc.scalar.activation(hs[PACK + i], accs[i][:], ACT.Silu)
         nc.vector.tensor_tensor(hw3[:, :TIE_COLS], hs[3][:, :TIE_COLS], wg[:, :TIE_COLS], ALU.mult)
         scatter(3, hw3)
-        weigh(nc.gpsimd, 2, whole)
-        w2g0 = [sbuf([P, G], BF16, slot) for slot in ("ga", "w1c3")]
-        w2g1 = sbuf([P, HB * G], BF16, "gb")
-        cast_weight(w2g0[0][:], raw2[0, 0])
-        h47 = sbuf([P, PACK, S], F32, "raw6")
-        hs.extend([h47[:, i, :] for i in range(PACK)])
-        silu(accs, 1, range(PACK))
-        cast_weight(w2g0[1][:], raw2[1, 0])
-        w4w = sbuf([P, HB * NG, PACK, 2 * P], U8, "w1s3")
-        nc.scalar.copy(
-            w4w[:].bitcast(U16), w4w_raw[:].bitcast(U16).rearrange("p a (g m t) -> p (a g) t m", g=NG, t=PACK)
-        )
-        for b in range(HB):
-            cast_weight(w2g1[:, b * G : (b + 1) * G], raw2[b, 1])
-
-        hw4 = sbuf([P, S], F32, "hw45")
-        nc.gpsimd.tensor_tensor(hw4[:], hs[4], wg, ALU.mult)
-        nc.gpsimd.tensor_tensor(hs[4], hs[5], wg, ALU.mult)
+        weigh(nc.gpsimd, 2, halves[0])
+        nc.gpsimd.tensor_tensor(hs[4], hs[4], wg, ALU.mult)
+        weigh(nc.gpsimd, 2, halves[1])
+        nc.gpsimd.tensor_tensor(hs[5], hs[5], wg, ALU.mult)
         nc.gpsimd.tensor_tensor(h47[:, 2:, :], h47[:, 2:, :], wg.unsqueeze(1).to_broadcast([P, 2, S]), ALU.mult)
-        for n, hw in ((4, hw4[:]), (5, hs[4]), (6, hs[6]), (7, hs[7])):
-            scatter(n, hw)
+        for n in range(PACK, PLANES):
+            scatter(n, hs[n])
+
+        w2_at = PACK * T2 - W
+        w2g00 = sbuf([P, G], BF16, "ga")
+        cast_weight(w2g00[:], raw2[0, 0])
+        late = sbuf([P, w2_at + G], BF16, "raw6")
+        w2g0 = [w2g00[:], late[:, w2_at:]]
+        cast_weight(w2g0[1], raw2[1, 0])
+        w2g1 = sbuf([P, HB * G], BF16, "gb")
+        cast_weight(w2g1[:, :G], raw2[0, 1])
+        for n in range(PACK, PLANES):
+            zplane[n] = late[:, (n - PACK) * T2 : (n - PACK + 1) * T2]
         for n in range(3, PLANES - 1):
             weigh(nc.gpsimd, n, whole)
-        quarters = [slice(j * C, (j + 1) * C) for j in range(T2 // C)]
 
-        def zplanes(b, cols):
-            return hz16[:, b * PACK * T2 : (b + 1) * PACK * T2].rearrange("p (t m) -> p t m", t=PACK)[:, :, cols]
+        pairs = work[:, : 2 * pair_step].bitcast(U32).rearrange("p (u x) -> p u x", u=2)
+        z0g = [sbuf([P, G], BF16, slot)[:] for slot in ("z0a", "gc")]
+        for mh in range(MH):
+            nc.scalar.copy(
+                z0g[mh].bitcast(U32).rearrange("p (c i u) -> p c u i", i=PACK, u=2),
+                pairs[:, :, halves[mh]].rearrange("p u (c i) -> p c u i", i=PACK),
+            )
+        cast_weight(w2g1[:, G:], raw2[1, 1])
+
+        def z1planes(cols):
+            return late[:, : PACK * T2].rearrange("p (t m) -> p t m", t=PACK)[:, :, cols]
 
         def split(store, pair, keys, width):
             codes, scales = pair
@@ -293,23 +318,21 @@ def tile_list_replacement_item_scores_kernel(
 
         zq = {}
         w2q = {}
-        z0g = sbuf([P, PACK * T2], BF16, "tab_w0")
-        interleave(nc.scalar.copy, z0g[:], zplanes(0, whole))
-        split(zq, quantise(z0g[:], T2, "raw6", "zs0"), [(0, j) for j in range(4)], C)
-        weigh(nc.vector, PLANES - 1, quarters[0])
-        z1g = [sbuf([P, PACK * C], BF16, slot) for slot in ("h0", "gc")]
-        interleave(nc.scalar.copy, z1g[0][:], zplanes(1, quarters[0]))
-        weigh(nc.vector, PLANES - 1, quarters[1])
-        interleave(nc.scalar.copy, z1g[1][:], zplanes(1, quarters[1]))
-        split(zq, quantise(z1g[0][:], C, "w1c0", "w1s0"), [(1, 0)], C)
-        codes = sbuf([P, HB * W], U32, "tab_w0")
+        split(zq, quantise(z0g[0], W, "tab_w1", "w1s0"), [(0, 0), (0, 1)], C)
+        weigh(nc.vector, PLANES - 1, halves[0])
+        z1g = [sbuf([P, PACK * C], BF16, slot) for slot in ("h0", "w4w_raw")]
+        for j in range(2):
+            interleave(nc.scalar.copy, z1g[j][:], z1planes(quarters[j]))
+        split(zq, quantise(z0g[1], W, "w1c1", "w1s1"), [(0, 2), (0, 3)], C)
+        codes = sbuf([P, HB * W], U32, "z0a")
         scales = sbuf([P, HB * W], U8, "w2s0")
         split(w2q, (codes, scales), [(0, 0), (1, 0)], W)
-        for b in range(HB):
-            nc.vector.quantize_mx(w2q[b, 0][0].bitcast(FP8X4), w2q[b, 0][1], w2g0[b][:])
+        nc.vector.quantize_mx(w2q[0, 0][0].bitcast(FP8X4), w2q[0, 0][1], w2g0[0])
+        split(zq, quantise(z1g[0][:], C, "w1c2", "w1s2"), [(1, 0)], C)
+        nc.vector.quantize_mx(w2q[1, 0][0].bitcast(FP8X4), w2q[1, 0][1], w2g0[1])
+        split(zq, quantise(z1g[1][:], C, "v_w0", "zs0"), [(1, 1)], C)
         weigh(nc.vector, PLANES - 1, halves[1])
-        split(zq, quantise(z1g[1][:], C, "w1c2", "w1s2"), [(1, 1)], C)
-        split(w2q, quantise(w2g1[:], HB * W, "gc", "w2s1"), [(0, 1), (1, 1)], W)
+        split(w2q, quantise(w2g1[:], HB * W, "h0", "w2s1"), [(0, 1), (1, 1)], W)
 
         y_s = sbuf([P, NG, T2], U8, "y_s")
         steps = [(mh, g, j) for mh in range(MH) for g in range(NG) for j in range(W // C)]
@@ -317,23 +340,24 @@ def tile_list_replacement_item_scores_kernel(
         rests = {}
         difs = {}
         pulls = {}
+        parts = {}
         q_banks = {}
+        gate_banks = {}
         ygrouped = {}
 
-        def fill_bank(bank, k, pair, stationary):
+        def passes(banks, k, b, stationary, planes=range(PACK)):
             mh, g, j = steps[k]
-            for b in range(HB):
-                for e in range(2):
-                    words, scales = stationary(b, g, 2 * pair + e)
-                    nc.tensor.matmul_mx(
-                        bank[:, e, :],
-                        lhsT=words,
-                        lhsT_scale=scales,
-                        rhs=zq[b, 2 * mh + j][0].bitcast(FP8X4),
-                        rhs_scale=zq[b, 2 * mh + j][1],
-                        start=(b == 0 and e == 0),
-                        stop=(b == HB - 1 and e == 1),
-                    )
+            for t in planes:
+                words, scales = stationary(b, g, t)
+                nc.tensor.matmul_mx(
+                    banks[t // 2][:, t % 2, :],
+                    lhsT=words,
+                    lhsT_scale=scales,
+                    rhs=zq[b, 2 * mh + j][0].bitcast(FP8X4),
+                    rhs_scale=zq[b, 2 * mh + j][1],
+                    start=(b == 0 and t % 2 == 0),
+                    stop=(b == HB - 1 and t % 2 == 1),
+                )
 
         def w2_columns(b, g, t):
             cols = slice(t * P, (t + 1) * P)
@@ -342,15 +366,39 @@ def tile_list_replacement_item_scores_kernel(
         def w4_columns(b, g, t):
             return w4w[:, b * NG + g, t, :].bitcast(FP4X4), w4s[:, b * NG + g, t, :]
 
-        def products(k):
+        def gate_passes(k, b):
+            if b == 0:
+                gate_banks[k] = [psum.tile([P, 2, C], F32, name="gate", bufs=2) for pair in range(2)]
+            passes(gate_banks[k], k, b, w4_columns)
+            if b == HB - 1:
+                rests[k] = sbuf([P, PACK, C], F32, ("aff01", "aff23", "raw0")[k % 3])
+                for pair in range(2):
+                    nc.scalar.activation(
+                        rests[k][:, 2 * pair : 2 * pair + 2, :], gate_banks[k][pair][:], ACT.Sigmoid, scale=-1.0
+                    )
+
+        def q_passes(k, b):
+            if b == 0:
+                q_banks[k] = [psum.tile([P, 2, C], F32, name="q", bufs=6) for pair in range(2)]
+            passes(q_banks[k], k, b, w2_columns)
+
+        def gates(k):
             rests[k] = sbuf([P, PACK, C], F32, ("aff01", "aff23", "raw0")[k % 3])
+            gate_banks[k] = []
             for pair in range(2):
-                bank = psum.tile([P, 2, C], F32, name="gate", bufs=2)
-                fill_bank(bank, k, pair, w4_columns)
-                nc.scalar.activation(rests[k][:, 2 * pair : 2 * pair + 2, :], bank[:], ACT.Sigmoid, scale=-1.0)
+                gate_banks[k].append(psum.tile([P, 2, C], F32, name="gate", bufs=2))
+                for b in range(HB):
+                    passes(gate_banks[k], k, b, w4_columns, (2 * pair, 2 * pair + 1))
+                nc.scalar.activation(
+                    rests[k][:, 2 * pair : 2 * pair + 2, :], gate_banks[k][pair][:], ACT.Sigmoid, scale=-1.0
+                )
+
+        def products(k):
+            gates(k)
             q_banks[k] = [psum.tile([P, 2, C], F32, name="q", bufs=6) for pair in range(2)]
             for pair in range(2):
-                fill_bank(q_banks[k][pair], k, pair, w2_columns)
+                for b in range(HB):
+                    passes(q_banks[k], k, b, w2_columns, (2 * pair, 2 * pair + 1))
 
         def fall_of(k):
             mh, g, j = steps[k]
@@ -362,16 +410,19 @@ def tile_list_replacement_item_scores_kernel(
         def difference(k):
             share = {0: GP_FIRST_COLS, last: GP_LAST_COLS}.get(k, GP_COLS)
             cut = PACK * C - share
-            shift = max(share, cut)
-            room = sbuf([P, shift + PACK * C], F32, ("raw7", "raw1", "w1g")[k % 3])
+            shift = max(share, cut) if k > 0 else PACK * C
+            room = sbuf([P, shift + PACK * C], F32, ("raw7", "raw1", "work")[k % 3])
             pulls[k] = room[:, : PACK * C]
             difs[k] = room[:, shift:]
             for pair in range(2):
                 nc.vector.tensor_tensor(
                     bank_view(difs[k], pair), fall_of(k)[:, 2 * pair : 2 * pair + 2, :], q_banks[k][pair][:], ALU.subtract
                 )
-            for engine, cols in ((nc.vector, slice(0, cut)), (nc.gpsimd, slice(cut, PACK * C))):
-                engine.tensor_tensor(pulls[k][:, cols], flat(rests[k])[:, cols], difs[k][:, cols], ALU.mult)
+            parts[k] = {"vector": slice(0, cut), "gpsimd": slice(cut, PACK * C)}
+
+        def pull(name, k):
+            cols = parts[k][name]
+            {"vector": nc.vector, "gpsimd": nc.gpsimd}[name].tensor_tensor(pulls[k][:, cols], flat(rests[k])[:, cols], difs[k][:, cols], ALU.mult)
 
         def bank_view(room, pair):
             return room[:, pair * W : (pair + 1) * W].rearrange("p (e m) -> p e m", e=2)
@@ -402,7 +453,7 @@ def tile_list_replacement_item_scores_kernel(
                 )
 
         def regroup(k):
-            ygrouped[k] = sbuf([P, PACK * C], BF16, ("ga", "gb", "hw45")[k % 3])
+            ygrouped[k] = sbuf([P, PACK * C], BF16, ("ga", "gb", "gc")[k % 3])
             cut = C if k < last else LAST_SCALAR_COLS
             interleave(nc.scalar.copy, ygrouped[k][:, : PACK * cut], fall_of(k)[:, :, :cut])
             if cut < C:
@@ -416,17 +467,29 @@ def tile_list_replacement_item_scores_kernel(
                 scales_out(mh)
 
         z1late = {}
-        products(0)
+        gate_passes(0, 0)
+        q_passes(0, 0)
+        gate_passes(0, 1)
+        q_passes(0, 1)
+        q_passes(1, 0)
         for k in range(len(steps)):
             if k < 2:
-                z1late[k] = sbuf([P, PACK * C], BF16, ("h12", "aff7")[k])
-                interleave(nc.scalar.copy, z1late[k][:], zplanes(1, quarters[2 + k]))
+                z1late[k] = sbuf([P, PACK * C], BF16, "gb")
+                interleave(nc.scalar.copy, z1late[k][:], z1planes(quarters[2 + k]))
             difference(k)
+            if k == 1:
+                pull("vector", 0)
+            if k > 0:
+                pull("vector", k)
+            pull("gpsimd", k)
             if k in (1, 2):
-                split(zq, quantise(z1late[k - 1][:], C, "w1c%d" % (2 * k - 1), "zs%d" % k), [(1, 1 + k)], C)
+                split(zq, quantise(z1late[k - 1][:], C, "v_w%d" % k, "zs%d" % k), [(1, 1 + k)], C)
             if k >= PLANES_LAG:
                 step_planes(k - PLANES_LAG)
-            if k < last:
+            if k == 0:
+                q_passes(1, 1)
+                gates(1)
+            elif k < last:
                 products(k + 1)
             if k >= 1:
                 blend(k - 1)

@@ -82,12 +82,14 @@ def tile_list_replacement_item_scores_kernel(
 
         tab_s = sbuf([P, T], U8, "tab_s")
         nc.gpsimd.memset(tab_s[:].bitcast(I32), 0)
-        w4s_raw = sbuf([P, HB, N], U8, "w4s_raw")
-        nc.gpsimd.memset(w4s_raw[:].rearrange("p a n -> p (a n)").bitcast(I32), 0)
+        w4s_raw = sbuf([P, N], U8, "w4s_raw")
+        nc.gpsimd.memset(w4s_raw[:].bitcast(I32), 0)
         for q in range(4):
             nc.scalar.dma_start(
                 tab_s[32 * q : 32 * q + 4 * KP, :].bitcast(I32), tab_scales[:, 4 * q : 4 * q + 4, :].bitcast(I32)
             )
+        w4s = sbuf([P, HB, N], U8, "w4s")
+        nc.gpsimd.memset(w4s[:].rearrange("p a n -> p (a n)").bitcast(I32), 0)
         pages = [keep.tile([P, T2], F32, name="page%d" % i) for i in range(PACK + 1)]
         for page in pages:
             nc.gpsimd.memset(page[:], 0.0)
@@ -101,11 +103,7 @@ def tile_list_replacement_item_scores_kernel(
         raw1 = {}
         raw1[0, 0] = load_rows(w1, 0, 0, "raw0", 4)
         raw1[1, 0] = load_rows(w1, W, 0, "raw1", 2)
-        for r in range(4):
-            nc.sync.dma_start(
-                w4s_raw[r:P:32, :, :].bitcast(I32),
-                w4_scales[:, r:16:4, :].rearrange("a q n -> q a n").bitcast(I32),
-            )
+        nc.sync.dma_start(w4s_raw[0:P:4, :].bitcast(I32), w4_scales.rearrange("a q n -> (a q) n").bitcast(I32))
         load_table(0)
         load_table(1)
         raw1[2, 0] = load_rows(w1, 2 * W, 0, "raw2")
@@ -126,22 +124,6 @@ def tile_list_replacement_item_scores_kernel(
             b, i = divmod(n, PACK)
             affs[n] = room
             nc.sync.dma_start(room, aff[b * W : (b + 1) * W, :].rearrange("(p i) m -> p i m", i=PACK)[:, i, :])
-
-        aff01 = sbuf([P, 2 * T2], F32, "aff01")
-        aff23 = sbuf([P, 2 * T2], F32, "aff23")
-        aff7 = sbuf([P, T2], F32, "aff7")
-        raw2 = {}
-        raw1[0, 1] = load_rows(w1, 0, W, "raw3")
-        load_aff(0, aff01[:, :T2])
-        raw1[1, 1] = load_rows(w1, W, W, "raw4")
-        load_aff(1, aff01[:, T2:])
-        raw1[2, 1] = load_rows(w1, 2 * W, W, "raw5")
-        w4w_raw = sbuf([P, HB, 2 * N], U8, "w4w_raw")
-        nc.sync.dma_start(w4w_raw[:].bitcast(I32), w4_words.rearrange("a p c -> p a c").bitcast(I32))
-        load_aff(2, aff23[:, :T2])
-        raw2[0, 0] = load_rows(w2, 0, 0, "raw6")
-        raw2[1, 0] = load_rows(w2, W, 0, "raw7")
-        load_aff(3, aff23[:, T2:])
 
         v_s = sbuf([P, S], U8, "v_s")
         v_w = [sbuf([P, S], U32, "v_w%d" % a) for a in range(KP)]
@@ -170,13 +152,40 @@ def tile_list_replacement_item_scores_kernel(
         head_weight(1, "gb", P)
         gather_words(0, listed)
         gather_words(1, listed)
-        w4s = sbuf([P, HB * NG, PACK, P], U8, "w4s")
-        nc.vector.tensor_copy(w4s[:], w4s_raw[:].rearrange("p a (g m t) -> p (a g) t m", g=NG, t=PACK))
+        w4s_dealt = sbuf([P, N], U8, "w4s_dealt")
+        nc.vector.tensor_copy(
+            w4s_dealt[:].rearrange("p (g t m) -> p g t m", g=NG, t=PACK),
+            w4s_raw[:].rearrange("p (g m t) -> p g t m", g=NG, t=PACK),
+        )
         head_weight(2, "gc", HEAD_SCALAR_PLACES)
         gather_words(2, early)
         gather_words(2, later)
 
+        def place_scales(r):
+            for b in range(HB):
+                nc.sync.dma_start(w4s[r:P:32, b, :].bitcast(I32), w4s_dealt[64 * b + 4 * r : 64 * (b + 1) : 16, :].bitcast(I32))
+
+        aff01 = sbuf([P, 2 * T2], F32, "aff01")
+        aff23 = sbuf([P, 2 * T2], F32, "aff23")
+        aff7 = sbuf([P, T2], F32, "aff7")
+        raw2 = {}
+        raw1[0, 1] = load_rows(w1, 0, W, "raw3")
+        load_aff(0, aff01[:, :T2])
+        raw1[1, 1] = load_rows(w1, W, W, "raw4")
+        load_aff(1, aff01[:, T2:])
+        raw1[2, 1] = load_rows(w1, 2 * W, W, "raw5")
+        w4w_raw = sbuf([P, HB, 2 * N], U8, "w4w_raw")
+        nc.sync.dma_start(w4w_raw[:].bitcast(I32), w4_words.rearrange("a p c -> p a c").bitcast(I32))
+        load_aff(2, aff23[:, :T2])
+        raw2[0, 0] = load_rows(w2, 0, 0, "raw6")
+        place_scales(0)
+        raw2[1, 0] = load_rows(w2, W, 0, "raw7")
+        place_scales(1)
+        load_aff(3, aff23[:, T2:])
+        place_scales(2)
+
         raw2[0, 1] = load_rows(w2, 0, W, "raw0")
+        place_scales(3)
         aff45 = sbuf([P, 2 * T2], F32, "raw1")
         load_aff(4, aff45[:, :T2])
         raw2[1, 1] = load_rows(w2, W, W, "tab_w0")
@@ -364,7 +373,7 @@ def tile_list_replacement_item_scores_kernel(
             return w2q[b, g][0][:, cols].bitcast(FP8X4), w2q[b, g][1][:, cols]
 
         def w4_columns(b, g, t):
-            return w4w[:, b * NG + g, t, :].bitcast(FP4X4), w4s[:, b * NG + g, t, :]
+            return w4w[:, b * NG + g, t, :].bitcast(FP4X4), w4s[:, b, g * W + t * P : g * W + (t + 1) * P]
 
         def gate_passes(k, b):
             if b == 0:

@@ -167,7 +167,6 @@ def tile_list_replacement_item_scores_kernel(
 
         aff01 = sbuf([P, 2 * T2], F32, "aff01")
         aff23 = sbuf([P, 2 * T2], F32, "aff23")
-        aff7 = sbuf([P, T2], F32, "aff7")
         raw2 = {}
         raw1[0, 1] = load_rows(w1, 0, W, "raw3")
         load_aff(0, aff01[:, :T2])
@@ -178,21 +177,24 @@ def tile_list_replacement_item_scores_kernel(
         nc.sync.dma_start(w4w_raw[:].bitcast(I32), w4_words.rearrange("a p c -> p a c").bitcast(I32))
         load_aff(2, aff23[:, :T2])
         raw2[0, 0] = load_rows(w2, 0, 0, "raw6")
-        place_scales(0)
-        raw2[1, 0] = load_rows(w2, W, 0, "raw7")
-        place_scales(1)
         load_aff(3, aff23[:, T2:])
-        place_scales(2)
-
-        raw2[0, 1] = load_rows(w2, 0, W, "raw0")
-        place_scales(3)
+        raw2[1, 0] = load_rows(w2, W, 0, "raw7")
         aff45 = sbuf([P, 2 * T2], F32, "raw1")
         load_aff(4, aff45[:, :T2])
-        raw2[1, 1] = load_rows(w2, W, W, "tab_w0")
+        place_scales(0)
+        raw2[0, 1] = load_rows(w2, 0, W, "raw0")
+        place_scales(1)
         load_aff(5, aff45[:, T2:])
+        place_scales(2)
         aff6 = sbuf([P, T2], F32, "tab_w1")
         load_aff(6, aff6[:])
-        load_aff(7, aff7[:])
+        place_scales(3)
+        w2g1 = sbuf([P, HB * G], BF16, "gb")
+        aff7 = [w2g1[:, G : G + 2 * W].bitcast(F32), sbuf([P, W], F32, "aff7")[:]]
+        rows7 = aff[W:, :].rearrange("(p i) m -> p i m", i=PACK)[:, PACK - 1, :]
+        nc.sync.dma_start(aff7[0], rows7[:, :W])
+        raw2[1, 1] = load_rows(w2, W, W, "tab_w0")
+        nc.sync.dma_start(aff7[1], rows7[:, W:])
         falls = {}
         falls[0, 0] = load_rows(fall, 0, 0, "raw2")
 
@@ -295,52 +297,55 @@ def tile_list_replacement_item_scores_kernel(
         for n in range(PACK, PLANES):
             scatter(n, hs[n])
 
-        w2_at = PACK * T2 - W
-        w2g00 = sbuf([P, G], BF16, "ga")
-        cast_weight(w2g00[:], raw2[0, 0])
-        late = sbuf([P, w2_at + G], BF16, "raw6")
-        w2g0 = [w2g00[:], late[:, w2_at:]]
-        cast_weight(w2g0[1], raw2[1, 0])
-        w2g1 = sbuf([P, HB * G], BF16, "gb")
+        w2g0 = [sbuf([P, G], BF16, slot)[:] for slot in ("ga", "w2g10")]
+        for b in range(HB):
+            cast_weight(w2g0[b], raw2[b, 0])
         cast_weight(w2g1[:, :G], raw2[0, 1])
+        late = sbuf([P, PACK * T2], BF16, "raw6")
         for n in range(PACK, PLANES):
-            zplane[n] = late[:, (n - PACK) * T2 : (n - PACK + 1) * T2]
+            zplane[n] = late[:].rearrange("p (u m e) -> p u e m", u=2, e=2)[:, n // 2 % 2, n % 2]
         for n in range(3, PLANES - 1):
             weigh(nc.gpsimd, n, whole)
 
-        pairs = work[:, : 2 * pair_step].bitcast(U32).rearrange("p (u x) -> p u x", u=2)
-        z0g = [sbuf([P, G], BF16, slot)[:] for slot in ("z0a", "gc")]
-        for mh in range(MH):
-            nc.scalar.copy(
-                z0g[mh].bitcast(U32).rearrange("p (c i u) -> p c u i", i=PACK, u=2),
-                pairs[:, :, halves[mh]].rearrange("p u (c i) -> p c u i", i=PACK),
-            )
-        cast_weight(w2g1[:, G:], raw2[1, 1])
+        pairs = [
+            work[:, : 2 * pair_step].bitcast(U32).rearrange("p (u x) -> p u x", u=2),
+            late[:].bitcast(U32).rearrange("p (u x) -> p u x", u=2),
+        ]
 
-        def z1planes(cols):
-            return late[:, : PACK * T2].rearrange("p (t m) -> p t m", t=PACK)[:, :, cols]
+        def weave(b, cols, slot):
+            grouped = sbuf([P, PACK * (cols.stop - cols.start)], BF16, slot)
+            nc.scalar.copy(
+                grouped[:].bitcast(U32).rearrange("p (c i u) -> p c u i", i=PACK, u=2),
+                pairs[b][:, :, cols].rearrange("p u (c i) -> p c u i", i=PACK),
+            )
+            return grouped[:]
+
+        z0g = [weave(0, halves[mh], ("z0a", "gc")[mh]) for mh in range(MH)]
 
         def split(store, pair, keys, width):
             codes, scales = pair
             for j, key in enumerate(keys):
                 store[key] = codes[:, j * width : (j + 1) * width], scales[:, j * width : (j + 1) * width]
 
+        def weigh_last(mh):
+            cols = halves[mh]
+            nc.vector.tensor_tensor(zplane[PLANES - 1][:, cols], page_of[PLANES - 1][:, cols], aff7[mh], ALU.mult)
+
         zq = {}
         w2q = {}
         split(zq, quantise(z0g[0], W, "tab_w1", "w1s0"), [(0, 0), (0, 1)], C)
-        weigh(nc.vector, PLANES - 1, halves[0])
-        z1g = [sbuf([P, PACK * C], BF16, slot) for slot in ("h0", "w4w_raw")]
-        for j in range(2):
-            interleave(nc.scalar.copy, z1g[j][:], z1planes(quarters[j]))
-        split(zq, quantise(z0g[1], W, "w1c1", "w1s1"), [(0, 2), (0, 3)], C)
+        weigh_last(0)
+        z1g = [weave(1, quarters[j], ("h0", "h3")[j]) for j in range(2)]
+        cast_weight(w2g1[:, G:], raw2[1, 1])
         codes = sbuf([P, HB * W], U32, "z0a")
         scales = sbuf([P, HB * W], U8, "w2s0")
         split(w2q, (codes, scales), [(0, 0), (1, 0)], W)
         nc.vector.quantize_mx(w2q[0, 0][0].bitcast(FP8X4), w2q[0, 0][1], w2g0[0])
-        split(zq, quantise(z1g[0][:], C, "w1c2", "w1s2"), [(1, 0)], C)
+        split(zq, quantise(z1g[0], C, "w1c2", "w1s2"), [(1, 0)], C)
         nc.vector.quantize_mx(w2q[1, 0][0].bitcast(FP8X4), w2q[1, 0][1], w2g0[1])
-        split(zq, quantise(z1g[1][:], C, "v_w0", "zs0"), [(1, 1)], C)
-        weigh(nc.vector, PLANES - 1, halves[1])
+        split(zq, quantise(z1g[1], C, "v_w0", "zs0"), [(1, 1)], C)
+        weigh_last(1)
+        split(zq, quantise(z0g[1], W, "ga", "w1s1"), [(0, 2), (0, 3)], C)
         split(w2q, quantise(w2g1[:], HB * W, "h0", "w2s1"), [(0, 1), (1, 1)], W)
 
         y_s = sbuf([P, NG, T2], U8, "y_s")
@@ -428,6 +433,8 @@ def tile_list_replacement_item_scores_kernel(
                     bank_view(difs[k], pair), fall_of(k)[:, 2 * pair : 2 * pair + 2, :], q_banks[k][pair][:], ALU.subtract
                 )
             parts[k] = {"vector": slice(0, cut), "gpsimd": slice(cut, PACK * C)}
+            if k == 0:
+                parts[k] = {"vector": slice(share, PACK * C), "gpsimd": slice(0, share)}
 
         def pull(name, k):
             cols = parts[k][name]
@@ -462,7 +469,7 @@ def tile_list_replacement_item_scores_kernel(
                 )
 
         def regroup(k):
-            ygrouped[k] = sbuf([P, PACK * C], BF16, ("ga", "gb", "gc")[k % 3])
+            ygrouped[k] = sbuf([P, PACK * C], BF16, ("w2g10", "gb", "gc")[k % 3])
             cut = C if k < last else LAST_SCALAR_COLS
             interleave(nc.scalar.copy, ygrouped[k][:, : PACK * cut], fall_of(k)[:, :, :cut])
             if cut < C:
@@ -483,8 +490,7 @@ def tile_list_replacement_item_scores_kernel(
         q_passes(1, 0)
         for k in range(len(steps)):
             if k < 2:
-                z1late[k] = sbuf([P, PACK * C], BF16, "gb")
-                interleave(nc.scalar.copy, z1late[k][:], z1planes(quarters[2 + k]))
+                z1late[k] = weave(1, quarters[2 + k], "gb")
             difference(k)
             if k == 1:
                 pull("vector", 0)
@@ -492,7 +498,7 @@ def tile_list_replacement_item_scores_kernel(
                 pull("vector", k)
             pull("gpsimd", k)
             if k in (1, 2):
-                split(zq, quantise(z1late[k - 1][:], C, "v_w%d" % k, "zs%d" % k), [(1, 1 + k)], C)
+                split(zq, quantise(z1late[k - 1], C, "v_w%d" % k, "zs%d" % k), [(1, 1 + k)], C)
             if k >= PLANES_LAG:
                 step_planes(k - PLANES_LAG)
             if k == 0:

@@ -109,13 +109,8 @@ def tile_list_replacement_item_scores_kernel(
         raw1[2, 0] = load_rows(w1, 2 * W, 0, "raw2")
         nc.sync.dma_start(idx2[:], offs2)
         load_table(2)
-        w1_at = T2
-        hw3_at = w1_at + KP * G // 2 - TIE_COLS
-        pair_step = hw3_at - T2
-        wg_at = hw3_at + S
-        work = sbuf([P, max(2 * pair_step, wg_at + 3 * S)], F32, "work")
-        work16 = work[:].bitcast(BF16)
-        wg = work[:, wg_at : wg_at + S]
+        early_h = sbuf([P, 3 * S], F32, "early_h")
+        wg = early_h[:, :S]
         nc.sync.dma_start(wg, wgs)
 
         affs = {}
@@ -172,7 +167,10 @@ def tile_list_replacement_item_scores_kernel(
         load_aff(0, aff01[:, :T2])
         raw1[1, 1] = load_rows(w1, W, W, "raw4")
         load_aff(1, aff01[:, T2:])
-        raw1[2, 1] = load_rows(w1, 2 * W, W, "raw5")
+        last_w1 = [sbuf([P, PACK, C], F32, slot) for slot in ("raw5", "ga")]
+        for half in range(2):
+            rows = w1[2 * W :, W + half * C : W + (half + 1) * C]
+            nc.sync.dma_start(last_w1[half][:], rows.rearrange("(p j) c -> p j c", j=PACK))
         w4w_raw = sbuf([P, HB, 2 * N], U8, "w4w_raw")
         nc.sync.dma_start(w4w_raw[:].bitcast(I32), w4_words.rearrange("a p c -> p a c").bitcast(I32))
         load_aff(2, aff23[:, :T2])
@@ -200,7 +198,7 @@ def tile_list_replacement_item_scores_kernel(
 
         h0 = sbuf([P, S], F32, "h0")
         h3 = sbuf([P, S], F32, "h3")
-        hs = [h0[:], work[:, wg_at + S : wg_at + 2 * S], work[:, wg_at + 2 * S : wg_at + 3 * S], h3[:]]
+        hs = [h0[:], early_h[:, S : 2 * S], early_h[:, 2 * S :], h3[:]]
 
         def first_pass(out, a, n, moving, start, stop):
             codes, scales = w1q[a, n]
@@ -216,11 +214,6 @@ def tile_list_replacement_item_scores_kernel(
 
         def scatter(n, hw):
             nc.vector.tensor_copy(page_of[n][:].indirect(idx2[:]), hw)
-
-        zplane = {}
-        for n in range(PACK):
-            at = 2 * pair_step * (n // 2)
-            zplane[n] = work16[:, at : at + 2 * T2].rearrange("p (m e) -> p m e", e=2)[:, :, n % 2]
 
         def weigh(engine, n, cols):
             engine.tensor_tensor(zplane[n][:, cols], page_of[n][:, cols], affs[n][:, cols], ALU.mult)
@@ -242,25 +235,43 @@ def tile_list_replacement_item_scores_kernel(
         for i in range(1, PACK):
             nc.scalar.activation(hs[i], accs[i][:], ACT.Silu)
 
+        w1_at = T2
+        hw3_at = w1_at + KP * G // 2 - TIE_COLS
+        pair_step = hw3_at - T2
+        work = sbuf([P, 2 * pair_step], F32, "w1c2")
+        work16 = work[:].bitcast(BF16)
+        zplane = {}
+        for n in range(PACK):
+            at = 2 * pair_step * (n // 2)
+            zplane[n] = work16[:, at : at + 2 * T2].rearrange("p (m e) -> p m e", e=2)[:, :, n % 2]
+
         w1g = work16[:, 2 * w1_at : 2 * w1_at + KP * G]
 
-        def cast_planes(a, t0, t1):
+        def cast_planes(a, raw, m0, t0, t1):
+            places = raw.shape[2] // PACK
             nc.scalar.copy(
-                w1g.rearrange("p (t a m j) -> p a m j t", t=PACK, a=KP, j=PACK)[:, a, :, :, t0:t1],
-                raw1[a, 1][:].rearrange("p j (m t) -> p m j t", t=PACK)[:, :, :, t0:t1],
+                w1g.rearrange("p (t a m j) -> p a m j t", t=PACK, a=KP, j=PACK)[:, a, m0 : m0 + places, :, t0:t1],
+                raw[:].rearrange("p j (m t) -> p m j t", t=PACK)[:, :, :, t0:t1],
             )
 
         for a in range(KP - 1):
-            cast_planes(a, 0, PACK)
-        cast_planes(KP - 1, 0, 2)
-        cast_planes(KP - 1, 2, PACK)
+            cast_planes(a, raw1[a, 1], 0, 0, PACK)
+        cast_planes(KP - 1, last_w1[0], 0, 0, PACK)
+        cast_planes(KP - 1, last_w1[1], P // 2, 0, 2)
+        cast_planes(KP - 1, last_w1[1], P // 2, 2, PACK)
         falls[1, 0] = load_rows(fall, W, 0, "raw3")
         falls[0, 1] = load_rows(fall, 0, W, "raw4")
         falls[1, 1] = load_rows(fall, W, W, "raw5")
-        w4w = sbuf([P, HB * NG, PACK, 2 * P], U8, "w4w")
-        nc.scalar.copy(
-            w4w[:].bitcast(U16), w4w_raw[:].bitcast(U16).rearrange("p a (g m t) -> p (a g) t m", g=NG, t=PACK)
-        )
+        w4w = {}
+
+        def deal_words(b):
+            w4w[b] = sbuf([P, NG, PACK, 2 * P], U8, ("w4w", "w1c3")[b])
+            nc.scalar.copy(
+                w4w[b][:].bitcast(U16),
+                w4w_raw[:, b, :].bitcast(U16).rearrange("p (g m t) -> p g t m", g=NG, t=PACK),
+            )
+
+        deal_words(0)
 
         nc.vector.tensor_tensor(page_of[0][:].indirect(entries(idx2, early)), hs[0][:, early], wg[:, early], ALU.mult)
         nc.vector.tensor_tensor(hs[0][:, later], hs[0][:, later], wg[:, later], ALU.mult)
@@ -287,17 +298,17 @@ def tile_list_replacement_item_scores_kernel(
                 w1q[a, PACK + i] = codes[:, i, a * P : (a + 1) * P], plane_scales[:, a * P : (a + 1) * P]
                 first_pass(accs[i][:], a, PACK + i, listed, a == 0, a == KP - 1)
             nc.scalar.activation(hs[PACK + i], accs[i][:], ACT.Silu)
+        deal_words(1)
         nc.vector.tensor_tensor(hw3[:, :TIE_COLS], hs[3][:, :TIE_COLS], wg[:, :TIE_COLS], ALU.mult)
         scatter(3, hw3)
-        weigh(nc.gpsimd, 2, halves[0])
+        weigh(nc.gpsimd, 2, whole)
         nc.gpsimd.tensor_tensor(hs[4], hs[4], wg, ALU.mult)
-        weigh(nc.gpsimd, 2, halves[1])
         nc.gpsimd.tensor_tensor(hs[5], hs[5], wg, ALU.mult)
         nc.gpsimd.tensor_tensor(h47[:, 2:, :], h47[:, 2:, :], wg.unsqueeze(1).to_broadcast([P, 2, S]), ALU.mult)
         for n in range(PACK, PLANES):
             scatter(n, hs[n])
 
-        w2g0 = [sbuf([P, G], BF16, slot)[:] for slot in ("ga", "w2g10")]
+        w2g0 = [sbuf([P, G], BF16, "w1s3")[:], work16[:, 2 * (hw3_at + S) : 2 * (hw3_at + S) + G]]
         for b in range(HB):
             cast_weight(w2g0[b], raw2[b, 0])
         cast_weight(w2g1[:, :G], raw2[0, 1])
@@ -341,11 +352,11 @@ def tile_list_replacement_item_scores_kernel(
         scales = sbuf([P, HB * W], U8, "w2s0")
         split(w2q, (codes, scales), [(0, 0), (1, 0)], W)
         nc.vector.quantize_mx(w2q[0, 0][0].bitcast(FP8X4), w2q[0, 0][1], w2g0[0])
-        split(zq, quantise(z1g[0], C, "w1c2", "w1s2"), [(1, 0)], C)
+        split(zq, quantise(z1g[0], C, "w1c1", "w1s2"), [(1, 0)], C)
         nc.vector.quantize_mx(w2q[1, 0][0].bitcast(FP8X4), w2q[1, 0][1], w2g0[1])
         split(zq, quantise(z1g[1], C, "v_w0", "zs0"), [(1, 1)], C)
         weigh_last(1)
-        split(zq, quantise(z0g[1], W, "ga", "w1s1"), [(0, 2), (0, 3)], C)
+        split(zq, quantise(z0g[1], W, "w1s3", "w1s1"), [(0, 2), (0, 3)], C)
         split(w2q, quantise(w2g1[:], HB * W, "h0", "w2s1"), [(0, 1), (1, 1)], W)
 
         y_s = sbuf([P, NG, T2], U8, "y_s")
@@ -378,7 +389,7 @@ def tile_list_replacement_item_scores_kernel(
             return w2q[b, g][0][:, cols].bitcast(FP8X4), w2q[b, g][1][:, cols]
 
         def w4_columns(b, g, t):
-            return w4w[:, b * NG + g, t, :].bitcast(FP4X4), w4s[:, b, g * W + t * P : g * W + (t + 1) * P]
+            return w4w[b][:, g, t, :].bitcast(FP4X4), w4s[:, b, g * W + t * P : g * W + (t + 1) * P]
 
         def gate_passes(k, b):
             if b == 0:
@@ -425,7 +436,7 @@ def tile_list_replacement_item_scores_kernel(
             share = {0: GP_FIRST_COLS, last: GP_LAST_COLS}.get(k, GP_COLS)
             cut = PACK * C - share
             shift = max(share, cut) if k > 0 else PACK * C
-            room = sbuf([P, shift + PACK * C], F32, ("raw7", "raw1", "work")[k % 3])
+            room = sbuf([P, shift + PACK * C], F32, ("raw7", "raw1", "w1c2")[k % 3])
             pulls[k] = room[:, : PACK * C]
             difs[k] = room[:, shift:]
             for pair in range(2):
@@ -469,7 +480,7 @@ def tile_list_replacement_item_scores_kernel(
                 )
 
         def regroup(k):
-            ygrouped[k] = sbuf([P, PACK * C], BF16, ("w2g10", "gb", "gc")[k % 3])
+            ygrouped[k] = sbuf([P, PACK * C], BF16, ("w4w_raw", "gb", "gc")[k % 3])
             cut = C if k < last else LAST_SCALAR_COLS
             interleave(nc.scalar.copy, ygrouped[k][:, : PACK * cut], fall_of(k)[:, :, :cut])
             if cut < C:

@@ -31,7 +31,7 @@ GP_FIRST_COLS = 384
 GP_LAST_COLS = 416
 PLANES_LAG = 3
 TIE_COLS = 16
-LAST_SCALAR_COLS = 80
+LAST_SCALAR_COLS = 128
 EARLY = 128
 HEAD_SCALAR_PLACES = 48
 
@@ -332,6 +332,9 @@ def tile_list_replacement_item_scores_kernel(
             return grouped[:]
 
         z0g = [weave(0, halves[mh], ("z0a", "gc")[mh]) for mh in range(MH)]
+
+        warm = sbuf([P, 1], F32, "warm")
+        nc.scalar.activation(warm[:], z0g[1][:, :1], ACT.Sigmoid)
 
         def split(store, pair, keys, width):
             codes, scales = pair

from contextlib import ExitStack

import concourse.mybir as mybir

K, H, N, T, S, T2 = 1536, 1024, 1024, 2048, 512, 1024
FLOPS = 2 * K * H * S + 2 * 2 * H * N * T2

F32 = mybir.dt.float32
BF16 = mybir.dt.bfloat16
I32 = mybir.dt.int32
U32 = mybir.dt.uint32
U16 = mybir.dt.uint16
U8 = mybir.dt.uint8
FP8X4 = mybir.dt.float8_e4m3fn_x4
FP4X4 = mybir.dt.float4_e2m1fn_x4
ALU = mybir.AluOpType
ACT = mybir.ActivationFunctionType

P = 128
PACK = 4
W = 512
G = PACK * W
KP = K // W
HB = H // W
NG = N // W
MH = T2 // W
PLANES = HB * PACK
C = 256
GP_COLS = 928
GP_FIRST_COLS = 384
GP_LAST_COLS = 416
PLANES_LAG = 3
TIE_COLS = 16
LAST_SCALAR_COLS = 128
EARLY = 128
HEAD_SCALAR_PLACES = 48


def tile_list_replacement_item_scores_kernel(
    tc, tab_words, tab_scales, offs, w1, wgs, offs2, aff, w4_words, w4_scales, w2, fall, out_0, out_1, out_2
):
    nc = tc.nc
    with ExitStack() as ctx:
        keep = ctx.enter_context(tc.tile_pool(name="keep", bufs=1))
        psum = ctx.enter_context(tc.psum_pool(name="psum", bufs=1))

        def sbuf(shape, dtype, slot):
            return keep.tile(shape, dtype, name=slot, align_bytes=64)

        idx = keep.tile([P, S // 16], U16, name="idx")
        idx2 = keep.tile([P, S // 16], U16, name="idx2")
        nc.sync.dma_start(idx[:], offs)

        def load_rows(src, k0, c0, slot, pieces=1):
            raw = sbuf([P, PACK, W], F32, slot)
            rows = src[k0 : k0 + W, c0 : c0 + W].rearrange("(p j) c -> p j c", j=PACK)
            step = PACK // pieces
            for j in range(0, PACK, step):
                nc.sync.dma_start(raw[:, j : j + step, :], rows[:, j : j + step, :])
            return raw

        def cast_part(copy, grouped, raw, m0, m1):
            copy(
                grouped.rearrange("p (t m j) -> p m j t", t=PACK, j=PACK)[:, m0:m1],
                raw[:].rearrange("p j (m t) -> p m j t", t=PACK)[:, m0:m1],
            )

        def cast_weight(grouped, raw):
            cast_part(nc.scalar.copy, grouped, raw, 0, P)

        def interleave(copy, grouped, planes):
            copy(
                grouped.rearrange("p (c i t) -> p c t i", i=PACK, t=PACK),
                planes.rearrange("p t (c i) -> p c t i", i=PACK),
            )

        def quantise(grouped, words, codes_slot, scales_slot):
            codes = sbuf([P, words], U32, codes_slot)
            scales = sbuf([P, words], U8, scales_slot)
            nc.vector.quantize_mx(codes[:].bitcast(FP8X4), scales[:], grouped)
            return codes, scales

        tab_s = sbuf([P, T], U8, "tab_s")
        nc.gpsimd.memset(tab_s[:].bitcast(I32), 0)
        w4s_raw = sbuf([P, N], U8, "w4s_raw")
        nc.gpsimd.memset(w4s_raw[:].bitcast(I32), 0)
        for q in range(4):
            nc.scalar.dma_start(
                tab_s[32 * q : 32 * q + 4 * KP, :].bitcast(I32), tab_scales[:, 4 * q : 4 * q + 4, :].bitcast(I32)
            )
        w4s = sbuf([P, HB, N], U8, "w4s")
        nc.gpsimd.memset(w4s[:].rearrange("p a n -> p (a n)").bitcast(I32), 0)
        pages = [keep.tile([P, T2], F32, name="page%d" % i) for i in range(PACK + 1)]
        for page in pages:
            nc.gpsimd.memset(page[:], 0.0)
        page_of = [pages[n % PACK] for n in range(PLANES - 1)] + [pages[PACK]]

        tab_w = [sbuf([P, T], U32, "tab_w%d" % a) for a in range(KP)]

        def load_table(a):
            nc.sync.dma_start(tab_w[a][:].bitcast(I32), tab_words[a].rearrange("p t i -> p (t i)").bitcast(I32))

        raw1 = {}
        raw1[0, 0] = load_rows(w1, 0, 0, "raw0", 4)
        raw1[1, 0] = load_rows(w1, W, 0, "raw1", 2)
        nc.sync.dma_start(w4s_raw[0:P:4, :].bitcast(I32), w4_scales.rearrange("a q n -> (a q) n").bitcast(I32))
        load_table(0)
        load_table(1)
        raw1[2, 0] = load_rows(w1, 2 * W, 0, "raw2")
        nc.sync.dma_start(idx2[:], offs2)
        load_table(2)
        early_h = sbuf([P, 3 * S], F32, "early_h")
        wg = early_h[:, :S]
        nc.sync.dma_start(wg, wgs)

        affs = {}

        def load_aff(n, room):
            b, i = divmod(n, PACK)
            affs[n] = room
            nc.sync.dma_start(room, aff[b * W : (b + 1) * W, :].rearrange("(p i) m -> p i m", i=PACK)[:, i, :])

        v_s = sbuf([P, S], U8, "v_s")
        v_w = [sbuf([P, S], U32, "v_w%d" % a) for a in range(KP)]
        w1q = {}

        def entries(offsets, cols):
            return offsets[:, cols.start // 16 : cols.stop // 16]

        def gather_words(a, cols):
            nc.vector.tensor_copy(v_w[a][:, cols], tab_w[a][:].indirect(entries(idx, cols)))

        def head_weight(a, slot, scalar_places):
            grouped = sbuf([P, G], BF16, slot)
            cast_part(nc.scalar.copy, grouped[:], raw1[a, 0], 0, scalar_places)
            if scalar_places < P:
                cast_part(nc.vector.tensor_copy, grouped[:], raw1[a, 0], scalar_places, P)
            codes, scales = quantise(grouped[:], W, "w1c%d" % a, "w1s%d" % a)
            for i in range(PACK):
                w1q[a, i] = codes[:, i * P : (i + 1) * P], scales[:, i * P : (i + 1) * P]

        nc.vector.tensor_copy(v_s[:], tab_s[:].indirect(idx[:]))
        listed = slice(0, S)
        early = slice(0, EARLY)
        later = slice(EARLY, S)
        head_weight(0, "ga", P)
        head_weight(1, "gb", P)
        gather_words(0, listed)
        gather_words(1, listed)
        w4s_dealt = sbuf([P, N], U8, "w4s_dealt")
        nc.vector.tensor_copy(
            w4s_dealt[:].rearrange("p (g t m) -> p g t m", g=NG, t=PACK),
            w4s_raw[:].rearrange("p (g m t) -> p g t m", g=NG, t=PACK),
        )
        head_weight(2, "gc", HEAD_SCALAR_PLACES)
        gather_words(2, early)
        gather_words(2, later)

        def place_scales(r):
            for b in range(HB):
                nc.sync.dma_start(w4s[r:P:32, b, :].bitcast(I32), w4s_dealt[64 * b + 4 * r : 64 * (b + 1) : 16, :].bitcast(I32))

        aff01 = sbuf([P, 2 * T2], F32, "aff01")
        aff23 = sbuf([P, 2 * T2], F32, "aff23")
        raw2 = {}
        raw1[0, 1] = load_rows(w1, 0, W, "raw3")
        load_aff(0, aff01[:, :T2])
        raw1[1, 1] = load_rows(w1, W, W, "raw4")
        load_aff(1, aff01[:, T2:])
        last_w1 = [sbuf([P, PACK, C], F32, slot) for slot in ("raw5", "ga")]
        for half in range(2):
            rows = w1[2 * W :, W + half * C : W + (half + 1) * C]
            nc.sync.dma_start(last_w1[half][:], rows.rearrange("(p j) c -> p j c", j=PACK))
        w4w_raw = sbuf([P, HB, 2 * N], U8, "w4w_raw")
        nc.sync.dma_start(w4w_raw[:].bitcast(I32), w4_words.rearrange("a p c -> p a c").bitcast(I32))
        load_aff(2, aff23[:, :T2])
        raw2[0, 0] = load_rows(w2, 0, 0, "raw6")
        load_aff(3, aff23[:, T2:])
        raw2[1, 0] = load_rows(w2, W, 0, "raw7")
        aff45 = sbuf([P, 2 * T2], F32, "raw1")
        load_aff(4, aff45[:, :T2])
        place_scales(0)
        raw2[0, 1] = load_rows(w2, 0, W, "raw0")
        place_scales(1)
        load_aff(5, aff45[:, T2:])
        place_scales(2)
        aff6 = sbuf([P, T2], F32, "tab_w1")
        load_aff(6, aff6[:])
        place_scales(3)
        w2g1 = sbuf([P, HB * G], BF16, "gb")
        aff7 = [w2g1[:, G : G + 2 * W].bitcast(F32), sbuf([P, W], F32, "aff7")[:]]
        rows7 = aff[W:, :].rearrange("(p i) m -> p i m", i=PACK)[:, PACK - 1, :]
        nc.sync.dma_start(aff7[0], rows7[:, :W])
        raw2[1, 1] = load_rows(w2, W, W, "tab_w0")
        nc.sync.dma_start(aff7[1], rows7[:, W:])
        falls = {}
        falls[0, 0] = load_rows(fall, 0, 0, "raw2")

        h0 = sbuf([P, S], F32, "h0")
        h3 = sbuf([P, S], F32, "h3")
        hs = [h0[:], early_h[:, S : 2 * S], early_h[:, 2 * S :], h3[:]]

        def first_pass(out, a, n, moving, start, stop):
            codes, scales = w1q[a, n]
            nc.tensor.matmul_mx(
                out,
                lhsT=codes.bitcast(FP8X4),
                lhsT_scale=scales,
                rhs=v_w[a][:, moving].bitcast(FP8X4),
                rhs_scale=v_s[4 * a :, moving],
                start=start,
                stop=stop,
            )

        def scatter(n, hw):
            nc.vector.tensor_copy(page_of[n][:].indirect(idx2[:]), hw)

        def weigh(engine, n, cols):
            engine.tensor_tensor(zplane[n][:, cols], page_of[n][:, cols], affs[n][:, cols], ALU.mult)

        whole = slice(0, T2)
        halves = [slice(mh * W, (mh + 1) * W) for mh in range(MH)]
        quarters = [slice(j * C, (j + 1) * C) for j in range(T2 // C)]

        acc_early = psum.tile([P, S], F32, name="q", bufs=6)
        accs = [psum.tile([P, S], F32, name="q", bufs=6) for i in range(PACK)]
        for a in range(KP):
            first_pass(acc_early[:, early], a, 0, early, a == 0, a == KP - 1)
            first_pass(accs[0][:, EARLY:C], a, 0, slice(EARLY, C), a == 0, False)
            first_pass(accs[0][:, C:], a, 0, slice(C, S), False, a == KP - 1)
            for i in range(1, PACK):
                first_pass(accs[i][:], a, i, listed, a == 0, a == KP - 1)
        nc.scalar.activation(hs[0][:, early], acc_early[:, early], ACT.Silu)
        nc.scalar.activation(hs[0][:, later], accs[0][:, later], ACT.Silu)
        for i in range(1, PACK):
            nc.scalar.activation(hs[i], accs[i][:], ACT.Silu)

        w1_at = T2
        hw3_at = w1_at + KP * G // 2 - TIE_COLS
        pair_step = hw3_at - T2
        work = sbuf([P, 2 * pair_step], F32, "w1c2")
        work16 = work[:].bitcast(BF16)
        zplane = {}
        for n in range(PACK):
            at = 2 * pair_step * (n // 2)
            zplane[n] = work16[:, at : at + 2 * T2].rearrange("p (m e) -> p m e", e=2)[:, :, n % 2]

        w1g = work16[:, 2 * w1_at : 2 * w1_at + KP * G]

        def cast_planes(a, raw, m0, t0, t1):
            places = raw.shape[2] // PACK
            nc.scalar.copy(
                w1g.rearrange("p (t a m j) -> p a m j t", t=PACK, a=KP, j=PACK)[:, a, m0 : m0 + places, :, t0:t1],
                raw[:].rearrange("p j (m t) -> p m j t", t=PACK)[:, :, :, t0:t1],
            )

        for a in range(KP - 1):
            cast_planes(a, raw1[a, 1], 0, 0, PACK)
        cast_planes(KP - 1, last_w1[0], 0, 0, PACK)
        cast_planes(KP - 1, last_w1[1], P // 2, 0, 2)
        cast_planes(KP - 1, last_w1[1], P // 2, 2, PACK)
        falls[1, 0] = load_rows(fall, W, 0, "raw3")
        falls[0, 1] = load_rows(fall, 0, W, "raw4")
        falls[1, 1] = load_rows(fall, W, W, "raw5")
        w4w = {}

        def deal_words(b):
            w4w[b] = sbuf([P, NG, PACK, 2 * P], U8, ("w4w", "w1c3")[b])
            nc.scalar.copy(
                w4w[b][:].bitcast(U16),
                w4w_raw[:, b, :].bitcast(U16).rearrange("p (g m t) -> p g t m", g=NG, t=PACK),
            )

        deal_words(0)

        nc.vector.tensor_tensor(page_of[0][:].indirect(entries(idx2, early)), hs[0][:, early], wg[:, early], ALU.mult)
        nc.vector.tensor_tensor(hs[0][:, later], hs[0][:, later], wg[:, later], ALU.mult)
        for n in (1, 2):
            nc.gpsimd.tensor_tensor(hs[n], hs[n], wg, ALU.mult)
        hw3 = work[:, hw3_at : hw3_at + S]
        nc.gpsimd.tensor_tensor(hw3[:, TIE_COLS:], hs[3][:, TIE_COLS:], wg[:, TIE_COLS:], ALU.mult)
        nc.vector.tensor_copy(page_of[0][:].indirect(entries(idx2, later)), hs[0][:, later])
        for n in (1, 2):
            scatter(n, hs[n])
        for n in range(2):
            weigh(nc.gpsimd, n, whole)

        accs = [psum.tile([P, S], F32, name="q", bufs=6) for i in range(2)]
        accs = accs + [psum.tile([P, S], F32, name="gate", bufs=2) for i in range(2)]
        h47 = sbuf([P, PACK, S], F32, "tab_w2")
        hs.extend([h47[:, i, :] for i in range(PACK)])
        codes = sbuf([P, PACK, KP * P], U32, "w1c3")
        scales = sbuf([P, PACK * KP * P], U8, "w1s3")
        for i in range(PACK):
            plane_scales = scales[:, i * KP * P : (i + 1) * KP * P]
            nc.vector.quantize_mx(codes[:, i, :].bitcast(FP8X4), plane_scales, w1g[:, i * KP * W : (i + 1) * KP * W])
            for a in range(KP):
                w1q[a, PACK + i] = codes[:, i, a * P : (a + 1) * P], plane_scales[:, a * P : (a + 1) * P]
                first_pass(accs[i][:], a, PACK + i, listed, a == 0, a == KP - 1)
            nc.scalar.activation(hs[PACK + i], accs[i][:], ACT.Silu)
        deal_words(1)
        nc.vector.tensor_tensor(hw3[:, :TIE_COLS], hs[3][:, :TIE_COLS], wg[:, :TIE_COLS], ALU.mult)
        scatter(3, hw3)
        weigh(nc.gpsimd, 2, whole)
        nc.gpsimd.tensor_tensor(hs[4], hs[4], wg, ALU.mult)
        nc.gpsimd.tensor_tensor(hs[5], hs[5], wg, ALU.mult)
        nc.gpsimd.tensor_tensor(h47[:, 2:, :], h47[:, 2:, :], wg.unsqueeze(1).to_broadcast([P, 2, S]), ALU.mult)
        for n in range(PACK, PLANES):
            scatter(n, hs[n])

        w2g0 = [sbuf([P, G], BF16, "w1s3")[:], work16[:, 2 * (hw3_at + S) : 2 * (hw3_at + S) + G]]
        for b in range(HB):
            cast_weight(w2g0[b], raw2[b, 0])
        cast_weight(w2g1[:, :G], raw2[0, 1])
        late = sbuf([P, PACK * T2], BF16, "raw6")
        for n in range(PACK, PLANES):
            zplane[n] = late[:].rearrange("p (u m e) -> p u e m", u=2, e=2)[:, n // 2 % 2, n % 2]
        for n in range(3, PLANES - 1):
            weigh(nc.gpsimd, n, whole)

        pairs = [
            work[:, : 2 * pair_step].bitcast(U32).rearrange("p (u x) -> p u x", u=2),
            late[:].bitcast(U32).rearrange("p (u x) -> p u x", u=2),
        ]

        def weave(b, cols, slot):
            grouped = sbuf([P, PACK * (cols.stop - cols.start)], BF16, slot)
            nc.scalar.copy(
                grouped[:].bitcast(U32).rearrange("p (c i u) -> p c u i", i=PACK, u=2),
                pairs[b][:, :, cols].rearrange("p u (c i) -> p c u i", i=PACK),
            )
            return grouped[:]

        z0g = [weave(0, halves[mh], ("z0a", "gc")[mh]) for mh in range(MH)]

        warm = sbuf([P, 1], F32, "warm")
        nc.scalar.activation(warm[:], z0g[1][:, :1], ACT.Sigmoid)

        def split(store, pair, keys, width):
            codes, scales = pair
            for j, key in enumerate(keys):
                store[key] = codes[:, j * width : (j + 1) * width], scales[:, j * width : (j + 1) * width]

        def weigh_last(mh):
            cols = halves[mh]
            nc.vector.tensor_tensor(zplane[PLANES - 1][:, cols], page_of[PLANES - 1][:, cols], aff7[mh], ALU.mult)

        zq = {}
        w2q = {}
        split(zq, quantise(z0g[0], W, "tab_w1", "w1s0"), [(0, 0), (0, 1)], C)
        weigh_last(0)
        z1g = [weave(1, quarters[j], ("h0", "h3")[j]) for j in range(2)]
        cast_weight(w2g1[:, G:], raw2[1, 1])
        codes = sbuf([P, HB * W], U32, "z0a")
        scales = sbuf([P, HB * W], U8, "w2s0")
        split(w2q, (codes, scales), [(0, 0), (1, 0)], W)
        nc.vector.quantize_mx(w2q[0, 0][0].bitcast(FP8X4), w2q[0, 0][1], w2g0[0])
        split(zq, quantise(z1g[0], C, "w1c1", "w1s2"), [(1, 0)], C)
        nc.vector.quantize_mx(w2q[1, 0][0].bitcast(FP8X4), w2q[1, 0][1], w2g0[1])
        split(zq, quantise(z1g[1], C, "v_w0", "zs0"), [(1, 1)], C)
        weigh_last(1)
        split(zq, quantise(z0g[1], W, "w1s3", "w1s1"), [(0, 2), (0, 3)], C)
        split(w2q, quantise(w2g1[:], HB * W, "h0", "w2s1"), [(0, 1), (1, 1)], W)

        y_s = sbuf([P, NG, T2], U8, "y_s")
        steps = [(mh, g, j) for mh in range(MH) for g in range(NG) for j in range(W // C)]
        last = len(steps) - 1
        rests = {}
        difs = {}
        pulls = {}
        parts = {}
        q_banks = {}
        gate_banks = {}
        ygrouped = {}

        def passes(banks, k, b, stationary, planes=range(PACK)):
            mh, g, j = steps[k]
            for t in planes:
                words, scales = stationary(b, g, t)
                nc.tensor.matmul_mx(
                    banks[t // 2][:, t % 2, :],
                    lhsT=words,
                    lhsT_scale=scales,
                    rhs=zq[b, 2 * mh + j][0].bitcast(FP8X4),
                    rhs_scale=zq[b, 2 * mh + j][1],
                    start=(b == 0 and t % 2 == 0),
                    stop=(b == HB - 1 and t % 2 == 1),
                )

        def w2_columns(b, g, t):
            cols = slice(t * P, (t + 1) * P)
            return w2q[b, g][0][:, cols].bitcast(FP8X4), w2q[b, g][1][:, cols]

        def w4_columns(b, g, t):
            return w4w[b][:, g, t, :].bitcast(FP4X4), w4s[:, b, g * W + t * P : g * W + (t + 1) * P]

        def gate_passes(k, b):
            if b == 0:
                gate_banks[k] = [psum.tile([P, 2, C], F32, name="gate", bufs=2) for pair in range(2)]
            passes(gate_banks[k], k, b, w4_columns)
            if b == HB - 1:
                rests[k] = sbuf([P, PACK, C], F32, ("aff01", "aff23", "raw0")[k % 3])
                for pair in range(2):
                    nc.scalar.activation(
                        rests[k][:, 2 * pair : 2 * pair + 2, :], gate_banks[k][pair][:], ACT.Sigmoid, scale=-1.0
                    )

        def q_passes(k, b):
            if b == 0:
                q_banks[k] = [psum.tile([P, 2, C], F32, name="q", bufs=6) for pair in range(2)]
            passes(q_banks[k], k, b, w2_columns)

        def gates(k):
            rests[k] = sbuf([P, PACK, C], F32, ("aff01", "aff23", "raw0")[k % 3])
            gate_banks[k] = []
            for pair in range(2):
                gate_banks[k].append(psum.tile([P, 2, C], F32, name="gate", bufs=2))
                for b in range(HB):
                    passes(gate_banks[k], k, b, w4_columns, (2 * pair, 2 * pair + 1))
                nc.scalar.activation(
                    rests[k][:, 2 * pair : 2 * pair + 2, :], gate_banks[k][pair][:], ACT.Sigmoid, scale=-1.0
                )

        def products(k):
            gates(k)
            q_banks[k] = [psum.tile([P, 2, C], F32, name="q", bufs=6) for pair in range(2)]
            for pair in range(2):
                for b in range(HB):
                    passes(q_banks[k], k, b, w2_columns, (2 * pair, 2 * pair + 1))

        def fall_of(k):
            mh, g, j = steps[k]
            return falls[g, mh][:, :, j * C : (j + 1) * C]

        def flat(tile):
            return tile[:].rearrange("p t m -> p (t m)")

        def difference(k):
            share = {0: GP_FIRST_COLS, last: GP_LAST_COLS}.get(k, GP_COLS)
            cut = PACK * C - share
            shift = max(share, cut) if k > 0 else PACK * C
            room = sbuf([P, shift + PACK * C], F32, ("raw7", "raw1", "w1c2")[k % 3])
            pulls[k] = room[:, : PACK * C]
            difs[k] = room[:, shift:]
            for pair in range(2):
                nc.vector.tensor_tensor(
                    bank_view(difs[k], pair), fall_of(k)[:, 2 * pair : 2 * pair + 2, :], q_banks[k][pair][:], ALU.subtract
                )
            parts[k] = {"vector": slice(0, cut), "gpsimd": slice(cut, PACK * C)}
            if k == 0:
                parts[k] = {"vector": slice(share, PACK * C), "gpsimd": slice(0, share)}

        def pull(name, k):
            cols = parts[k][name]
            {"vector": nc.vector, "gpsimd": nc.gpsimd}[name].tensor_tensor(pulls[k][:, cols], flat(rests[k])[:, cols], difs[k][:, cols], ALU.mult)

        def bank_view(room, pair):
            return room[:, pair * W : (pair + 1) * W].rearrange("p (e m) -> p e m", e=2)

        def blend(k):
            mh, g, j = steps[k]
            for pair in range(2):
                planes = slice(2 * pair, 2 * pair + 2)
                nc.vector.tensor_tensor(
                    fall_of(k)[:, planes, :], q_banks[k][pair][:], bank_view(pulls[k], pair), ALU.add
                )
            rows = out_0[g * W : (g + 1) * W, quarters[2 * mh + j]].rearrange("(p t) m -> p t m", t=PACK)
            nc.sync.dma_start(rows, fall_of(k))

        def planes_out(g, out_cols, grouped, slot, queue):
            codes = sbuf([P, out_cols.stop - out_cols.start], U32, slot)
            nc.vector.quantize_mx(codes[:].bitcast(FP8X4), y_s[:, g, out_cols], grouped)
            queue.dma_start(
                out_1[g, :, out_cols, :].rearrange("p m t -> p (m t)").bitcast(I32), codes[:].bitcast(I32)
            )

        def scales_out(mh):
            for r in range(4):
                eng = nc.sync if r % 2 == 0 else nc.scalar
                eng.dma_start(
                    out_2[:, r:16:4, halves[mh]].rearrange("g q m -> q g m").bitcast(I32),
                    y_s[r:P:32, :, halves[mh]].bitcast(I32),
                )

        def regroup(k):
            ygrouped[k] = sbuf([P, PACK * C], BF16, ("w4w_raw", "gb", "gc")[k % 3])
            cut = C if k < last else LAST_SCALAR_COLS
            interleave(nc.scalar.copy, ygrouped[k][:, : PACK * cut], fall_of(k)[:, :, :cut])
            if cut < C:
                interleave(nc.vector.tensor_copy, ygrouped[k][:, PACK * cut :], fall_of(k)[:, :, cut:])

        def step_planes(k):
            mh, g, j = steps[k]
            queue = nc.sync if k < last - 1 else nc.scalar
            planes_out(g, quarters[2 * mh + j], ygrouped[k][:], "y_codes%d" % (k % 3), queue)
            if g == NG - 1 and j == W // C - 1:
                scales_out(mh)

        z1late = {}
        gate_passes(0, 0)
        q_passes(0, 0)
        gate_passes(0, 1)
        q_passes(0, 1)
        q_passes(1, 0)
        for k in range(len(steps)):
            if k < 2:
                z1late[k] = weave(1, quarters[2 + k], "gb")
            difference(k)
            if k == 1:
                pull("vector", 0)
            if k > 0:
                pull("vector", k)
            pull("gpsimd", k)
            if k in (1, 2):
                split(zq, quantise(z1late[k - 1], C, "v_w%d" % k, "zs%d" % k), [(1, 1 + k)], C)
            if k >= PLANES_LAG:
                step_planes(k - PLANES_LAG)
            if k == 0:
                q_passes(1, 1)
                gates(1)
            elif k < last:
                products(k + 1)
            if k >= 1:
                blend(k - 1)
                regroup(k - 1)
        step_planes(last - 2)
        blend(last)
        regroup(last)
        step_planes(last - 1)
        step_planes(last)
